import numpy as np, ml_dtypes
CORES = [2,3,42,43,82,83,122,123]
N = 8
BF = ml_dtypes.bfloat16
S, NM, L, RO, TAU = 2048, 4096, 128, 4, 4
ST, C0, LN = S // L, 16 - RO, NM.bit_length() - 1
def pack(nm, st, kd, ac, fu):
    return np.where(fu, 1 + 2048 * nm + 32 * st + 16 * kd + ac, 0)
def done(e, x, w, kp):
    return {"ent": np.ascontiguousarray(e.reshape(N, 128, S)).astype(np.int32), "feat": np.ascontiguousarray(x.reshape(N, 128, NM)).astype(np.float32).astype(BF),
            "wt": np.ascontiguousarray(w.reshape(N, 128, 1)).astype(np.int32), "kap": np.ascontiguousarray(kp.reshape(N, 128, 1)).astype(np.int32)}
def pooled(rng, n, other):
    pool = rng.integers(0, NM, (8, 16, n)); pool[..., 0] = rng.choice(np.array([0, NM - 1]), (8, 16))
    j = (n * rng.random((N, 8, 16, S)) ** 2).astype(np.int64)
    v = pool[np.arange(8)[:, None, None], np.arange(16)[None, :, None], j]
    return np.where(rng.random(v.shape) < other, rng.integers(0, NM, v.shape), v)
def parts(rng, n, other):
    sh = (N, 8, 16, S); nm = pooled(rng, n, other)
    st = rng.integers(0, 64, sh); kd = (rng.random(sh) < 0.45).astype(np.int64); ac = rng.integers(0, 16, sh); fu = rng.random(sh) < 0.8
    x = (64 * rng.random((N, 8, 16, NM)) ** 2).astype(np.int64)
    return nm, st, kd, ac, fu, x, rng.integers(0, 256, (N, 8, 16)), rng.integers(0, 256, (N, 8, 16))
def setup_inputs(rng):
    nm, st, kd, ac, fu, x, w, kp = parts(rng, 24, 0.3)
    return done(pack(nm, st, kd, ac, fu), x, w, kp)
def setup_inputs_spread(rng):
    sh = (N, 8, 16, S)
    nm = np.exp2(LN * rng.random(sh)).astype(np.int64) - 1; nm = np.where(rng.random((1, 8, 16, 1)) < 0.5, NM - 1 - nm, nm)
    st = np.exp2(6 * rng.random(sh)).astype(np.int64) - 1; st = np.where(rng.random(sh) < 0.5, 63 - st, st)
    kd = (rng.random(sh) < rng.choice(np.array([0.1, 0.4, 0.8]), (N, 8, 1, 1))).astype(np.int64)
    fu = rng.random(sh) < rng.random((N, 8, 1, S))
    x = (np.exp2(6 * rng.random((N, 8, 1, NM))) * rng.random((N, 8, 16, NM))).astype(np.int64)
    w = np.exp2(8 * rng.random((N, 8, 16))).astype(np.int64) - 1; kp = 256 - np.exp2(8 * rng.random((N, 8, 16))).astype(np.int64)
    return done(pack(nm, st, kd, rng.integers(0, 16, sh), fu), x, w, kp)
def at_ends(rng, hi):
    o = np.argsort(rng.random((N, 8, 16)), axis=-1)
    return np.where(o < 11, hi * rng.integers(0, 2, o.shape), rng.integers(0, hi + 1, o.shape))
def setup_inputs_ends(rng):
    sh = (N, 8, 16, S); top = 2048 * NM
    z = 32 * 63 * rng.integers(0, 2, sh) + 15 * rng.integers(0, 2, sh) + 1
    e = np.where(rng.random(sh) < 0.28, 2048 * rng.integers(0, NM, sh) + z, top * rng.integers(0, 2, sh))
    k = rng.random((N, 8, 1, S)); last = 2048 * (NM - 1) + z
    e = np.where(k < 0.41, 16 + z, e); e = np.where(k < 0.37, z, e); e = np.where(k < 0.33, last, e)
    e = np.where(k < 0.26, 0, e); e = np.where(k < 0.16, top, e)
    x = 63 * (rng.random((N, 8, 16, NM)) < 0.2).astype(np.int64); x[..., NM - 1] = 63; x[..., 0] = 0
    w = at_ends(rng, 255); kp = at_ends(rng, 255); w[0, 7] = 255; w[N - 1, 7] = 255
    for c in [0, ST] + list(range(S - ST, S)): e[:, 7, :, c] = last[:, 7, :, c]
    u = 16 * 63 * 255 & 4095
    for m in (8, 15): e[0, 7, :, ((u * u >> 5) + int(kp[N - 1, 7, m]) * u) & (S - 1)] = top
    return done(e, x, w, kp)
def setup_inputs_corners(rng):
    nm, st, kd, ac, fu, x, w, kp = parts(rng, 6, 0.1); sh = kd.shape
    o = rng.permutation(8); md = o[(np.arange(8)[None, :] + (np.arange(N)[:, None] & 1)) & 7]; m4 = md[:, :, None, None]
    kd = np.where(m4 == 0, 1, np.where(m4 == 1, 0, kd)); fu = fu | (m4 == 1)
    fu = np.where(m4 == 2, rng.random((N, 8, 1, S)) < 0.5, fu)
    ac = np.where(m4 == 3, C0 - TAU - 1 + rng.integers(0, RO + 1, sh), ac); kd = np.where(m4 == 3, (rng.random(sh) < 0.7).astype(np.int64), kd)
    st = np.where(m4 == 4, 63 * rng.integers(0, 2, sh), st); st = np.where(m4 == 7, 31, st)
    kd = np.where(m4 == 6, ((np.arange(S)[None, :] & 15) != np.arange(16)[:, None]).astype(np.int64), kd); fu = fu | (m4 == 6)
    x = np.where(m4 == 5, 63, x); m3 = md[:, :, None]
    w = np.where(m3 == 4, 0, np.where(m3 == 7, 255, w)); kp = np.where(m3 == 6, 0, np.where(m3 == 7, 255, kp))
    return done(pack(nm, st, kd, ac, fu), x, w, kp)
def setup_inputs_ties(rng):
    nm, st, kd, ac, fu, x, w, kp = parts(rng, 3, 0.02); sh = st.shape
    st = rng.integers(0, 63, (1, 8, 16, 1)) + rng.integers(0, 2, sh)
    ac = rng.choice(np.array([0, C0 - TAU - 1, C0 - TAU, C0 - TAU + 1, C0, 15]), sh); fu = rng.random(sh) < 0.9
    e = pack(nm, st, kd, ac, fu)
    w[..., 0] |= 1; kp = np.argsort(rng.random((N, 8, 256)), axis=-1)[..., :16]
    nn = rng.integers(0, NM, (N, 8, 16)); c = np.zeros((N, 8, 16), np.int64)
    for r in range(N):
        for g in range(8):
            n = int(nn[r, g, 0])
            if int(np.add.reduce(w[r, g] * x[r, g, :, n])) & 1 == 0: x[r, g, 0, n] ^= 1
            u = int(np.add.reduce(w[r, g] * x[r, g, :, n])) & 4095
            c[r, g] = ((u * u >> 5) + kp[r, g] * u) & (S - 1)
    for r in range(N):
        for g in range(8):
            q = (r + 1) % N; l = min(i for i in range(17) if not np.any(c[r - 1, g] == ST * i))
            s = rng.integers(0, 64, 16); own = pack(nn[r, g], s, (np.arange(16) > 0).astype(np.int64), rng.integers(0, 16, 16), True)
            e[r, g, :, ST * l] = own
            d = rng.integers(1, 4, 16); m = np.sort(rng.permutation(16)[:2]); d[m] = np.array([1, 0]) if (r + g) & 1 else np.array([0, 1])
            miss = np.argsort(rng.random((16, 16)), axis=0) < d[None, :]
            hit = pack(nn[r, g][:, None], s[:, None] ^ rng.integers(1, 64, (16, 16)), rng.integers(0, 2, (16, 16)), rng.integers(0, 16, (16, 16)), True)
            no = np.where(rng.random((16, 16)) < 0.5, 0, (((own - 1) >> 4) << 4)[:, None] + 1 + rng.integers(0, 16, (16, 16)))
            e[q, g][:, c[r, g]] = np.where(miss, no, hit)
    return done(e, x, w, kp)
def gone(v, c):
    return np.where((((37 * c + v) >> 3) & 7) == 0, v ^ 8, v)
def setup_inputs_crowd(rng):
    nm, st, kd, ac, fu, x, w, kp = parts(rng, 8, 0.2)
    e = np.take_along_axis(pack(nm, st, kd, ac, fu), rng.integers(0, 24, (N, 8, 1, S)), 3)
    kp[:, ::2] = kp[:, ::2, :1]
    h = int(rng.integers(0, 8)); kp[:, h] = 0; w[:, h] = 0; w[:, h, 0] = 1; w[:, h, 15] = 64
    cols = ST * np.arange(1, L); sh = (16, L - 1)
    for r in range(N):
        q = (r + 1) % N; o = rng.permutation(4096); c = (o * o >> 5) & (S - 1)
        first = np.unique(c, return_index=True)[1]; first = first[c[first] % ST != 0]
        u = o[rng.permutation(first)[:L - 1]]; p = (u * u >> 5) & (S - 1)
        names = rng.permutation(NM)[:L - 1]; x[r, h, 0, names] = u & 63; x[r, h, 15, names] = u >> 6
        it = rng.random(sh) < 0.4; it[0] = True; it[15] = True
        a = pack(np.where(it, names[None, :], rng.integers(0, NM, sh)), rng.integers(0, 64, sh), 1 - it.astype(np.int64), rng.integers(0, C0 - TAU, sh), True)
        b = pack(gone(rng.integers(0, NM, sh), p[None, :]), rng.integers(0, 64, sh), 1, rng.integers(0, C0 - TAU, sh), True)
        full = rng.random(L - 1) < 0.5; full[-1] = True
        e[r, h][:, cols] = a
        e[q, h][:, p] = np.where(full[None, :], b, a)
    e[:, h, :, 0] = pack(gone(rng.integers(0, NM, 16), 0), rng.integers(0, 64, 16), 1, rng.integers(0, C0 - TAU, 16), True)[None, :]
    return done(e, x, w, kp)
def check_inputs(d):
    bad = []
    for k, lo, hi in (("ent", 0, 2048 * NM), ("feat", 0, 63), ("wt", 0, 255), ("kap", 0, 255)):
        v = np.asarray(d[k]).astype(np.float64)
        if not (np.min(v) >= lo and np.max(v) <= hi): bad.append("range of " + k)
        elif np.any(v != np.floor(v)): bad.append("whole numbers in " + k)
    return bad
def item(a):
    return (a > 0) & ((((a - 1) >> 4) & 1) == 0)
def asleep(a, clock):
    return (a > 0) & ((((a - 1) >> 4) & 1) == 1) & (clock - ((a - 1) & 15) > TAU)
def stay(a, site, clock):
    return np.where(asleep(a, clock) & ((((37 * site + ((a - 1) >> 11)) >> 3) & 7) != 0), 0, a)
def meet(a, b, clock):
    same = (a > 0) & (b > 0) & (((a - 1) >> 11) == ((b - 1) >> 11)); big = np.maximum(a, b)
    wake = same & asleep(big, clock) & item(np.minimum(a, b))
    big = np.where(wake, (((big - 1) >> 4) << 4) + clock + 1, big)
    return np.where(same, big, np.where((a == 0) & ~asleep(b, clock), b, a)), np.where(same, big, np.where((b == 0) & ~asleep(a, clock), a, b))
def reference(ent, feat, wt, kap):
    E = ent.astype(np.int64).reshape(N, 8, 16, S); X = feat.astype(np.float32).astype(np.int64).reshape(N, 8, 16, NM)
    w = wt.astype(np.int64).reshape(N, 8, 16, 1); kp = kap.astype(np.int64).reshape(N, 8, 16, 1); A = [0] * N
    for t in range(RO):
        clock = C0 + t; lane = ST * np.arange(L) + t % ST; new = E.copy(); called = []
        for r in range(N):
            q = (r + 1 + t % (N - 1)) % N
            a = E[r][:, :, lane]
            x = np.take_along_axis(X[r], np.maximum((a - 1) >> 11, 0).reshape(8, 1, 16 * L), 2).reshape(8, 16, 16, L)
            y = np.max(np.where(item(a)[:, None], x, 0), axis=2)
            u = np.add.reduce(w[r] * y, axis=1)[:, None, :] & 4095
            e = ((u * u >> 5) + kp[r] * u + A[r]) & (S - 1)
            cand = np.take_along_axis(E[q], e.reshape(8, 1, 16 * L), 2).reshape(8, 16, 16, L) - 1
            own = a[:, :, None, :] - 1
            score = np.add.reduce((((cand >> 11) == (own >> 11)) & ((cand >> 4) != (own >> 4))).astype(np.int64), axis=1)
            p = np.take_along_axis(e, np.argmax(score, axis=1)[:, None, :], 1)
            win = np.zeros((8, L), bool)
            for g in range(8): win[g, np.unique(p[g, 0], return_index=True)[1]] = True
            b = np.take_along_axis(E[q], p, 2)
            na, nb = meet(stay(a, lane[None, None, :], clock), stay(b, p, clock), clock)
            new[r][:, :, lane] = np.where(win[:, None, :], na, a)
            called.append((q, p[:, 0], win, nb)); A[r] = int(np.count_nonzero(win)) & 31
        for q, p, win, nb in called:
            for g in range(8): new[q, g][:, p[g, win[g]]] = nb[g][:, win[g]]
        E = new
    return {"yent": E.reshape(N, 128, S).astype(np.float32)}

@@ -1,0 +1,551 @@
+from concourse.mybir import AluOpType, ActivationFunctionType
+
+N = 8
+RO = 4
+M0 = 12582912.0
+MB = M0 * 2048.0
+BIG = 1048576.0
+W = 2048 + 128
+NE = 8
+M16 = M0 * 16.0
+VS, VS0 = 40, 16
+
+_F, _B, _I, _H, _U = "float32", "bfloat16", "int32", "float16", "uint16"
+SCRATCH = {}
+for _n, _w, _d in [
+        ("ents", 2048, _I), ("raw", W, _F), ("cod", W, _F), ("st", 2048, _F), ("fw", 4112, _B), ("cf1", 2048, _F), ("cf2", 2048, _F),
+        ("wti", 4, _I), ("kpi", 4, _I), ("bcol", 16, _F),
+        ("ones", 160, _B), ("one16", 128, _B), ("bd0", 128, _B), ("bd", 128, _B), ("z0", 144, _B), ("z1", 144, _B), ("z2", 144, _B),
+        ("z", 144, _B), ("zl", 144, _B), ("zn", 144, _B), ("iz", 160, _B), ("iz0", 160, _H), ("iz1", 160, _H), ("sb", 128, _H), ("wblk", 128, _B),
+        ("fm", 2048, _B), ("cli", 128, _I), ("cl", 128, _U), ("pi", 4, _I), ("pcol", 16, _F), ("p16", 4, _I), ("ii", 8, _I),
+        ("dum", 8, _F), ("dmc", 8, _F), ("ji", 16, _I), ("sti", 64, _I), ("stj", 64, _I),
+        ("i1", 128, _I), ("i2", 128, _I), ("i3", 128, _I), ("lst", 128, _U), ("fg", 2048, _B), ("fs", 2048, _B),
+        ("u1", 128, _I), ("u2", 128, _I), ("u4", 128, _F), ("u5", 128, _I), ("u6", 128, _I),
+        ("se", 512, _U), ("le", 512, _U), ("so", 1024, _F), ("lo", 1024, _F), ("sa", 16, _F), ("la", 16, _F),
+        ("sx", 4 * 384, _F), ("ln", 4 * 256, _F), ("nbc", 512, _F), ("c1", 256, _F), ("c2", 256, _F), ("o1", 128, _F), ("o2", 128, _F),
+        ("ox", 2048, _F), ("dd", 2048, _B), ("da", 2048, _B), ("db", 2048, _B), ("mt", 2048, _B),
+        ("eb", 128, _F), ("key", 128, _F), ("kt", 128, _F), ("ks", 128, _F), ("et", 128, _H), ("rt", 128, _H),
+        ("l1", 8, _U), ("l2", 32, _U), ("dl2", 8, _F), ("w2", 8, _F), ("w2b", 8, _F),
+        ("win", 128, _B), ("wj", 128, _B), ("cab", 4, _B),
+        ("ah", 128, _I), ("al", 128, _I), ("ak", 128, _I), ("ap", 128, _F), ("as2", 128, _F), ("ad", 128, _F), ("ea", 128, _F),
+        ("ac1", 128, _F), ("ac2", 128, _F),
+        ("bg", 128, _F), ("bh", 128, _I), ("bl", 128, _I), ("bk", 128, _I), ("bs", 128, _F), ("bp", 128, _F), ("di", 128, _F),
+        ("dq", 128, _F), ("sg", 128, _F), ("ebz", 128, _F), ("bd2", 128, _F), ("t2b", 128, _F), ("pp", 128, _F), ("d2", 128, _F)]:
+    SCRATCH[_n] = ("sbuf", [128, _w], _d)
+for _n, _w, _d in [("idf", 128, _F), ("trb", 512, _B), ("big", 1024, _B), ("pb", 1024, _B), ("pc", 1024, _H), ("nc", 1024, _H), ("wg", 240, _B),
+                   ("sq", 512, _B), ("eq", 1024, _B), ("aa", 4, _F)]:
+    SCRATCH[_n] = ("sbuf", [128, _w], _d)
+for _n in ("ji", "sb", "key"):
+    SCRATCH.pop(_n)
+for _n in ("psU", "psK0", "psK1", "psL", "psR", "psC", "psG", "psV"):
+    SCRATCH[_n] = ("psum", [128, 512], _F)
+SEMAPHORES = (["sV", "sA", "sP", "sG", "dent", "dsm", "dfe", "dy", "loc"]
+              + ["%s%d" % (k, t) for k in ("ro", "re", "rn", "ra") for t in range(RO)])
+
+
+def rank_program(g, core, T, topo):
+    rank = T.rank_of(core)
+    if rank is None:
+        return
+    A = AluOpType
+    F = ActivationFunctionType
+    Q = {"V": g.vector, "A": g.scalar, "P": g.tensor, "G": g, "S": g.sync}
+    tot = {}
+    seen = {"V": {}, "A": {}, "P": {}, "G": {}, "S": {}}
+    wr, rd, bank = {}, {}, {}
+    v, a, pe = g.vector, g.scalar, g.tensor
+
+    def wait(q, evs):
+        evs = [e for e in evs if seen[q].get(e[0], 0) < e[1]]
+        for e in evs:
+            if seen[q].get(e[0], 0) >= e[1]:
+                continue
+            if any(o is not e and o[2].get(e[0], 0) >= e[1] and (o[0] != e[0] or o[1] > e[1]) for o in evs):
+                continue
+            Q[q].wait_ge(T.sem[e[0]], e[1])
+            seen[q][e[0]] = e[1]
+        for e in evs:
+            for s, n in e[2].items():
+                if seen[q].get(s, 0) < n:
+                    seen[q][s] = n
+
+    def deps(q, r, w):
+        evs = []
+        for k in r:
+            evs += [e for o, e in wr.get(k, [])]
+        for k in w:
+            evs += [e for o, e in wr.get(k, []) if o != q]
+            evs += [e for o, e in rd.get(k, []) if o != q]
+        for k in list(r) + list(w):
+            if k[:2] == "ps":
+                evs += [e for o, e in bank.get(k.split(":")[0], {}).items() if o != q]
+        return evs
+
+    def note(q, r, w, ev):
+        for k in w:
+            wr[k] = [(q, ev)]
+            rd[k] = []
+        for k in r:
+            rd[k] = [x for x in rd.get(k, []) if x[0] != q or q == "D"] + [(q, ev)]
+        for k in list(r) + list(w):
+            if k[:2] == "ps":
+                bank.setdefault(k.split(":")[0], {})[q] = ev
+
+    def op(q, fn, r, w):
+        wait(q, deps(q, r, w))
+        s = "s" + q
+        tot[s] = tot.get(s, 0) + 1
+        fn().then_inc(T.sem[s], 1)
+        clk = dict(seen[q])
+        clk[s] = tot[s]
+        note(q, r, w, (s, tot[s], clk))
+
+    def dma(q, out, in_, r, w, s):
+        wait(q, deps("D" + q, r, w))
+        Q[q].dma_start(out, in_).then_inc(T.sem[s], 16)
+        tot[s] = tot.get(s, 0) + 16
+        clk = dict(seen[q])
+        clk[s] = tot[s]
+        note("D", r, w, (s, tot[s], clk))
+
+    def joined(k, s):
+        wr[k] = [("D", (s, tot[s], {s: tot[s]}))]
+
+    def send(dst, out, in_, r, s):
+        wait("G", deps("G", r, []))
+        rid, pid = topo.addr(dst)[:2]
+        m = 0
+        for e in topo.engines(core, dst)[:NE]:
+            m |= 1 << e
+        g.remote_dma(out, in_, T.sem[s], T.sem["loc"], pid, rid, m)
+        tot["loc"] = tot.get("loc", 0) + NE
+
+    def landed(k, s):
+        tot[s] = NE
+        wr[k] = [("R", (s, NE, {s: NE}))]
+
+    def ts(out, in0, s1, s2, o0, o1, r, w):
+        if o1 is None:
+            op("V", lambda: v.tensor_scalar(out, in0, s1, None, o0), r, w)
+        else:
+            op("V", lambda: v.tensor_scalar(out, in0, s1, s2, o0, o1), r, w)
+
+    def tt(out, i0, i1, o, r, w):
+        op("V", lambda: v.tensor_tensor(out, i0, i1, o), r, w)
+
+    def vc(out, in_, r, w):
+        op("V", lambda: v.tensor_copy(out, in_), r, w)
+
+    def act(out, in_, f, r, w, bias=0.0, scale=1.0):
+        op("A", lambda: a.activation(out, in_, f, bias=bias, scale=scale), r, w)
+
+    def mm(out, l, rh, st, sp, r, w):
+        op("P", lambda: pe.matmul(out, l, rh, st, sp), r, w)
+
+    def ms(ap, c, w):
+        op("V", lambda: v.memset(ap, c), [], w)
+
+    BC = {}
+
+    def bias(c):
+        if c not in BC:
+            i = len(BC)
+            BC[c] = i
+            ms(T.bcol[:, i:i + 1], c, ["bc%d" % i])
+        return T.bcol[:, BC[c]:BC[c] + 1]
+
+    dma("S", T.ents[:, 0:1024], T.ent[:, 0:1024], [], [], "dent")
+    dma("A", T.ents[:, 1024:2048], T.ent[:, 1024:2048], [], [], "dent")
+    joined("ents", "dent")
+    dma("S", T.wti[:, 0:1], T.wt[:, 0:1], [], [], "dsm")
+    dma("A", T.kpi[:, 0:1], T.kap[:, 0:1], [], [], "dsm")
+    joined("wti", "dsm")
+    joined("kpi", "dsm")
+    dma("S", T.fw[:, 0:2048], T.feat[:, 0:2048], [], [], "dfe")
+    dma("A", T.fw[:, 2048:4096], T.feat[:, 2048:4096], [], [], "dfe")
+    joined("fw", "dfe")
+
+    ms(T.ones[:], 1.0, ["ones"])
+    ms(T.big[:], 4096.0, ["big"])
+    op("G", lambda: g.iota(T.sti[:], [[37, 64]], 0, 0), [], ["sti"])
+    op("G", lambda: g.iota(T.pi[:, 0:1], [[1, 1]], 0, 1), [], ["pi"])
+    op("G", lambda: g.affine_select(T.bd0[:], T.ones[:, 0:128], [[-16, 8], [0, 16]], A.is_ge, 0.0, 0, 1), ["ones"], ["bd0"])
+    op("G", lambda: g.affine_select(T.bd[:], T.bd0[:], [[16, 8], [0, 16]], A.is_ge, 0.0, 15, -1), ["bd0"], ["bd"])
+    op("G", lambda: g.iota(T.cli[:], [[1, 128]], 0, 0), [], ["cli"])
+    op("G", lambda: g.affine_select(T.z0[:], T.ones[:, 0:144], [[-16, 9], [0, 16]], A.is_ge, 0.0, 0, 1), ["ones"], ["z0"])
+    op("G", lambda: g.affine_select(T.z1[:], T.z0[:], [[16, 9], [0, 16]], A.is_ge, 0.0, 15, -1), ["z0"], ["z1"])
+    op("G", lambda: g.affine_select(T.z2[:], T.z1[:], [[0, 9], [1, 16]], A.is_equal, 0.0, -15, 0), ["z1"], ["z2"])
+    op("G", lambda: g.affine_select(T.iz[:], T.ones[:], [[-1, 160]], A.is_equal, 0.0, 16, 1), ["ones"], ["iz"])
+    op("G", lambda: g.iota(T.ii[:], [[16, 8]], 2048, 0), [], ["ii"])
+    op("G", lambda: g.affine_select(T.trb[:], T.big[:, 0:512], [[0, 4], [-1, 128]], A.is_ge, 0.0, 0, 1), ["big"], ["trb"])
+    op("G", lambda: g.affine_select(T.pb[:], T.big[:], [[-16, 8], [0, 128]], A.is_equal, 0.0, -15, 1), ["big"], ["pb"])
+    ts(T.stj[:], T.sti[:], 63, None, A.bitwise_and, None, ["sti"], ["stj"])
+    ts(T.st[:, 0:64], T.stj[:], 2048.0, -17.0, A.mult, A.add, ["stj"], ["st"])
+    n = 64
+    while n < 2048:
+        act(T.st[:, n:2 * n], T.st[:, 0:n], F.Copy, ["st"], ["st"])
+        n *= 2
+    b_w, b_f, b_w1, b_mb, b_mmb, b_64, b_ea, b_one, b_15, b_m32 = [
+        bias(c) for c in (-8.5, M16, -1024.5, MB, -MB, -64.0, 1.0 / BIG, 1.0, -15.5, M0 * 32)]
+    wait("A", [wr["bc%d" % i][0][1] for i in range(len(BC))])
+    ms(T.fm[:], 1.0, ["fm"])
+    op("V", lambda: v.memset(T.fm[:, 0:2048:16], 0.0), ["fm"], ["fm"])
+    ms(T.fw[:, 4096:4112], 0.0, ["fwz"])
+    ms(T.pcol[:, 8:9], 0.0, ["acol"])
+    ts(T.p16[:, 0:1], T.pi[:, 0:1], 15, None, A.bitwise_and, None, ["pi"], ["p16"])
+    ts(T.p16[:, 1:2], T.pi[:, 0:1], 16, None, A.bitwise_and, None, ["pi"], ["p16b"])
+    ts(T.pcol[:, 3:4], T.p16[:, 0:1], -2048.0, 15 * 2048 - 1023.5, A.mult, A.add, ["p16"], ["pc3"])
+    vc(T.cl[:], T.cli[:], ["cli"], ["cl"])
+    vc(T.pcol[:, 6:7], T.wti[:, 0:1], ["wti"], ["wcol"])
+    vc(T.pcol[:, 7:8], T.kpi[:, 0:1], ["kpi"], ["kcol"])
+    ts(T.wblk[:], T.bd[:], T.pcol[:, 6:7], None, A.mult, None, ["bd", "wcol"], ["wblk"])
+
+    def more_constants():
+        ms(T.one16[:], 0.0625, ["one16"])
+        ms(T.sa[:], 0.0, ["sa"])
+        vc(T.pcol[:, 0:1], T.p16[:, 0:1], ["p16"], ["pc0"])
+        ts(T.pcol[:, 1:2], T.p16[:, 1:2], 0.0, None, A.is_equal, None, ["p16b"], ["pc1"])
+        ts(T.pcol[:, 2:3], T.p16[:, 1:2], 0.0, None, A.is_gt, None, ["p16b"], ["pc2"])
+        ts(T.pc[:], T.pb[:], 2.0 ** -12, None, A.mult, None, ["pb"], ["pc"])
+        ts(T.nc[:], T.pb[:], -2.0 ** -12, None, A.mult, None, ["pb"], ["nc"])
+        ms(T.wg[:], 0.0, ["wg0"])
+        op("V", lambda: v.memset(T.wg[:, 112:128], 1.0), ["wg0"], ["wg"])
+        ts(T.zl[:], T.z2[:], 0.0625, None, A.mult, None, ["z2"], ["zl"])
+        ts(T.iz0[:], T.iz[:], T.pcol[:, 1:2], None, A.mult, None, ["iz", "pc1"], ["iz0"])
+        ts(T.iz1[:], T.iz[:], T.pcol[:, 2:3], None, A.mult, None, ["iz", "pc2"], ["iz1"])
+        ts(T.dum[:], T.ii[:], T.pcol[:, 0:1], None, A.add, None, ["ii", "pc0"], ["dum"])
+        yield
+        ts(T.dmc[:], T.dum[:], -1023.5, None, A.add, None, ["dum"], ["dmc"])
+        for i in range(4):
+            s = slice(512 * i, 512 * i + 512)
+            vc(T.raw[:, s], T.ents[:, s], ["ents"], ["raw"])
+            if i % 2:
+                yield
+
+    banks = ["psK0", "psK1", "psR", "psC"]
+
+    def first_parts(blocks):
+        for i in blocks:
+            s = slice(512 * i, 512 * i + 512)
+            k = "@%d" % i
+            ts(T.cf1[:, s], T.ents[:, s], -1024.5, MB, A.add, A.add, ["ents"], ["cf1" + k])
+            act(T[banks[i]][:], T.cf1[:, s], F.Identity, ["cf1" + k], [banks[i]], bias=b_mmb)
+            ts(T.cf2[:, s], T.ents[:, s], -8.5, M16, A.add, A.add, ["ents"], ["cf2" + k])
+
+    def first_cod():
+        for i in range(4):
+            s = slice(512 * i, 512 * i + 512)
+            tt(T.cod[:, s], T[banks[i]][:], T.cf2[:, s], A.add, [banks[i], "cf2@%d" % i], ["cod"])
+
+    def code_parts(src, sk, t1, t2, k, ps):
+        act(t2, src, F.Identity, sk, [k + "2"], bias=b_w)
+        act(t1, src, F.Identity, sk, [k + "1"], bias=b_w1)
+        act(t2, t2, F.Identity, [k + "2"], [k + "2"], bias=b_f)
+        act(t1, t1, F.Identity, [k + "1"], [k + "1"], bias=b_mb)
+        act(ps, t1, F.Identity, [k + "1"], [("psG:" if k == "n" else "psL:") + k], bias=b_mmb)
+
+    def lane_list(t):
+        src, sk = (T.ents, "ents") if t == 0 else (T.raw, "raw")
+        ts(T.i1[:], src[:, t:2048:16], -1.0, None, A.add, None, [sk], ["i1"])
+        ts(T.i3[:], T.i1[:], 16, None, A.bitwise_and, None, ["i1"], ["i3"])
+        ts(T.i2[:], T.i1[:], 11, None, A.arith_shift_right, None, ["i1"], ["i2"])
+        ts(T.psV[:, 0:128], T.i3[:], 512.0, None, A.mult, None, ["i3"], ["psV:1"])
+        tt(T.psV[:, 128:256], T.i2[:], T.psV[:, 0:128], A.add, ["i2", "psV:1"], ["psV:2"])
+        ts(T.lst[:], T.psV[:, 128:256], 4096.0, None, A.min, None, ["psV:2"], ["lst"])
+
+    def own_parts(t):
+        o = 256 * t
+        if t == 0:
+            vc(T.so[:, 0:128], T.ents[:, 0:2048:16], ["ents"], ["so0"])
+        else:
+            act(T.so[:, o:o + 128], T.raw[:, t:2048:16], F.Copy, ["raw"], ["so%d" % t])
+        code_parts(T.so[:, o:o + 128], ["so%d" % t], T.o1[:], T.o2[:], "o", T.psL[:, 256:384])
+
+    def own_send(t, dst):
+        o = 256 * t
+        tt(T.so[:, o + 128:o + 256], T.psL[:, 256:384], T.o2[:], A.add, ["psL:o", "o2"], ["soc%d" % t])
+        send(dst, T.lo[:, o:o + 256], T.so[:, o:o + 256], ["so%d" % t, "soc%d" % t], "ro%d" % t)
+
+    def features(vs):
+        rk = ["lst", "fw", "fwz"]
+        op("A", lambda: a.activation(T.fg[:, 16 * vs:2048], T.fw[:].indirect(T.lst[:, vs:128]), F.Copy), rk, ["fgA"])
+        op("V", lambda: v.tensor_copy(T.fg[:, 0:16 * vs], T.fw[:].indirect(T.lst[:, 0:vs])), rk, ["fgV"])
+
+    def scans(vs):
+        for n0, n1, k in ((0, vs, "V"), (vs, 128, "A")):
+            c = slice(16 * n0, 16 * n1)
+            op("V", lambda: v.tensor_tensor_scan(T.fs[:, c], T.fm[:, c], T.fg[:, c], 0.0, A.mult, A.max), ["fm", "fg" + k], ["fs" + k])
+        mm(T.psU[:, 0:128], T.wblk[:], T.fs[:, 15:2048:16], True, True, ["wblk", "fsV", "fsA"], ["psU"])
+
+    def cand(t, dst):
+        o = 128 * t
+        ac, ak = (T.pcol[:, 8:9], "acol") if t == 0 else (T.la[:, 4 * t - 4:4 * t - 3], "la%d" % (t - 1))
+        vc(T.u1[:], T.psU[:, 0:128], ["psU"], ["u1"])
+        ts(T.u2[:], T.u1[:], 4095, None, A.bitwise_and, None, ["u1"], ["u2"])
+        ts(T.psV[:, 0:128], T.u2[:], 0.03125, T.pcol[:, 7:8], A.mult, A.add, ["u2", "kcol"], ["psV:1"])
+        tt(T.u4[:], T.psV[:, 0:128], T.u2[:], A.mult, ["psV:1", "u2"], ["u4"])
+        ts(T.u5[:], T.u4[:], ac, -0.375, A.add, A.add, ["u4", ak], ["u5"])
+        ts(T.u6[:], T.u5[:], 2047, None, A.bitwise_and, None, ["u5"], ["u6"])
+        vc(T.se[:, o:o + 128], T.u6[:], ["u6"], ["se%d" % t])
+        send(dst, T.le[:, o:o + 128], T.se[:, o:o + 128], ["se%d" % t], "re%d" % t)
+
+    def scatter(tab, lists, vals, r):
+        op("V", lambda: v.tensor_copy(T[tab][:].indirect(lists), vals), r, [tab])
+
+    def own_side(t):
+        o = 256 * t
+        th = 8.0 + t
+        av, lk = T.lo[:, o:o + 128], "lo%d" % t
+        tt(T.ah[:], av, T.st[:, t:2048:16], A.add, [lk, "st"], ["ah"])
+        ts(T.al[:], T.ah[:], 31, None, A.bitwise_and, None, ["ah"], ["al"])
+        ts(T.ak[:], T.ah[:], 114688, None, A.bitwise_and, None, ["ah"], ["ak"])
+        ts(T.psV[:, 0:128], T.al[:], th, BIG, A.is_ge, A.mult, ["al"], ["psV:1"])
+        ts(T.psV[:, 256:384], T.al[:], 16.0, None, A.is_ge, None, ["al"], ["psV:ia"])
+        tt(T.psV[:, 128:256], T.ak[:], T.psV[:, 0:128], A.is_le, ["ak", "psV:1"], ["psV:2"])
+        tt(T.as2[:], T.al[:], T.psV[:, 0:128], A.add, ["al", "psV:1"], ["as2"])
+        tt(T.psV[:, 384:512], av, T.psV[:, 0:128], A.mult, [lk, "psV:1"], ["psV:ga"])
+        tt(T.ap[:], av, T.psV[:, 128:256], A.mult, [lk, "psV:2"], ["ap"])
+
+    def own_side_scalar(t):
+        act(T.ad[:], T.as2[:], F.Relu, ["as2"], ["ad"], bias=b_ck[t], scale=-1.0)
+        act(T.ac1[:], T.ap[:], F.Identity, ["ap"], ["ac1"], bias=b_w1)
+        act(T.ea[:], T.ap[:], F.Relu, ["ap"], ["ea"], bias=b_ea, scale=-1.0 / BIG)
+        act(T.ac2[:], T.ac1[:], F.Identity, ["ac1"], ["ac2"], bias=b_mb)
+        act(T.psG[:, 384:512], T.ac2[:], F.Identity, ["ac2"], ["psG:c"], bias=b_mmb)
+
+    def expand(t, h):
+        o = 256 * t + 128
+        op("A", lambda: a.activation(T.ox[:, 1024 * h:1024 * h + 1024],
+                                     T.lo[:, o:o + 128].indirect(T.cl[:, 64 * h:64 * h + 64]), F.Copy),
+           ["lo%d" % t, "cl"], ["ox%d" % h])
+
+    CH = [0, 32, 64, 104, 128]
+    todo = [more_constants()]
+
+    def fill():
+        return next(todo[0], 1) is None
+
+    def score(t):
+        def gat(i):
+            c = slice(16 * CH[i], 16 * CH[i + 1])
+            o = 128 * t
+            op("V", lambda: v.tensor_tensor(T.dd[:, c], T.cod[:, 0:2048].indirect(T.le[:, o + CH[i]:o + CH[i + 1]]), T.ox[:, c], A.subtract),
+               ["cod", "le%d" % t, "ox%d" % (i // 2)], ["dd%d" % i])
+            act(T.da[:, c], T.dd[:, c], F.Abs, ["dd%d" % i], ["da%d" % i], scale=0.0625)
+            if i > 1:
+                act(T.db[:, c], T.da[:, c], F.Abs, ["da%d" % i], ["db%d" % i], bias=b_64)
+
+        def thr(i):
+            c = slice(16 * CH[i], 16 * CH[i + 1])
+            if i > 1:
+                ts(T.mt[:, c], T.db[:, c], 63.75, None, A.is_lt, None, ["db%d" % i], ["mt%d" % i])
+            else:
+                ts(T.mt[:, c], T.da[:, c], 127.5, None, A.is_lt, None, ["da%d" % i], ["mt%d" % i])
+
+        def same(i):
+            c = slice(16 * CH[i], 16 * CH[i + 1])
+            ts(T.db[:, c], T.da[:, c], 0.5, None, A.is_lt, None, ["da%d" % i], ["db%d" % i])
+
+        def add(h):
+            k = "psK0:k%d" % h
+            s = slice(64 * h, 64 * h + 64)
+            mm(T.psK0[:, s], T.idf[:], T.eb[:, s], True, False, ["idf", "eb"], [k])
+            for m in range(16):
+                mm(T.psK0[:, s], T.z[:, 15 - m:143 - m], T.mt[:, 1024 * h + m:1024 * h + 1024:16], False, m == 15 and h == 1,
+                   ["z", "mt%d" % (2 * h), "mt%d" % (2 * h + 1)], [k])
+
+        def sub():
+            for m in range(16):
+                mm(T.psK0[:, 0:64], T.zn[:, 15 - m:143 - m], T.db[:, m:1024:16], False, m == 15,
+                   ["zn", "db0", "db1"], ["psK0:k0"])
+
+        gat(0)
+        gat(1)
+        ts(T.eb[:], T.le[:, 128 * t:128 * t + 128], T.pcol[:, 3:4], None, A.add, None, ["le%d" % t, "pc3"], ["eb"])
+        gat(2)
+        thr(0)
+        thr(1)
+        add(0)
+        gat(3)
+        same(0)
+        same(1)
+        sub()
+        fill()
+        thr(2)
+        fill()
+        thr(3)
+        add(1)
+        while fill():
+            pass
+
+    def partner(t):
+        for i, k in enumerate(("psU", "psR")):
+            mm(T[k][:], T.iz[:, 16:144], T.trb[:], True, False, ["iz", "trb"], [k + ":d"])
+        op("V", lambda: v.transpose(T.kt[:], T.psK0[:, 0:128]), ["psK0:k0", "psK0:k1"], ["kt"])
+        op("V", lambda: v.tensor_tensor_scan(T.ks[:], T.fm[:, 0:128], T.kt[:], 0.0, A.mult, A.max), ["fm", "kt"], ["ks"])
+        ts(T.psK1[:, 0:128], T.ks[:], MB, -MB, A.add, A.add, ["ks"], ["psK1:0"])
+        tt(T.et[:], T.ks[:], T.psK1[:, 0:128], A.subtract, ["ks", "psK1:0"], ["et"])
+        for h in range(2):
+            for g2 in range(2):
+                b = 16 - 16 * (g2 - h)
+                mm(T.psL[:, h:8:2], T["iz%d" % h][:, b:b + 128], T.et[:, 16 * g2 + 15:128:32], g2 == 0, g2 == 1,
+                   ["iz%d" % h, "et"], ["psL"])
+        op("V", lambda: v.transpose(T.rt[:], T.et[:]), ["et"], ["rt"])
+        for i, k in enumerate(("psU", "psR")):
+            mm(T[k][:], T.rt[:], T.nc[:, 512 * i:512 * i + 512], False, False, ["rt", "nc"], [k + ":d"])
+            for b in range(4):
+                c = 512 * i + 128 * b
+                mm(T[k][:, 128 * b:128 * b + 128], T.pc[:, c:c + 128], T.rt[:], False, b == 3, ["rt", "pc"], [k + ":d"])
+        act(T.sq[:], T.psU[:], F.Square, ["psU:d"], ["sq"])
+        act(T.eq[:, 0:512], T.sq[:], F.Relu, ["sq"], ["eq0"], bias=b_one, scale=-1.0)
+        ts(T.l1[:], T.psL[:, 0:8], 1023.5, None, A.add, None, ["psL"], ["l1"])
+        tt(T.dl2[:], T.psL[:, 0:8], T.dmc[:], A.subtract, ["psL", "dmc"], ["dl2"])
+        op("V", lambda: v.tensor_copy(T.bg[:], T.raw[:, 0:2048].indirect(T.l1[:])), ["raw", "l1"], ["bg"])
+        op("V", lambda: v.tensor_tensor(T.bh[:], T.st[:].indirect(T.l1[:]), T.bg[:], A.add), ["st", "l1", "bg"], ["bh"])
+
+    K0, K1 = T.psK0, T.psK1
+
+    def meet(t, dst):
+        th = 8.0 + t
+        X = 384 * t
+        last = t == RO - 1
+        ts(T.bl[:], T.bh[:], 31, None, A.bitwise_and, None, ["bh"], ["bl"])
+        ts(T.bk[:], T.bh[:], 114688, None, A.bitwise_and, None, ["bh"], ["bk"])
+        ts(K0[:, 0:128], T.bl[:], th, BIG, A.is_ge, A.mult, ["bl"], ["psK0:bn"])
+        ts(K1[:, 0:128], T.bl[:], 16.0, None, A.is_ge, None, ["bl"], ["psK1:0"])
+        tt(K0[:, 128:256], T.bk[:], K0[:, 0:128], A.is_le, ["bk", "psK0:bn"], ["psK0:bv"])
+        tt(T.bs[:], T.bl[:], K0[:, 0:128], A.add, ["bl", "psK0:bn"], ["bs"])
+        act(T.bd2[:], T.bs[:], F.Relu, ["bs"], ["bd2"], bias=b_ck[t], scale=-1.0)
+        tt(T.bp[:], T.bg[:], K0[:, 128:256], A.mult, ["bg", "psK0:bv"], ["bp"])
+        ts(T.eq[:, 512:1024], T.psR[:], 0.0, None, A.is_equal, None, ["psR:d"], ["eq1"])
+        for c in range(8):
+            mm(T.psC[:, 0:128], T.wg[:, 112 - 16 * c:240 - 16 * c], T.eq[:, 128 * c:128 * c + 128], c == 0, c == 7,
+               ["wg", "eq%d" % (c // 4)], ["psC"])
+        tt(T.di[:], T.bp[:], T.psG[:, 384:512], A.subtract, ["bp", "psG:c"], ["di"])
+        act(T.dq[:], T.di[:], F.Square, ["di"], ["dq"], bias=b_sq, scale=1.0 / 1024)
+        act(T.sg[:], T.dq[:], F.Sign, ["dq"], ["sg"], bias=b_one, scale=-1.0)
+        act(T.ebz[:], T.bp[:], F.Relu, ["bp"], ["ebz"], bias=b_ea, scale=-1.0 / BIG)
+        act(T.win[:], T.psC[:, 0:128], F.Relu, ["psC"], ["win"], bias=b_one, scale=-1.0)
+        for s in range(16):
+            mm(T.psC[:, 128:136], T.zl[:, 15 - s:143 - s], T.win[:, s:128:16], s == 0, s == 15, ["zl", "win"], ["psC:l"])
+        if not last:
+            op("A", lambda: a.activation(T.wj[:], T.win[:], F.Copy, accum_out=T.pcol[:, 9:10]), ["win"], ["wj", "ca"])
+            act(T.cab[:, 0:1], T.pcol[:, 9:10], F.Copy, ["ca"], ["cab"])
+            mm(T.psC[:, 136:137], T.one16[:], T.cab[:, 0:1], True, True, ["one16", "cab"], ["psC:a"])
+            pa = T.psC[:, 136:137]
+            act(T.aa[:, 0:1], pa, F.Identity, ["psC:a"], ["aa0"], bias=b_15)
+            act(T.aa[:, 1:2], T.aa[:, 0:1], F.Identity, ["aa0"], ["aa1"], bias=b_m32)
+            act(T.aa[:, 2:3], T.aa[:, 1:2], F.Identity, ["aa1"], ["aa2"], bias=b_m32, scale=-1.0)
+            act(T.sa[:, 4 * t:4 * t + 1], pa, F.Identity, ["psC:a", "aa2", "sa"], ["sa%d" % t], bias=T.aa[:, 2:3])
+            send(dst, T.la[:, 4 * t:4 * t + 4], T.sa[:, 4 * t:4 * t + 4], ["sa", "sa%d" % t], "ra%d" % t)
+        tt(K0[:, 256:384], T.bg[:], K0[:, 0:128], A.mult, ["bg", "psK0:bn"], ["psK0:gb"])
+        tt(K1[:, 128:256], K1[:, 0:128], T.ad[:], A.mult, ["psK1:0", "ad"], ["psK1:1"])
+        tt(K1[:, 256:384], T.bd2[:], T.psV[:, 256:384], A.mult, ["bd2", "psV:ia"], ["psK1:2"])
+        tt(K1[:, 0:128], K1[:, 128:256], T.ap[:], A.add, ["psK1:1", "ap"], ["psK1:3"])
+        tt(T.t2b[:], K1[:, 256:384], T.bp[:], A.add, ["psK1:2", "bp"], ["t2b"])
+
+        def a_new1():
+            tt(K0[:, 384:512], K0[:, 256:384], T.ea[:], A.mult, ["psK0:gb", "ea"], ["psK0:x"])
+            tt(K0[:, 0:128], K0[:, 384:512], T.ap[:], A.max, ["psK0:x", "ap"], ["psK0:y"])
+            tt(K0[:, 128:256], K0[:, 0:128], T.pp[:], A.max, ["psK0:y", "pp"], ["psK0:z"])
+            tt(T.d2[:], K0[:, 128:256], T.lo[:, 256 * t:256 * t + 128], A.subtract, ["psK0:z", "lo%d" % t], ["d2"])
+
+        def a_new2():
+            tt(K0[:, 256:384], T.d2[:], T.win[:], A.mult, ["d2", "win"], ["psK0:w"])
+            tt(T.sx[:, X + 128:X + 256], K0[:, 256:384], T.lo[:, 256 * t:256 * t + 128], A.add, ["psK0:w", "lo%d" % t], ["na%d" % t])
+
+        tt(K1[:, 128:256], T.t2b[:], K1[:, 0:128], A.max, ["t2b", "psK1:3"], ["psK1:4"])
+        tt(K1[:, 256:384], T.ebz[:], T.psV[:, 384:512], A.mult, ["ebz", "psV:ga"], ["psK1:5"])
+        tt(T.pp[:], K1[:, 128:256], T.sg[:], A.mult, ["psK1:4", "sg"], ["pp"])
+        a_new1()
+        if last:
+            a_new2()
+            send(dst, T.ln[:, 256 * t:256 * t + 128], T.sx[:, X + 128:X + 256], ["na%d" % t], "rn%d" % t)
+        tt(K1[:, 384:512], K1[:, 256:384], T.bp[:], A.max, ["psK1:5", "bp"], ["psK1:6"])
+        tt(T.w2[:], T.psC[:, 128:136], T.dl2[:], A.mult, ["psC:l", "dl2"], ["w2"])
+        tt(T.sx[:, X:X + 128], K1[:, 384:512], T.pp[:], A.max, ["psK1:6", "pp"], ["nb%d" % t])
+        tt(T.w2b[:], T.w2[:], T.dum[:], A.add, ["w2", "dum"], ["w2b"])
+        vc(T.l2[:, 8 * t:8 * t + 8], T.w2b[:], ["w2b"], ["l2%d" % t])
+        if last:
+            return
+        scatter("raw", T.l2[:, 8 * t:8 * t + 8], T.sx[:, X:X + 128], ["l2%d" % t, "nb%d" % t])
+        meet_rest.append(a_new2)
+
+    meet_rest = []
+
+    def new_parts(t):
+        X = 384 * t
+        code_parts(T.sx[:, X:X + 256], ["nb%d" % t, "na%d" % t], T.c1[:], T.c2[:], "n", T.psG[:, 0:256])
+
+    def finish(t, dst):
+        X = 384 * t
+        tt(T.sx[:, X + 256:X + 384], T.psG[:, 128:256], T.c2[:, 128:256], A.add, ["psG:n", "n2"], ["nc%d" % t])
+        tt(T.nbc[:, 128 * t:128 * t + 128], T.psG[:, 0:128], T.c2[:, 0:128], A.add, ["psG:n", "n2"], ["nbc%d" % t])
+        send(dst, T.ln[:, 256 * t:256 * t + 256], T.sx[:, X + 128:X + 384], ["na%d" % t, "nc%d" % t], "rn%d" % t)
+
+    def back_scalar(t):
+        o = 256 * t
+        lk = "ln%d" % t
+        act(T.raw[:, t:2048:16], T.ln[:, o:o + 128], F.Copy, [lk], ["raw"])
+        if t < RO - 1:
+            act(T.cod[:, t:2048:16], T.ln[:, o + 128:o + 256], F.Copy, [lk], ["cod"])
+
+    def back(t):
+        X = 384 * t
+        l2 = T.l2[:, 8 * t:8 * t + 8]
+        if t < RO - 1:
+            scatter("cod", l2, T.nbc[:, 128 * t:128 * t + 128], ["l2%d" % t, "nbc%d" % t, "cod"])
+        scatter("raw", l2, T.sx[:, X:X + 128], ["l2%d" % t, "nb%d" % t, "raw"])
+
+    b_sq = T.pcol[:, 11:12]
+    b_ck = [T.pcol[:, 12 + t:13 + t] for t in range(RO)]
+    for t in range(RO):
+        callee = T.cores[(rank + 1 + t % 7) % N]
+        caller = T.cores[(rank - 1 - t % 7) % N]
+        landed("lo%d" % t, "ro%d" % t)
+        landed("le%d" % t, "re%d" % t)
+        landed("ln%d" % t, "rn%d" % t)
+        if t < RO - 1:
+            landed("la%d" % t, "ra%d" % t)
+        own_parts(t)
+        lane_list(t)
+        vs = VS if t else VS0
+        features(vs)
+        own_send(t, callee)
+        if t == 0:
+            first_parts((0, 1))
+        else:
+            meet_rest.pop()()
+            new_parts(t - 1)
+        scans(vs)
+        if t:
+            finish(t - 1, prev)
+        cand(t, callee)
+        if t == 0:
+            first_parts((2, 3))
+            ts(T.z[:], T.z2[:], 32768.0, None, A.mult, None, ["z2"], ["z"])
+            vc(T.idf[:], T.iz[:, 16:144], ["iz"], ["idf"])
+            ts(T.zn[:], T.z2[:], -32768.0, None, A.mult, None, ["z2"], ["zn"])
+            ms(b_sq, -1024.5 / 1024, ["bx1"])
+            for i in range(RO):
+                ms(b_ck[i], 12.0 + i, ["bx2"])
+            first_cod()
+        expand(t, 0)
+        expand(t, 1)
+        own_side(t)
+        if t:
+            back_scalar(t - 1)
+            back(t - 1)
+        score(t)
+        if t == 0:
+            wait("A", [wr[k][0][1] for k in ("bx1", "bx2")])
+        own_side_scalar(t)
+        partner(t)
+        meet(t, caller)
+        prev = caller
+    back_scalar(RO - 1)
+    back(RO - 1)
+    dma("S", T.yent[:, 0:1024], T.raw[:, 0:1024], ["raw"], [], "dy")
+    dma("A", T.yent[:, 1024:2048], T.raw[:, 1024:2048], ["raw"], [], "dy")
+    for s in tot:
+        wait("G", [(s, tot[s], {})])

@@ -1,43 +1,40 @@
-from concourse.mybir import AluOpType, ActivationFunctionType
+from concourse.mybir import AluOpType, ActivationFunctionType, AxisListType
 
 N = 8
 RO = 4
-M0 = 12582912.0
-MB = M0 * 2048.0
-BIG = 1048576.0
+M0 = 1.5 * 2.0 ** 23
+M16, M32, MB, MN = M0 * 16, M0 * 32, M0 * 2048, M0 * 4096
+OFF = 2.0 ** 23
 W = 2048 + 128
 NE = 8
-M16 = M0 * 16.0
-VS, VS0 = 40, 16
+VS, VS0 = 40, 48
+HA = 3
+SEG = [8 * c * (c + 1) for c in range(9)]
+SPLIT = 6
 
 _F, _B, _I, _H, _U = "float32", "bfloat16", "int32", "float16", "uint16"
 SCRATCH = {}
 for _n, _w, _d in [
-        ("ents", 2048, _I), ("raw", W, _F), ("cod", W, _F), ("st", 2048, _F), ("fw", 4112, _B), ("cf1", 2048, _F), ("cf2", 2048, _F),
-        ("wti", 4, _I), ("kpi", 4, _I), ("bcol", 16, _F),
-        ("ones", 160, _B), ("one16", 128, _B), ("bd0", 128, _B), ("bd", 128, _B), ("z0", 144, _B), ("z1", 144, _B), ("z2", 144, _B),
-        ("z", 144, _B), ("zl", 144, _B), ("zn", 144, _B), ("iz", 160, _B), ("iz0", 160, _H), ("iz1", 160, _H), ("sb", 128, _H), ("wblk", 128, _B),
-        ("fm", 2048, _B), ("cli", 128, _I), ("cl", 128, _U), ("pi", 4, _I), ("pcol", 16, _F), ("p16", 4, _I), ("ii", 8, _I),
-        ("dum", 8, _F), ("dmc", 8, _F), ("ji", 16, _I), ("sti", 64, _I), ("stj", 64, _I),
-        ("i1", 128, _I), ("i2", 128, _I), ("i3", 128, _I), ("lst", 128, _U), ("fg", 2048, _B), ("fs", 2048, _B),
-        ("u1", 128, _I), ("u2", 128, _I), ("u4", 128, _F), ("u5", 128, _I), ("u6", 128, _I),
-        ("se", 512, _U), ("le", 512, _U), ("so", 1024, _F), ("lo", 1024, _F), ("sa", 16, _F), ("la", 16, _F),
-        ("sx", 4 * 384, _F), ("ln", 4 * 256, _F), ("nbc", 512, _F), ("c1", 256, _F), ("c2", 256, _F), ("o1", 128, _F), ("o2", 128, _F),
-        ("ox", 2048, _F), ("dd", 2048, _B), ("da", 2048, _B), ("db", 2048, _B), ("mt", 2048, _B),
-        ("eb", 128, _F), ("key", 128, _F), ("kt", 128, _F), ("ks", 128, _F), ("et", 128, _H), ("rt", 128, _H),
-        ("l1", 8, _U), ("l2", 32, _U), ("dl2", 8, _F), ("w2", 8, _F), ("w2b", 8, _F),
-        ("win", 128, _B), ("wj", 128, _B), ("cab", 4, _B),
-        ("ah", 128, _I), ("al", 128, _I), ("ak", 128, _I), ("ap", 128, _F), ("as2", 128, _F), ("ad", 128, _F), ("ea", 128, _F),
-        ("ac1", 128, _F), ("ac2", 128, _F),
-        ("bg", 128, _F), ("bh", 128, _I), ("bl", 128, _I), ("bk", 128, _I), ("bs", 128, _F), ("bp", 128, _F), ("di", 128, _F),
-        ("dq", 128, _F), ("sg", 128, _F), ("ebz", 128, _F), ("bd2", 128, _F), ("t2b", 128, _F), ("pp", 128, _F), ("d2", 128, _F)]:
+        ("ents", 2048, _I), ("tab", W, _F), ("fin", W, _F), ("st", 2048, _F), ("fw", 4112, _B), ("cf", 2048, _F),
+        ("wti", 4, _I), ("kpi", 4, _I), ("pi", 4, _I), ("pj", 4, _I), ("pcol", 16, _F), ("sti", 64, _I), ("stj", 64, _I),
+        ("ones", 128, _B), ("onef", 128, _F), ("bd0", 128, _B), ("bd", 128, _B), ("wblk", 128, _B), ("w4", 512, _B),
+        ("ramp", 240, _B), ("r16", 128, _B), ("r4", 128, _B), ("cm", 128, _B), ("idb", 128, _B), ("ka0", 128, _B), ("ka", 128, _B),
+        ("kr", 4, _B), ("kb", 4, _F), ("kq", 4, _F), ("k16", 4, _F), ("k8", 4, _F), ("kc", 16, _F), ("uc", 32, _B), ("c2k", 32, _B), ("mx", 4, _F),
+        ("zg", 8, _F), ("zp", 8, _B), ("zn", 8, _B), ("zh", 8, _B), ("cb", 8, _H), ("sel", 32, _H), ("cl", 32, _U), ("c8", 8, _U),
+        ("pmk", 128, _F), ("ri", 576, _H), ("rn", 576, _H), ("mk", 576, _B), ("dmc", 8, _F), ("ls", 32, _F), ("fm", 2048, _B),
+        ("i1", 128, _I), ("i3", 128, _I), ("ly", 128, _F), ("lst", 128, _U), ("fg", 2048, _B), ("fs", 2048, _B),
+        ("ur", 32, _F), ("uu", 32, _F), ("vq", 128, _F), ("u5", 128, _I), ("u6", 128, _I),
+        ("se", 512, _U), ("le", 512, _U), ("so", 512, _F), ("lo", 512, _F), ("sa", 48, _F), ("la", 48, _F),
+        ("sn", 512, _F), ("ln", 512, _F), ("nb", 512, _F), ("lr", 8, _U), ("c1", 128, _F), ("c2", 128, _F), ("c3", 128, _F),
+        ("ox", 512, _F), ("dd", 2048, _B), ("da", 2048, _B), ("db", 2048, _B), ("mt", 2048, _B), ("eh", 512, _H),
+        ("ks", 128, _F), ("p8", 8, _F), ("pe", 128, _H), ("pm", 128, _H), ("l1", 8, _U), ("l2", 32, _U),
+        ("mn", 8, _F), ("y2", 8, _F), ("z2", 8, _F), ("wj", 8, _F), ("aa", 8, _F),
+        ("ah", 128, _I), ("al", 128, _I), ("ak", 128, _I), ("av", 128, _F), ("ap", 128, _F), ("as2", 128, _F), ("ac", 128, _F),
+        ("bg", 128, _F), ("bh", 128, _I), ("bl", 128, _I), ("bk", 128, _I), ("bi", 128, _I), ("bs", 128, _F), ("bp", 128, _F),
+        ("di", 128, _F), ("dq", 128, _F), ("sg", 128, _F), ("bd2", 128, _F), ("t2", 128, _F), ("m2", 128, _F), ("na", 128, _F),
+        ("e1", 128, _F)]:
     SCRATCH[_n] = ("sbuf", [128, _w], _d)
-for _n, _w, _d in [("idf", 128, _F), ("trb", 512, _B), ("big", 1024, _B), ("pb", 1024, _B), ("pc", 1024, _H), ("nc", 1024, _H), ("wg", 240, _B),
-                   ("sq", 512, _B), ("eq", 1024, _B), ("aa", 4, _F)]:
-    SCRATCH[_n] = ("sbuf", [128, _w], _d)
-for _n in ("ji", "sb", "key"):
-    SCRATCH.pop(_n)
-for _n in ("psU", "psK0", "psK1", "psL", "psR", "psC", "psG", "psV"):
+for _n in ("psU", "psK", "psD0", "psD1", "psL", "psA", "psV", "psW"):
     SCRATCH[_n] = ("psum", [128, 512], _F)
 SEMAPHORES = (["sV", "sA", "sP", "sG", "dent", "dsm", "dfe", "dy", "loc"]
               + ["%s%d" % (k, t) for k in ("ro", "re", "rn", "ra") for t in range(RO)])
@@ -142,17 +139,14 @@ def rank_program(g, core, T, topo):
     def mm(out, l, rh, st, sp, r, w):
         op("P", lambda: pe.matmul(out, l, rh, st, sp), r, w)
 
-    def ms(ap, c, w):
-        op("V", lambda: v.memset(ap, c), [], w)
+    def ms(ap, c, w, r=()):
+        op("V", lambda: v.memset(ap, c), list(r), w)
 
-    BC = {}
+    def iota(out, pattern, base, w):
+        op("G", lambda: g.iota(out, pattern, base, 0, allow_small_or_imprecise_dtypes=True), [], w)
 
-    def bias(c):
-        if c not in BC:
-            i = len(BC)
-            BC[c] = i
-            ms(T.bcol[:, i:i + 1], c, ["bc%d" % i])
-        return T.bcol[:, BC[c]:BC[c] + 1]
+    def col(i):
+        return T.pcol[:, i:i + 1]
 
     dma("S", T.ents[:, 0:1024], T.ent[:, 0:1024], [], [], "dent")
     dma("A", T.ents[:, 1024:2048], T.ent[:, 1024:2048], [], [], "dent")
@@ -166,386 +160,352 @@ def rank_program(g, core, T, topo):
     joined("fw", "dfe")
 
     ms(T.ones[:], 1.0, ["ones"])
-    ms(T.big[:], 4096.0, ["big"])
-    op("G", lambda: g.iota(T.sti[:], [[37, 64]], 0, 0), [], ["sti"])
     op("G", lambda: g.iota(T.pi[:, 0:1], [[1, 1]], 0, 1), [], ["pi"])
-    op("G", lambda: g.affine_select(T.bd0[:], T.ones[:, 0:128], [[-16, 8], [0, 16]], A.is_ge, 0.0, 0, 1), ["ones"], ["bd0"])
+    op("G", lambda: g.iota(T.sti[:], [[37, 64]], 0, 0), [], ["sti"])
+    iota(T.ramp[:], [[1, 240]], -112, ["ramp"])
+    op("G", lambda: g.affine_select(T.bd0[:], T.ones[:], [[-16, 8], [0, 16]], A.is_ge, 0.0, 0, 1), ["ones"], ["bd0"])
     op("G", lambda: g.affine_select(T.bd[:], T.bd0[:], [[16, 8], [0, 16]], A.is_ge, 0.0, 15, -1), ["bd0"], ["bd"])
-    op("G", lambda: g.iota(T.cli[:], [[1, 128]], 0, 0), [], ["cli"])
-    op("G", lambda: g.affine_select(T.z0[:], T.ones[:, 0:144], [[-16, 9], [0, 16]], A.is_ge, 0.0, 0, 1), ["ones"], ["z0"])
-    op("G", lambda: g.affine_select(T.z1[:], T.z0[:], [[16, 9], [0, 16]], A.is_ge, 0.0, 15, -1), ["z0"], ["z1"])
-    op("G", lambda: g.affine_select(T.z2[:], T.z1[:], [[0, 9], [1, 16]], A.is_equal, 0.0, -15, 0), ["z1"], ["z2"])
-    op("G", lambda: g.affine_select(T.iz[:], T.ones[:], [[-1, 160]], A.is_equal, 0.0, 16, 1), ["ones"], ["iz"])
-    op("G", lambda: g.iota(T.ii[:], [[16, 8]], 2048, 0), [], ["ii"])
-    op("G", lambda: g.affine_select(T.trb[:], T.big[:, 0:512], [[0, 4], [-1, 128]], A.is_ge, 0.0, 0, 1), ["big"], ["trb"])
-    op("G", lambda: g.affine_select(T.pb[:], T.big[:], [[-16, 8], [0, 128]], A.is_equal, 0.0, -15, 1), ["big"], ["pb"])
+    iota(T.r4[:], [[0, 32], [1, 4]], 0, ["r4"])
+    iota(T.r16[:], [[0, 8], [1, 16]], 0, ["r16"])
+    R = T.ramp[:, 112:240]
+    ms(T.fm[:], 1.0, ["fm0"])
+    ms(T.fm[:, 0:2048:16], 0.0, ["fm"], ["fm0"])
+    ms(T.fw[:, 4096:4112], 0.0, ["fwz"])
+    ms(T.uc[0:64, :], -32.0, ["uc0"])
+    ms(T.uc[64:128, :], 1.0 / 128, ["uc"])
+    ms(T.c2k[:], 2048.0, ["c2k"])
+    ms(T.onef[:], -1.0, ["onef"])
+    ms(T.sa[:], 0.0, ["sa"])
+    ts(T.pj[:, 0:1], T.pi[:, 0:1], 15, None, A.bitwise_and, None, ["pi"], ["pj0"])
+    ts(T.pj[:, 1:2], T.pi[:, 0:1], 2, 3, A.arith_shift_right, A.bitwise_and, ["pi"], ["pj1"])
+    ts(T.pj[:, 2:3], T.pi[:, 0:1], 3, None, A.bitwise_and, None, ["pi"], ["pj2"])
+    ts(T.pj[:, 3:4], T.pi[:, 0:1], 4, None, A.arith_shift_right, None, ["pi"], ["pj3"])
     ts(T.stj[:], T.sti[:], 63, None, A.bitwise_and, None, ["sti"], ["stj"])
-    ts(T.st[:, 0:64], T.stj[:], 2048.0, -17.0, A.mult, A.add, ["stj"], ["st"])
+    vc(T.pcol[:, 0:4], T.pj[:, 0:4], ["pj0", "pj1", "pj2", "pj3"], ["pc"])
+    vc(col(4), T.pi[:, 0:1], ["pi"], ["pc4"])
+    ts(T.st[:, 0:64], T.stj[:], 4096.0, -2065.0 - OFF, A.mult, A.add, ["stj"], ["st"])
     n = 64
     while n < 2048:
         act(T.st[:, n:2 * n], T.st[:, 0:n], F.Copy, ["st"], ["st"])
         n *= 2
-    b_w, b_f, b_w1, b_mb, b_mmb, b_64, b_ea, b_one, b_15, b_m32 = [
-        bias(c) for c in (-8.5, M16, -1024.5, MB, -MB, -64.0, 1.0 / BIG, 1.0, -15.5, M0 * 32)]
-    wait("A", [wr["bc%d" % i][0][1] for i in range(len(BC))])
-    ms(T.fm[:], 1.0, ["fm"])
-    op("V", lambda: v.memset(T.fm[:, 0:2048:16], 0.0), ["fm"], ["fm"])
-    ms(T.fw[:, 4096:4112], 0.0, ["fwz"])
-    ms(T.pcol[:, 8:9], 0.0, ["acol"])
-    ts(T.p16[:, 0:1], T.pi[:, 0:1], 15, None, A.bitwise_and, None, ["pi"], ["p16"])
-    ts(T.p16[:, 1:2], T.pi[:, 0:1], 16, None, A.bitwise_and, None, ["pi"], ["p16b"])
-    ts(T.pcol[:, 3:4], T.p16[:, 0:1], -2048.0, 15 * 2048 - 1023.5, A.mult, A.add, ["p16"], ["pc3"])
-    vc(T.cl[:], T.cli[:], ["cli"], ["cl"])
-    vc(T.pcol[:, 6:7], T.wti[:, 0:1], ["wti"], ["wcol"])
-    vc(T.pcol[:, 7:8], T.kpi[:, 0:1], ["kpi"], ["kcol"])
-    ts(T.wblk[:], T.bd[:], T.pcol[:, 6:7], None, A.mult, None, ["bd", "wcol"], ["wblk"])
+    ts(col(5), col(3), 4.0, col(2), A.mult, A.add, ["pc"], ["pc5"])
+    ts(col(8), col(0), 1024.5, None, A.add, None, ["pc"], ["pc8"])
+    ts(col(9), col(0), 16.0, -1023.5, A.mult, A.add, ["pc"], ["pc9"])
+    ts(T.zg[:], T.ramp[:, 112:120], col(3), None, A.is_equal, None, ["ramp", "pc"], ["zg"])
+    ts(T.mx[:], T.ramp[:, 112:116], col(1), None, A.is_equal, None, ["ramp", "pc"], ["mx"])
+    ts(T.cl[:], T.ramp[:, 112:144], 4.0, col(1), A.mult, A.add, ["ramp", "pc"], ["cl"])
+    vc(T.c8[:], T.ramp[:, 112:120], ["ramp"], ["c8"])
+    ts(T.sel[:], T.ramp[:, 112:144], col(5), None, A.is_equal, None, ["ramp", "pc5"], ["sel"])
+    ts(T.idb[:], R, col(4), None, A.is_equal, None, ["ramp", "pc4"], ["idb"])
+    ts(T.dmc[:], T.ramp[:, 112:120], 16.0, col(8), A.mult, A.add, ["ramp", "pc8"], ["dmc"])
+    ts(T.ls[:, 0:8], T.ramp[:, 112:120], 256.0, col(9), A.mult, A.add, ["ramp", "pc9"], ["ls0"])
+    ts(T.zp[:], T.zg[:], 32768.0, None, A.mult, None, ["zg"], ["zp"])
+    ts(T.zn[:], T.zg[:], -32768.0, None, A.mult, None, ["zg"], ["zn"])
+    ts(T.zh[:], T.zg[:], 16384.0, None, A.mult, None, ["zg"], ["zh"])
+    vc(T.cb[:], T.zg[:], ["zg"], ["cb"])
+    for t in range(1, RO):
+        ts(T.ls[:, 8 * t:8 * t + 8], T.ls[:, 0:8], float(t), None, A.add, None, ["ls0"], ["ls%d" % t])
+    vc(col(6), T.wti[:, 0:1], ["wti"], ["wcol"])
+    vc(col(7), T.kpi[:, 0:1], ["kpi"], ["kcol"])
+    ts(T.ka0[:], T.r4[:], col(1), None, A.is_equal, None, ["r4", "pc"], ["ka0"])
+    ts(T.wblk[:], T.bd[:], col(6), None, A.mult, None, ["bd", "wcol"], ["wblk"])
+    for x in range(4):
+        op("G", lambda: g.affine_select(T.w4[:, 128 * x:128 * x + 128], T.wblk[:], [[0, 8], [1, 4], [0, 4]], A.is_equal, 0.0, -x, 0),
+           ["wblk"], ["w4%d" % x])
+    ts(T.kr[:], T.ramp[:, 112:116], col(2), col(7), A.is_equal, A.mult, ["ramp", "pc", "kcol"], ["kr"])
+    tt(T.ka[:], T.ka0[:], T.bd[:], A.mult, ["ka0", "bd"], ["ka"])
+    mm(T.psL[:, 16:20], T.ka[:], T.kr[:], True, True, ["ka", "kr"], ["psL:k"])
+    ts(T.pmk[:], T.r16[:], col(0), None, A.is_equal, None, ["r16", "pc"], ["pmk"])
+    ts(T.cm[:], T.r16[:], -16.0, 240.0, A.mult, A.add, ["r16"], ["cm"])
+    vc(T.kb[:], T.psL[:, 16:20], ["psL:k"], ["kb"])
+    ts(T.k16[:], T.psL[:, 16:20], 16.0, 2047.5, A.mult, A.add, ["psL:k"], ["k16"])
+    tt(T.kq[:], T.kb[:], T.psL[:, 16:20], A.mult, ["kb", "psL:k"], ["kq"])
+    ts(T.k8[:], T.kq[:], -8.0, -0.375, A.mult, A.add, ["kq"], ["k8"])
 
-    def more_constants():
-        ms(T.one16[:], 0.0625, ["one16"])
-        ms(T.sa[:], 0.0, ["sa"])
-        vc(T.pcol[:, 0:1], T.p16[:, 0:1], ["p16"], ["pc0"])
-        ts(T.pcol[:, 1:2], T.p16[:, 1:2], 0.0, None, A.is_equal, None, ["p16b"], ["pc1"])
-        ts(T.pcol[:, 2:3], T.p16[:, 1:2], 0.0, None, A.is_gt, None, ["p16b"], ["pc2"])
-        ts(T.pc[:], T.pb[:], 2.0 ** -12, None, A.mult, None, ["pb"], ["pc"])
-        ts(T.nc[:], T.pb[:], -2.0 ** -12, None, A.mult, None, ["pb"], ["nc"])
-        ms(T.wg[:], 0.0, ["wg0"])
-        op("V", lambda: v.memset(T.wg[:, 112:128], 1.0), ["wg0"], ["wg"])
-        ts(T.zl[:], T.z2[:], 0.0625, None, A.mult, None, ["z2"], ["zl"])
-        ts(T.iz0[:], T.iz[:], T.pcol[:, 1:2], None, A.mult, None, ["iz", "pc1"], ["iz0"])
-        ts(T.iz1[:], T.iz[:], T.pcol[:, 2:3], None, A.mult, None, ["iz", "pc2"], ["iz1"])
-        ts(T.dum[:], T.ii[:], T.pcol[:, 0:1], None, A.add, None, ["ii", "pc0"], ["dum"])
-        yield
-        ts(T.dmc[:], T.dum[:], -1023.5, None, A.add, None, ["dum"], ["dmc"])
+    def pair_constants():
+        for c in range(8):
+            s, w = slice(SEG[c], SEG[c + 1]), 16 * c + 16
+            ts(T.ri[:, s], T.ramp[:, 112:112 + w], col(4), 4096.0, A.is_equal, A.mult, ["ramp", "pc4"], ["ri"])
+            ts(T.rn[:, s], T.ones[:, 0:w], T.zg[:, c:c + 1], -4096.0, A.mult, A.mult, ["ones", "zg"], ["rn"])
+            ts(T.mk[:, s], T.ramp[:, 112 - 16 * c:128], col(0), 2.0 ** 24, A.is_ge, A.mult, ["ramp", "pc"], ["mk"])
+
+    banks = ["psK", "psD0", "psD1", "psW"]
+    CZ = -(MB + OFF - 2048.0)
+
+    def first_lanes():
+        e = T.ents[:, 0:2048:16]
+        ts(T.e1[:], e, -1024.5, MB, A.add, A.add, ["ents"], ["e1"])
+        ts(T.psV[:, 0:128], T.e1[:], CZ, None, A.add, None, ["e1"], ["psV:0"])
+        tt(T.so[:, 0:128], e, T.psV[:, 0:128], A.add, ["ents", "psV:0"], ["so0"])
+
+    def first_table():
         for i in range(4):
             s = slice(512 * i, 512 * i + 512)
-            vc(T.raw[:, s], T.ents[:, s], ["ents"], ["raw"])
-            if i % 2:
-                yield
-
-    banks = ["psK0", "psK1", "psR", "psC"]
-
-    def first_parts(blocks):
-        for i in blocks:
-            s = slice(512 * i, 512 * i + 512)
-            k = "@%d" % i
-            ts(T.cf1[:, s], T.ents[:, s], -1024.5, MB, A.add, A.add, ["ents"], ["cf1" + k])
-            act(T[banks[i]][:], T.cf1[:, s], F.Identity, ["cf1" + k], [banks[i]], bias=b_mmb)
-            ts(T.cf2[:, s], T.ents[:, s], -8.5, M16, A.add, A.add, ["ents"], ["cf2" + k])
-
-    def first_cod():
+            ts(T.cf[:, s], T.ents[:, s], -1024.5, MB, A.add, A.add, ["ents"], ["cf%d" % i])
+            act(T[banks[i]][:], T.cf[:, s], F.Identity, ["cf%d" % i], [banks[i]], bias=CZ)
         for i in range(4):
             s = slice(512 * i, 512 * i + 512)
-            tt(T.cod[:, s], T[banks[i]][:], T.cf2[:, s], A.add, [banks[i], "cf2@%d" % i], ["cod"])
+            tt(T.tab[:, s], T.ents[:, s], T[banks[i]][:], A.add, [banks[i], "ents"], ["tab"])
 
-    def code_parts(src, sk, t1, t2, k, ps):
-        act(t2, src, F.Identity, sk, [k + "2"], bias=b_w)
-        act(t1, src, F.Identity, sk, [k + "1"], bias=b_w1)
-        act(t2, t2, F.Identity, [k + "2"], [k + "2"], bias=b_f)
-        act(t1, t1, F.Identity, [k + "1"], [k + "1"], bias=b_mb)
-        act(ps, t1, F.Identity, [k + "1"], [("psG:" if k == "n" else "psL:") + k], bias=b_mmb)
-
-    def lane_list(t):
-        src, sk = (T.ents, "ents") if t == 0 else (T.raw, "raw")
-        ts(T.i1[:], src[:, t:2048:16], -1.0, None, A.add, None, [sk], ["i1"])
-        ts(T.i3[:], T.i1[:], 16, None, A.bitwise_and, None, ["i1"], ["i3"])
-        ts(T.i2[:], T.i1[:], 11, None, A.arith_shift_right, None, ["i1"], ["i2"])
-        ts(T.psV[:, 0:128], T.i3[:], 512.0, None, A.mult, None, ["i3"], ["psV:1"])
-        tt(T.psV[:, 128:256], T.i2[:], T.psV[:, 0:128], A.add, ["i2", "psV:1"], ["psV:2"])
-        ts(T.lst[:], T.psV[:, 128:256], 4096.0, None, A.min, None, ["psV:2"], ["lst"])
-
-    def own_parts(t):
-        o = 256 * t
-        if t == 0:
-            vc(T.so[:, 0:128], T.ents[:, 0:2048:16], ["ents"], ["so0"])
-        else:
-            act(T.so[:, o:o + 128], T.raw[:, t:2048:16], F.Copy, ["raw"], ["so%d" % t])
-        code_parts(T.so[:, o:o + 128], ["so%d" % t], T.o1[:], T.o2[:], "o", T.psL[:, 256:384])
-
-    def own_send(t, dst):
-        o = 256 * t
-        tt(T.so[:, o + 128:o + 256], T.psL[:, 256:384], T.o2[:], A.add, ["psL:o", "o2"], ["soc%d" % t])
-        send(dst, T.lo[:, o:o + 256], T.so[:, o:o + 256], ["so%d" % t, "soc%d" % t], "ro%d" % t)
-
-    def features(vs):
-        rk = ["lst", "fw", "fwz"]
-        op("A", lambda: a.activation(T.fg[:, 16 * vs:2048], T.fw[:].indirect(T.lst[:, vs:128]), F.Copy), rk, ["fgA"])
-        op("V", lambda: v.tensor_copy(T.fg[:, 0:16 * vs], T.fw[:].indirect(T.lst[:, 0:vs])), rk, ["fgV"])
-
-    def scans(vs):
-        for n0, n1, k in ((0, vs, "V"), (vs, 128, "A")):
-            c = slice(16 * n0, 16 * n1)
-            op("V", lambda: v.tensor_tensor_scan(T.fs[:, c], T.fm[:, c], T.fg[:, c], 0.0, A.mult, A.max), ["fm", "fg" + k], ["fs" + k])
-        mm(T.psU[:, 0:128], T.wblk[:], T.fs[:, 15:2048:16], True, True, ["wblk", "fsV", "fsA"], ["psU"])
-
-    def cand(t, dst):
+    def lane_list(t, dst):
         o = 128 * t
-        ac, ak = (T.pcol[:, 8:9], "acol") if t == 0 else (T.la[:, 4 * t - 4:4 * t - 3], "la%d" % (t - 1))
-        vc(T.u1[:], T.psU[:, 0:128], ["psU"], ["u1"])
-        ts(T.u2[:], T.u1[:], 4095, None, A.bitwise_and, None, ["u1"], ["u2"])
-        ts(T.psV[:, 0:128], T.u2[:], 0.03125, T.pcol[:, 7:8], A.mult, A.add, ["u2", "kcol"], ["psV:1"])
-        tt(T.u4[:], T.psV[:, 0:128], T.u2[:], A.mult, ["psV:1", "u2"], ["u4"])
-        ts(T.u5[:], T.u4[:], ac, -0.375, A.add, A.add, ["u4", ak], ["u5"])
-        ts(T.u6[:], T.u5[:], 2047, None, A.bitwise_and, None, ["u5"], ["u6"])
+        src, sk = (T.so[:, 0:128], "so0") if t == 0 else (T.tab[:, t:2048:16], "tab")
+        act(T.psA[:, 0:128], src, F.Identity, [sk], ["psA:0"], bias=-2048.75 / 16, scale=2.0 ** -16)
+        if t:
+            act(T.so[:, o:o + 128], src, F.Copy, [sk], ["so%d" % t])
+        send(dst, T.lo[:, o:o + 128], T.so[:, o:o + 128], ["so%d" % t], "ro%d" % t)
+        ts(T.i1[:], src, -2033.0, None, A.add, None, [sk], ["i1"])
+        ts(T.i3[:], T.i1[:], 16, None, A.bitwise_and, None, ["i1"], ["i3"])
+        tt(T.ly[:], T.i3[:], T.psA[:, 0:128], A.mult, ["i3", "psA:0"], ["ly"])
+        ts(T.lst[:], T.ly[:], M0 + 4096.0, -M0, A.add, A.add, ["ly"], ["lst"])
+
+    def gather_scalar(n0, n1, k):
+        op("A", lambda: a.activation(T.fg[:, 16 * n0:16 * n1], T.fw[:].indirect(T.lst[:, n0:n1]), F.Copy), ["lst", "fw", "fwz"], ["fg" + k])
+
+    def gather_vector(n0, n1, k):
+        op("V", lambda: v.tensor_copy(T.fg[:, 16 * n0:16 * n1], T.fw[:].indirect(T.lst[:, n0:n1])), ["lst", "fw", "fwz"], ["fg" + k])
+
+    def scan(n0, n1, k):
+        c = slice(16 * n0, 16 * n1)
+        op("V", lambda: v.tensor_tensor_scan(T.fs[:, c], T.fm[:, c], T.fg[:, c], 0.0, A.mult, A.max), ["fm", "fg" + k], ["fs" + k])
+
+    def cand(t, dst, ks):
+        o = 128 * t
+        U = T.psU[:, 0:32]
+        for x in range(4):
+            mm(U, T.w4[:, 128 * x:128 * x + 128], T.fs[:, 16 * x + 15:2048:64], False, x == 3, ["w4%d" % x] + ["fs" + k for k in ks], ["psU"])
+        kc, kk = T.k8, "k8"
+        if t:
+            kc, kk = T.kc[:, 4 * t:4 * t + 4], "kc"
+            ts(kc, T.k8[:], T.la[:, 12 * t - 4:12 * t - 3], None, A.add, None, ["k8", "la%d" % (t - 1)], ["kc"])
+        ts(T.ur[:], U, MN, -MN, A.add, A.add, ["psU"], ["ur"])
+        tt(T.uu[:], U, T.ur[:], A.subtract, ["psU", "ur"], ["uu"])
+        for b in range(4):
+            s = slice(32 * b, 32 * b + 32)
+            act(T.vq[:, s], T.uu[:], F.Square, ["uu", "k16"], ["vq%d" % b], bias=T.k16[:, b:b + 1])
+            c = 4 * t + b if t else b
+            ts(T.u5[:, s], T.vq[:, s], 0.03125, (T.kc if t else T.k8)[:, c:c + 1], A.mult, A.add, ["vq%d" % b, kk], ["u5%d" % b])
+        ts(T.u6[:], T.u5[:], 2047, None, A.bitwise_and, None, ["u5%d" % b for b in range(4)], ["u6"])
         vc(T.se[:, o:o + 128], T.u6[:], ["u6"], ["se%d" % t])
         send(dst, T.le[:, o:o + 128], T.se[:, o:o + 128], ["se%d" % t], "re%d" % t)
 
-    def scatter(tab, lists, vals, r):
-        op("V", lambda: v.tensor_copy(T[tab][:].indirect(lists), vals), r, [tab])
+    def scatter(tab, lists, vals, r, off):
+        op("V", lambda: v.tensor_scalar(T[tab][:].indirect(lists), vals, 1.0, off, A.mult, A.add), r, [tab])
+
+    PA, PV, PW = T.psA, T.psV, T.psW
+
+    def expand(t):
+        av, lk = T.lo[:, 128 * t:128 * t + 128], "lo%d" % t
+        act(T.c1[:], av, F.Identity, [lk], ["c1"], bias=-8.5)
+        act(PA[:, 0:128], av, F.Identity, [lk], ["psA:0"], bias=OFF)
+        act(T.c2[:], T.c1[:], F.Identity, ["c1"], ["c2"], bias=M16 + 16.0)
+        act(T.c3[:], T.c2[:], F.Identity, ["c2"], ["c3"], bias=-M16 - 16.0)
+        act(T.ox[:], T.c3[:].indirect(T.cl[:]), F.Identity, ["c3", "cl"], ["ox"], bias=8.5)
 
     def own_side(t):
-        o = 256 * t
         th = 8.0 + t
-        av, lk = T.lo[:, o:o + 128], "lo%d" % t
-        tt(T.ah[:], av, T.st[:, t:2048:16], A.add, [lk, "st"], ["ah"])
+        tt(T.ah[:], T.st[:, t:2048:16], PA[:, 0:128], A.add, ["psA:0", "st"], ["ah"])
         ts(T.al[:], T.ah[:], 31, None, A.bitwise_and, None, ["ah"], ["al"])
-        ts(T.ak[:], T.ah[:], 114688, None, A.bitwise_and, None, ["ah"], ["ak"])
-        ts(T.psV[:, 0:128], T.al[:], th, BIG, A.is_ge, A.mult, ["al"], ["psV:1"])
-        ts(T.psV[:, 256:384], T.al[:], 16.0, None, A.is_ge, None, ["al"], ["psV:ia"])
-        tt(T.psV[:, 128:256], T.ak[:], T.psV[:, 0:128], A.is_le, ["ak", "psV:1"], ["psV:2"])
-        tt(T.as2[:], T.al[:], T.psV[:, 0:128], A.add, ["al", "psV:1"], ["as2"])
-        tt(T.psV[:, 384:512], av, T.psV[:, 0:128], A.mult, [lk, "psV:1"], ["psV:ga"])
-        tt(T.ap[:], av, T.psV[:, 128:256], A.mult, [lk, "psV:2"], ["ap"])
+        ts(T.ak[:], T.ah[:], 15, 7, A.arith_shift_right, A.bitwise_and, ["ah"], ["ak"])
+        ts(PV[:, 0:128], T.al[:], th, 64.0, A.is_ge, A.mult, ["al"], ["psV:0"])
+        tt(T.av[:], T.ak[:], PV[:, 0:128], A.is_le, ["ak", "psV:0"], ["av"])
+        tt(T.as2[:], T.al[:], PV[:, 0:128], A.add, ["al", "psV:0"], ["as2"])
+        tt(T.ap[:], T.av[:], PA[:, 0:128], A.mult, ["av", "psA:0"], ["ap"])
 
     def own_side_scalar(t):
-        act(T.ad[:], T.as2[:], F.Relu, ["as2"], ["ad"], bias=b_ck[t], scale=-1.0)
-        act(T.ac1[:], T.ap[:], F.Identity, ["ap"], ["ac1"], bias=b_w1)
-        act(T.ea[:], T.ap[:], F.Relu, ["ap"], ["ea"], bias=b_ea, scale=-1.0 / BIG)
-        act(T.ac2[:], T.ac1[:], F.Identity, ["ac1"], ["ac2"], bias=b_mb)
-        act(T.psG[:, 384:512], T.ac2[:], F.Identity, ["ac2"], ["psG:c"], bias=b_mmb)
-
-    def expand(t, h):
-        o = 256 * t + 128
-        op("A", lambda: a.activation(T.ox[:, 1024 * h:1024 * h + 1024],
-                                     T.lo[:, o:o + 128].indirect(T.cl[:, 64 * h:64 * h + 64]), F.Copy),
-           ["lo%d" % t, "cl"], ["ox%d" % h])
-
-    CH = [0, 32, 64, 104, 128]
-    todo = [more_constants()]
-
-    def fill():
-        return next(todo[0], 1) is None
+        act(T.ac[:], T.ap[:], F.Identity, ["ap"], ["ac"], bias=MN)
+        act(PA[:, 128:256], T.as2[:], F.Relu, ["as2"], ["psA:1"], bias=12.0 + t, scale=-1.0)
+        act(PA[:, 256:384], T.as2[:], F.Relu, ["as2"], ["psA:2"], bias=-1264.0, scale=16.0)
+        act(PA[:, 384:512], T.ac[:], F.Identity, ["ac"], ["psA:3"], bias=-MN)
 
     def score(t):
-        def gat(i):
-            c = slice(16 * CH[i], 16 * CH[i + 1])
-            o = 128 * t
-            op("V", lambda: v.tensor_tensor(T.dd[:, c], T.cod[:, 0:2048].indirect(T.le[:, o + CH[i]:o + CH[i + 1]]), T.ox[:, c], A.subtract),
-               ["cod", "le%d" % t, "ox%d" % (i // 2)], ["dd%d" % i])
-            act(T.da[:, c], T.dd[:, c], F.Abs, ["dd%d" % i], ["da%d" % i], scale=0.0625)
-            if i > 1:
-                act(T.db[:, c], T.da[:, c], F.Abs, ["da%d" % i], ["db%d" % i], bias=b_64)
+        o = 128 * t
+        K = T.psK
+        lk = "le%d" % t
+        mm(K[:, 0:128], T.ones[:], T.cm[:], True, False, ["ones", "cm"], ["psK"])
+        for i in range(HA, 4):
+            mm(K[:, i:128:4], T.ones[:], T.c2k[:], False, False, ["ones", "c2k"], ["psK"])
 
-        def thr(i):
-            c = slice(16 * CH[i], 16 * CH[i + 1])
-            if i > 1:
-                ts(T.mt[:, c], T.db[:, c], 63.75, None, A.is_lt, None, ["db%d" % i], ["mt%d" % i])
-            else:
-                ts(T.mt[:, c], T.da[:, c], 127.5, None, A.is_lt, None, ["da%d" % i], ["mt%d" % i])
+        def sums(i, tile, k, z, last=False):
+            for x in range(4):
+                mm(K[:, 4 * x + i:128:16], tile[:, 512 * i + x:512 * i + 512:4], T[z][:], False, last and x == 3, [k, z], ["psK"])
 
-        def same(i):
-            c = slice(16 * CH[i], 16 * CH[i + 1])
-            ts(T.db[:, c], T.da[:, c], 0.5, None, A.is_lt, None, ["da%d" % i], ["db%d" % i])
+        for i in range(4):
+            c = slice(512 * i, 512 * i + 512)
+            tt(T.dd[:, c], T.tab[:, 0:2048].indirect(T.le[:, o + 32 * i:o + 32 * i + 32]), T.ox[:], A.subtract, ["tab", lk, "ox"], ["dd%d" % i])
+            if i < HA:
+                act(T.da[:, c], T.dd[:, c], F.Abs, ["dd%d" % i], ["da%d" % i])
+                act(T.db[:, c], T.da[:, c], F.Sign, ["da%d" % i], ["db%d" % i], bias=-8.25)
+            if i == 0:
+                for x in range(4):
+                    ts(T.eh[:, x:512:4], T.le[:, o:o + 128], -1023.5, T.mx[:, x:x + 1], A.add, A.mult, [lk, "mx"], ["eh%d" % x])
+                for b in range(4):
+                    mm(K[:, b:128:4], T.eh[:, 128 * b:128 * b + 128], T.sel[:], False, False, ["sel"] + ["eh%d" % x for x in range(4)], ["psK"])
+            ts(T.mt[:, c], T.dd[:, c], MN + 4096.0, MN + 4096.0, A.add, A.is_equal, ["dd%d" % i], ["mt%d" % i])
+            if i and i - 1 < HA:
+                sums(i - 1, T.db, "db%d" % (i - 1), "zh")
+            sums(i, T.mt, "mt%d" % i, "zp")
+            if i >= HA:
+                ts(T.db[:, c], T.dd[:, c], M16, M16, A.add, A.is_equal, ["dd%d" % i], ["db%d" % i])
+                sums(i, T.db, "db%d" % i, "zn", i == 3)
+        if HA == 4:
+            sums(3, T.db, "db3", "zh", True)
 
-        def add(h):
-            k = "psK0:k%d" % h
-            s = slice(64 * h, 64 * h + 64)
-            mm(T.psK0[:, s], T.idf[:], T.eb[:, s], True, False, ["idf", "eb"], [k])
-            for m in range(16):
-                mm(T.psK0[:, s], T.z[:, 15 - m:143 - m], T.mt[:, 1024 * h + m:1024 * h + 1024:16], False, m == 15 and h == 1,
-                   ["z", "mt%d" % (2 * h), "mt%d" % (2 * h + 1)], [k])
-
-        def sub():
-            for m in range(16):
-                mm(T.psK0[:, 0:64], T.zn[:, 15 - m:143 - m], T.db[:, m:1024:16], False, m == 15,
-                   ["zn", "db0", "db1"], ["psK0:k0"])
-
-        gat(0)
-        gat(1)
-        ts(T.eb[:], T.le[:, 128 * t:128 * t + 128], T.pcol[:, 3:4], None, A.add, None, ["le%d" % t, "pc3"], ["eb"])
-        gat(2)
-        thr(0)
-        thr(1)
-        add(0)
-        gat(3)
-        same(0)
-        same(1)
-        sub()
-        fill()
-        thr(2)
-        fill()
-        thr(3)
-        add(1)
-        while fill():
-            pass
+    DB = [("psD0", slice(0, SEG[SPLIT])), ("psD1", slice(SEG[SPLIT], SEG[8]))]
 
     def partner(t):
-        for i, k in enumerate(("psU", "psR")):
-            mm(T[k][:], T.iz[:, 16:144], T.trb[:], True, False, ["iz", "trb"], [k + ":d"])
-        op("V", lambda: v.transpose(T.kt[:], T.psK0[:, 0:128]), ["psK0:k0", "psK0:k1"], ["kt"])
-        op("V", lambda: v.tensor_tensor_scan(T.ks[:], T.fm[:, 0:128], T.kt[:], 0.0, A.mult, A.max), ["fm", "kt"], ["ks"])
-        ts(T.psK1[:, 0:128], T.ks[:], MB, -MB, A.add, A.add, ["ks"], ["psK1:0"])
-        tt(T.et[:], T.ks[:], T.psK1[:, 0:128], A.subtract, ["ks", "psK1:0"], ["et"])
-        for h in range(2):
-            for g2 in range(2):
-                b = 16 - 16 * (g2 - h)
-                mm(T.psL[:, h:8:2], T["iz%d" % h][:, b:b + 128], T.et[:, 16 * g2 + 15:128:32], g2 == 0, g2 == 1,
-                   ["iz%d" % h, "et"], ["psL"])
-        op("V", lambda: v.transpose(T.rt[:], T.et[:]), ["et"], ["rt"])
-        for i, k in enumerate(("psU", "psR")):
-            mm(T[k][:], T.rt[:], T.nc[:, 512 * i:512 * i + 512], False, False, ["rt", "nc"], [k + ":d"])
-            for b in range(4):
-                c = 512 * i + 128 * b
-                mm(T[k][:, 128 * b:128 * b + 128], T.pc[:, c:c + 128], T.rt[:], False, b == 3, ["rt", "pc"], [k + ":d"])
-        act(T.sq[:], T.psU[:], F.Square, ["psU:d"], ["sq"])
-        act(T.eq[:, 0:512], T.sq[:], F.Relu, ["sq"], ["eq0"], bias=b_one, scale=-1.0)
+        for k, s in DB:
+            mm(T[k][:, 0:s.stop - s.start], T.idb[:], T.mk[:, s], True, False, ["idb", "mk"], [k])
+        op("V", lambda: v.tensor_tensor_scan(T.ks[:], T.fm[:, 0:128], T.psK[:, 0:128], 0.0, A.mult, A.max), ["fm", "psK"], ["ks"])
+        ts(PV[:, 128:136], T.ks[:, 15:128:16], MB, -MB, A.add, A.add, ["ks"], ["psV:1"])
+        tt(T.p8[:], T.ks[:, 15:128:16], PV[:, 128:136], A.subtract, ["ks", "psV:1"], ["p8"])
+        tt(T.pm[:], T.p8[:].indirect(T.c8[:]), T.pmk[:], A.mult, ["p8", "c8", "pmk"], ["pm"])
+        mm(T.psL[:, 0:8], T.pm[:], T.cb[:], True, True, ["pm", "cb"], ["psL"])
+        vc(T.pe[:], T.p8[:].indirect(T.c8[:]), ["p8", "c8"], ["pe"])
+        for k, s in DB:
+            mm(T[k][:, 0:s.stop - s.start], T.pm[:], T.rn[:, s], False, False, ["pm", "rn"], [k])
+        for k, s in DB:
+            mm(T[k][:, 0:s.stop - s.start], T.pe[:], T.ri[:, s], False, True, ["pe", "ri"], [k])
         ts(T.l1[:], T.psL[:, 0:8], 1023.5, None, A.add, None, ["psL"], ["l1"])
-        tt(T.dl2[:], T.psL[:, 0:8], T.dmc[:], A.subtract, ["psL", "dmc"], ["dl2"])
-        op("V", lambda: v.tensor_copy(T.bg[:], T.raw[:, 0:2048].indirect(T.l1[:])), ["raw", "l1"], ["bg"])
-        op("V", lambda: v.tensor_tensor(T.bh[:], T.st[:].indirect(T.l1[:]), T.bg[:], A.add), ["st", "l1", "bg"], ["bh"])
+        ts(T.bg[:], T.tab[:, 0:2048].indirect(T.l1[:]), OFF, None, A.add, None, ["tab", "l1"], ["bg"])
+        tt(T.bh[:], T.st[:].indirect(T.l1[:]), T.bg[:], A.add, ["st", "l1", "bg"], ["bh"])
 
-    K0, K1 = T.psK0, T.psK1
+    def winners(t, cs):
+        for c in cs:
+            k, s = DB[c >= SPLIT]
+            op("V", lambda: v.tensor_reduce(T.mn[:, c:c + 1], T[k][:, SEG[c] - s.start:SEG[c + 1] - s.start], AxisListType.X, A.min,
+                                            negate=True, apply_absolute_value=True), [k], ["mn%d" % c])
+
+    def lists(t, dst):
+        mk = ["mn%d" % c for c in range(8)]
+        o = 12 * t
+        tt(T.y2[:], T.mn[:], T.dmc[:], A.add, mk + ["dmc"], ["y2"])
+        if t < RO - 1:
+            op("A", lambda: a.activation(T.wj[:], T.mn[:], F.Sign, accum_out=T.aa[:, 0:1]), mk, ["wj", "aa0"])
+            mm(T.psU[:, 64:65], T.onef[:], T.aa[:, 0:1], True, True, ["onef", "aa0"], ["psU"])
+            pa = T.psU[:, 64:65]
+            act(T.aa[:, 1:2], pa, F.Identity, ["psU"], ["aa1"], bias=-15.5)
+            act(T.aa[:, 2:3], T.aa[:, 1:2], F.Identity, ["aa1"], ["aa2"], bias=M32)
+            act(T.aa[:, 3:4], T.aa[:, 2:3], F.Identity, ["aa2"], ["aa3"], bias=M32, scale=-1.0)
+            act(T.sa[:, o + 8:o + 9], pa, F.Identity, ["psU", "aa3", "sa"], ["sb%d" % t], bias=T.aa[:, 3:4])
+        tt(T.sa[:, o:o + 8], T.y2[:], T.ls[:, 8 * t:8 * t + 8], A.max, ["y2", "ls%d" % t, "sa"], ["sa%d" % t])
+        send(dst, T.la[:, o:o + 12], T.sa[:, o:o + 12], ["sa", "sa%d" % t, "sb%d" % t], "ra%d" % t)
+        tt(T.z2[:], T.y2[:], T.psL[:, 0:8], A.max, ["y2", "psL"], ["z2"])
+        ts(T.l2[:, 8 * t:8 * t + 8], T.z2[:], 1023.5, None, A.add, None, ["z2"], ["l2%d" % t])
+
+    def to_numbers(out, y, r, w):
+        ts(T.e1[:], y, 0.5, MB, A.mult, A.add, r, ["e1"])
+        ts(PV[:, 128:256], T.e1[:], -MB, None, A.add, None, ["e1"], ["psV:1"])
+        tt(out, y, PV[:, 128:256], A.subtract, r + ["psV:1"], w)
+
+    def lane_new(t, dst):
+        o = 128 * t
+        last = t == RO - 1
+        tt(PV[:, 128:256], T.ap[:], PW[:, 0:128], A.is_lt, ["ap", "psW:0"], ["psV:1"])
+        tt(T.m2[:], T.sg[:], PV[:, 128:256], A.max, ["sg", "psV:1"], ["m2"])
+        tt(PV[:, 256:384], T.m2[:], PW[:, 384:512], A.mult, ["m2", "psW:3"], ["psV:2"])
+        tt(T.na[:] if last else T.sn[:, o:o + 128], T.ap[:], PV[:, 256:384], A.max, ["ap", "psV:2"], ["na" if last else "sn%d" % t])
+        if last:
+            to_numbers(T.sn[:, o:o + 128], T.na[:], ["na"], ["sn%d" % t])
+        send(dst, T.ln[:, o:o + 128], T.sn[:, o:o + 128], ["sn%d" % t], "rn%d" % t)
 
     def meet(t, dst):
         th = 8.0 + t
-        X = 384 * t
+        o = 128 * t
         last = t == RO - 1
         ts(T.bl[:], T.bh[:], 31, None, A.bitwise_and, None, ["bh"], ["bl"])
-        ts(T.bk[:], T.bh[:], 114688, None, A.bitwise_and, None, ["bh"], ["bk"])
-        ts(K0[:, 0:128], T.bl[:], th, BIG, A.is_ge, A.mult, ["bl"], ["psK0:bn"])
-        ts(K1[:, 0:128], T.bl[:], 16.0, None, A.is_ge, None, ["bl"], ["psK1:0"])
-        tt(K0[:, 128:256], T.bk[:], K0[:, 0:128], A.is_le, ["bk", "psK0:bn"], ["psK0:bv"])
-        tt(T.bs[:], T.bl[:], K0[:, 0:128], A.add, ["bl", "psK0:bn"], ["bs"])
-        act(T.bd2[:], T.bs[:], F.Relu, ["bs"], ["bd2"], bias=b_ck[t], scale=-1.0)
-        tt(T.bp[:], T.bg[:], K0[:, 128:256], A.mult, ["bg", "psK0:bv"], ["bp"])
-        ts(T.eq[:, 512:1024], T.psR[:], 0.0, None, A.is_equal, None, ["psR:d"], ["eq1"])
-        for c in range(8):
-            mm(T.psC[:, 0:128], T.wg[:, 112 - 16 * c:240 - 16 * c], T.eq[:, 128 * c:128 * c + 128], c == 0, c == 7,
-               ["wg", "eq%d" % (c // 4)], ["psC"])
-        tt(T.di[:], T.bp[:], T.psG[:, 384:512], A.subtract, ["bp", "psG:c"], ["di"])
-        act(T.dq[:], T.di[:], F.Square, ["di"], ["dq"], bias=b_sq, scale=1.0 / 1024)
-        act(T.sg[:], T.dq[:], F.Sign, ["dq"], ["sg"], bias=b_one, scale=-1.0)
-        act(T.ebz[:], T.bp[:], F.Relu, ["bp"], ["ebz"], bias=b_ea, scale=-1.0 / BIG)
-        act(T.win[:], T.psC[:, 0:128], F.Relu, ["psC"], ["win"], bias=b_one, scale=-1.0)
-        for s in range(16):
-            mm(T.psC[:, 128:136], T.zl[:, 15 - s:143 - s], T.win[:, s:128:16], s == 0, s == 15, ["zl", "win"], ["psC:l"])
-        if not last:
-            op("A", lambda: a.activation(T.wj[:], T.win[:], F.Copy, accum_out=T.pcol[:, 9:10]), ["win"], ["wj", "ca"])
-            act(T.cab[:, 0:1], T.pcol[:, 9:10], F.Copy, ["ca"], ["cab"])
-            mm(T.psC[:, 136:137], T.one16[:], T.cab[:, 0:1], True, True, ["one16", "cab"], ["psC:a"])
-            pa = T.psC[:, 136:137]
-            act(T.aa[:, 0:1], pa, F.Identity, ["psC:a"], ["aa0"], bias=b_15)
-            act(T.aa[:, 1:2], T.aa[:, 0:1], F.Identity, ["aa0"], ["aa1"], bias=b_m32)
-            act(T.aa[:, 2:3], T.aa[:, 1:2], F.Identity, ["aa1"], ["aa2"], bias=b_m32, scale=-1.0)
-            act(T.sa[:, 4 * t:4 * t + 1], pa, F.Identity, ["psC:a", "aa2", "sa"], ["sa%d" % t], bias=T.aa[:, 2:3])
-            send(dst, T.la[:, 4 * t:4 * t + 4], T.sa[:, 4 * t:4 * t + 4], ["sa", "sa%d" % t], "ra%d" % t)
-        tt(K0[:, 256:384], T.bg[:], K0[:, 0:128], A.mult, ["bg", "psK0:bn"], ["psK0:gb"])
-        tt(K1[:, 128:256], K1[:, 0:128], T.ad[:], A.mult, ["psK1:0", "ad"], ["psK1:1"])
-        tt(K1[:, 256:384], T.bd2[:], T.psV[:, 256:384], A.mult, ["bd2", "psV:ia"], ["psK1:2"])
-        tt(K1[:, 0:128], K1[:, 128:256], T.ap[:], A.add, ["psK1:1", "ap"], ["psK1:3"])
-        tt(T.t2b[:], K1[:, 256:384], T.bp[:], A.add, ["psK1:2", "bp"], ["t2b"])
+        ts(T.bk[:], T.bh[:], 15, 7, A.arith_shift_right, A.bitwise_and, ["bh"], ["bk"])
+        ts(PW[:, 0:128], T.bl[:], th, 64.0, A.is_ge, A.mult, ["bl"], ["psW:0"])
+        ts(T.bi[:], T.bh[:], 16, None, A.bitwise_and, None, ["bh"], ["bi"])
+        tt(PW[:, 128:256], T.bk[:], PW[:, 0:128], A.is_le, ["bk", "psW:0"], ["psW:1"])
+        tt(T.bs[:], T.bl[:], PW[:, 0:128], A.add, ["bl", "psW:0"], ["bs"])
+        act(T.bd2[:], T.bs[:], F.Relu, ["bs"], ["bd2"], bias=12.0 + t, scale=-1.0)
+        tt(T.bp[:], T.bg[:], PW[:, 128:256], A.mult, ["bg", "psW:1"], ["bp"])
+        tt(PW[:, 256:384], T.bi[:], PA[:, 128:256], A.min, ["bi", "psA:1"], ["psW:2"])
+        tt(T.di[:], T.bp[:], PA[:, 384:512], A.subtract, ["bp", "psA:3"], ["di"])
+        act(T.dq[:], T.di[:], F.Square, ["di"], ["dq"], scale=1.0 / 2048)
+        act(T.sg[:], T.dq[:], F.Sign, ["dq"], ["sg"], bias=1.0, scale=-1.0)
+        tt(PW[:, 128:256], T.bd2[:], PA[:, 256:384], A.min, ["bd2", "psA:2"], ["psW:1"])
+        winners(t, range(0, 3))
+        tt(PW[:, 256:384], T.ap[:], PW[:, 256:384], A.add, ["ap", "psW:2"], ["psW:2"])
+        tt(T.t2[:], T.bp[:], PW[:, 128:256], A.add, ["bp", "psW:1"], ["t2"])
+        tt(PV[:, 128:256], T.bp[:], PV[:, 0:128], A.is_lt, ["bp", "psV:0"], ["psV:1"])
+        tt(PW[:, 384:512], T.t2[:], PW[:, 256:384], A.max, ["t2", "psW:2"], ["psW:3"])
+        winners(t, range(3, 8))
 
-        def a_new1():
-            tt(K0[:, 384:512], K0[:, 256:384], T.ea[:], A.mult, ["psK0:gb", "ea"], ["psK0:x"])
-            tt(K0[:, 0:128], K0[:, 384:512], T.ap[:], A.max, ["psK0:x", "ap"], ["psK0:y"])
-            tt(K0[:, 128:256], K0[:, 0:128], T.pp[:], A.max, ["psK0:y", "pp"], ["psK0:z"])
-            tt(T.d2[:], K0[:, 128:256], T.lo[:, 256 * t:256 * t + 128], A.subtract, ["psK0:z", "lo%d" % t], ["d2"])
+        def site_new():
+            tt(T.t2[:], T.sg[:], PV[:, 384:512] if last else PV[:, 128:256], A.max, ["sg", "psV:3" if last else "psV:1"], ["t2"])
+            tt(PV[:, 256:384], T.t2[:], PW[:, 384:512], A.mult, ["t2", "psW:3"], ["psV:2"])
+            tt(T.na[:] if last else T.nb[:, o:o + 128], T.bp[:], PV[:, 256:384], A.max, ["bp", "psV:2"], ["na" if last else "nb%d" % t])
 
-        def a_new2():
-            tt(K0[:, 256:384], T.d2[:], T.win[:], A.mult, ["d2", "win"], ["psK0:w"])
-            tt(T.sx[:, X + 128:X + 256], K0[:, 256:384], T.lo[:, 256 * t:256 * t + 128], A.add, ["psK0:w", "lo%d" % t], ["na%d" % t])
-
-        tt(K1[:, 128:256], T.t2b[:], K1[:, 0:128], A.max, ["t2b", "psK1:3"], ["psK1:4"])
-        tt(K1[:, 256:384], T.ebz[:], T.psV[:, 384:512], A.mult, ["ebz", "psV:ga"], ["psK1:5"])
-        tt(T.pp[:], K1[:, 128:256], T.sg[:], A.mult, ["psK1:4", "sg"], ["pp"])
-        a_new1()
         if last:
-            a_new2()
-            send(dst, T.ln[:, 256 * t:256 * t + 128], T.sx[:, X + 128:X + 256], ["na%d" % t], "rn%d" % t)
-        tt(K1[:, 384:512], K1[:, 256:384], T.bp[:], A.max, ["psK1:5", "bp"], ["psK1:6"])
-        tt(T.w2[:], T.psC[:, 128:136], T.dl2[:], A.mult, ["psC:l", "dl2"], ["w2"])
-        tt(T.sx[:, X:X + 128], K1[:, 384:512], T.pp[:], A.max, ["psK1:6", "pp"], ["nb%d" % t])
-        tt(T.w2b[:], T.w2[:], T.dum[:], A.add, ["w2", "dum"], ["w2b"])
-        vc(T.l2[:, 8 * t:8 * t + 8], T.w2b[:], ["w2b"], ["l2%d" % t])
-        if last:
-            return
-        scatter("raw", T.l2[:, 8 * t:8 * t + 8], T.sx[:, X:X + 128], ["l2%d" % t, "nb%d" % t])
-        meet_rest.append(a_new2)
-
-    meet_rest = []
-
-    def new_parts(t):
-        X = 384 * t
-        code_parts(T.sx[:, X:X + 256], ["nb%d" % t, "na%d" % t], T.c1[:], T.c2[:], "n", T.psG[:, 0:256])
-
-    def finish(t, dst):
-        X = 384 * t
-        tt(T.sx[:, X + 256:X + 384], T.psG[:, 128:256], T.c2[:, 128:256], A.add, ["psG:n", "n2"], ["nc%d" % t])
-        tt(T.nbc[:, 128 * t:128 * t + 128], T.psG[:, 0:128], T.c2[:, 0:128], A.add, ["psG:n", "n2"], ["nbc%d" % t])
-        send(dst, T.ln[:, 256 * t:256 * t + 256], T.sx[:, X + 128:X + 384], ["na%d" % t, "nc%d" % t], "rn%d" % t)
-
-    def back_scalar(t):
-        o = 256 * t
-        lk = "ln%d" % t
-        act(T.raw[:, t:2048:16], T.ln[:, o:o + 128], F.Copy, [lk], ["raw"])
-        if t < RO - 1:
-            act(T.cod[:, t:2048:16], T.ln[:, o + 128:o + 256], F.Copy, [lk], ["cod"])
+            lists(t, dst)
+            lane_new(t, dst)
+            tt(PV[:, 384:512], T.bp[:], PV[:, 0:128], A.is_lt, ["bp", "psV:0"], ["psV:3"])
+            site_new()
+            to_numbers(T.nb[:, o:o + 128], T.na[:], ["na"], ["nb%d" % t])
+        else:
+            lists(t, dst)
+            site_new()
+            scatter("tab", T.l2[:, 8 * t:8 * t + 8], T.nb[:, o:o + 128], ["l2%d" % t, "nb%d" % t], -OFF)
 
     def back(t):
-        X = 384 * t
-        l2 = T.l2[:, 8 * t:8 * t + 8]
-        if t < RO - 1:
-            scatter("cod", l2, T.nbc[:, 128 * t:128 * t + 128], ["l2%d" % t, "nbc%d" % t, "cod"])
-        scatter("raw", l2, T.sx[:, X:X + 128], ["l2%d" % t, "nb%d" % t, "raw"])
+        o = 128 * t
+        tab, off = ("tab", -OFF) if t < RO - 1 else ("fin", 0.0)
+        ts(T.lr[:], T.la[:, 12 * t:12 * t + 8], 1023.5, None, A.add, None, ["la%d" % t], ["lr"])
+        scatter(tab, T.lr[:], T.ln[:, o:o + 128], ["lr", "ln%d" % t, tab], off)
+        scatter(tab, T.l2[:, 8 * t:8 * t + 8], T.nb[:, o:o + 128], ["l2%d" % t, "nb%d" % t, tab], off)
 
-    b_sq = T.pcol[:, 11:12]
-    b_ck = [T.pcol[:, 12 + t:13 + t] for t in range(RO)]
+    last_banks = ["psK", "psU", "psD0", "psD1"]
+
+    def last_table(step):
+        for i in range(4):
+            s = slice(512 * i, 512 * i + 512)
+            if step == 0:
+                act(T.cf[:, s], T.tab[:, s], F.Identity, ["tab"], ["cf%d" % i], bias=MB, scale=0.5)
+            elif step == 1:
+                act(T[last_banks[i]][:], T.cf[:, s], F.Identity, ["cf%d" % i], [last_banks[i]], bias=-MB - OFF / 2)
+            else:
+                tt(T.fin[:, s], T.tab[:, s], T[last_banks[i]][:], A.subtract, ["tab", last_banks[i]], ["fin"])
+
+    first_lanes()
     for t in range(RO):
         callee = T.cores[(rank + 1 + t % 7) % N]
         caller = T.cores[(rank - 1 - t % 7) % N]
-        landed("lo%d" % t, "ro%d" % t)
-        landed("le%d" % t, "re%d" % t)
-        landed("ln%d" % t, "rn%d" % t)
-        if t < RO - 1:
-            landed("la%d" % t, "ra%d" % t)
-        own_parts(t)
-        lane_list(t)
+        for k, s in (("lo", "ro"), ("le", "re"), ("ln", "rn"), ("la", "ra")):
+            landed("%s%d" % (k, t), "%s%d" % (s, t))
+        lane_list(t, callee)
+        mm(T.psU[:, 0:32], T.ones[:], T.uc[:], True, False, ["ones", "uc0", "uc"], ["psU"])
         vs = VS if t else VS0
-        features(vs)
-        own_send(t, callee)
+        mid = (vs + 128) // 4 * 2
         if t == 0:
-            first_parts((0, 1))
-        else:
-            meet_rest.pop()()
-            new_parts(t - 1)
-        scans(vs)
+            first_table()
+        gather_scalar(vs, mid, "A")
+        gather_scalar(mid, 128, "B")
         if t:
-            finish(t - 1, prev)
-        cand(t, callee)
-        if t == 0:
-            first_parts((2, 3))
-            ts(T.z[:], T.z2[:], 32768.0, None, A.mult, None, ["z2"], ["z"])
-            vc(T.idf[:], T.iz[:, 16:144], ["iz"], ["idf"])
-            ts(T.zn[:], T.z2[:], -32768.0, None, A.mult, None, ["z2"], ["zn"])
-            ms(b_sq, -1024.5 / 1024, ["bx1"])
-            for i in range(RO):
-                ms(b_ck[i], 12.0 + i, ["bx2"])
-            first_cod()
-        expand(t, 0)
-        expand(t, 1)
+            lane_new(t - 1, prev)
+        gather_vector(0, vs, "V")
+        scan(0, vs, "V")
+        scan(vs, mid, "A")
+        scan(mid, 128, "B")
+        cand(t, callee, "VAB")
+        expand(t)
         own_side(t)
-        if t:
-            back_scalar(t - 1)
-            back(t - 1)
-        score(t)
-        if t == 0:
-            wait("A", [wr[k][0][1] for k in ("bx1", "bx2")])
         own_side_scalar(t)
+        if t:
+            back(t - 1)
+        else:
+            pair_constants()
+        score(t)
+        if t == RO - 1:
+            last_table(0)
         partner(t)
         meet(t, caller)
         prev = caller
-    back_scalar(RO - 1)
+    last_table(1)
+    last_table(2)
     back(RO - 1)
-    dma("S", T.yent[:, 0:1024], T.raw[:, 0:1024], ["raw"], [], "dy")
-    dma("A", T.yent[:, 1024:2048], T.raw[:, 1024:2048], ["raw"], [], "dy")
+    dma("S", T.yent[:, 0:1024], T.fin[:, 0:1024], ["fin"], [], "dy")
+    dma("A", T.yent[:, 1024:2048], T.fin[:, 1024:2048], ["fin"], [], "dy")
     for s in tot:
         wait("G", [(s, tot[s], {})])

@@ -5,39 +5,100 @@ RO = 4
 M0 = 1.5 * 2.0 ** 23
 M16, M32, MB, MN = M0 * 16, M0 * 32, M0 * 2048, M0 * 4096
 OFF = 2.0 ** 23
-W = 2048 + 128
+SP = 128
+W = SP + 2048
 NE = 8
-VS, VS0 = 40, 48
-HA = 3
-SEG = [8 * c * (c + 1) for c in range(9)]
+VS, VS0 = 56, 56
+HA = 2
+SEG = [8 * c * (c + 1) + c for c in range(9)]
 SPLIT = 6
+HOP, FLIGHT, LATE, SLACK = 240, 2700, 4000, 120
+GATHER, SCATTER = 1.5, 3.8
+LOADED = {"wti": 2400, "kpi": 2400, "ents": 5600, "fw": 9400}
 
 _F, _B, _I, _H, _U = "float32", "bfloat16", "int32", "float16", "uint16"
 SCRATCH = {}
 for _n, _w, _d in [
         ("ents", 2048, _I), ("tab", W, _F), ("fin", W, _F), ("st", 2048, _F), ("fw", 4112, _B), ("cf", 2048, _F),
         ("wti", 4, _I), ("kpi", 4, _I), ("pi", 4, _I), ("pj", 4, _I), ("pcol", 16, _F), ("sti", 64, _I), ("stj", 64, _I),
-        ("ones", 128, _B), ("onef", 128, _F), ("bd0", 128, _B), ("bd", 128, _B), ("wblk", 128, _B), ("w4", 512, _B),
+        ("ones", 128, _B), ("half", 128, _F), ("bd0", 128, _B), ("bd", 128, _B), ("wblk", 128, _B), ("w4", 512, _B),
         ("ramp", 240, _B), ("r16", 128, _B), ("r4", 128, _B), ("cm", 128, _B), ("idb", 128, _B), ("ka0", 128, _B), ("ka", 128, _B),
-        ("kr", 4, _B), ("kb", 4, _F), ("kq", 4, _F), ("k16", 4, _F), ("k8", 4, _F), ("kc", 16, _F), ("uc", 32, _B), ("c2k", 32, _B), ("mx", 4, _F),
-        ("zg", 8, _F), ("zp", 8, _B), ("zn", 8, _B), ("zh", 8, _B), ("cb", 8, _H), ("sel", 32, _H), ("cl", 32, _U), ("c8", 8, _U),
-        ("pmk", 128, _F), ("ri", 576, _H), ("rn", 576, _H), ("mk", 576, _B), ("dmc", 8, _F), ("ls", 32, _F), ("fm", 2048, _B),
+        ("kr", 4, _B), ("kb", 4, _F), ("kq", 4, _F), ("k16", 4, _F), ("k8", 4, _F), ("kc", 4, _F), ("uc", 32, _B), ("c2k", 32, _B),
+        ("mx", 4, _F), ("zg", 8, _F), ("zp", 8, _B), ("zn", 8, _B), ("zh", 8, _B), ("cb", 8, _H), ("sel", 32, _H), ("cl", 32, _U),
+        ("c8", 8, _U), ("pmk", 128, _F), ("ri", 584, _H), ("rn", 584, _H), ("mk", 584, _B), ("spc", 8, _F), ("ls", 8, _F),
+        ("hd", 32, _F), ("md", 32, _F), ("rx", 136, _B), ("ramp2", 128, _B), ("am", 8, _F), ("fm", 2048, _B),
         ("i1", 128, _I), ("i3", 128, _I), ("ly", 128, _F), ("lst", 128, _U), ("fg", 2048, _B), ("fs", 2048, _B),
         ("ur", 32, _F), ("uu", 32, _F), ("vq", 128, _F), ("u5", 128, _I), ("u6", 128, _I),
         ("se", 512, _U), ("le", 512, _U), ("so", 512, _F), ("lo", 512, _F), ("sa", 48, _F), ("la", 48, _F),
         ("sn", 512, _F), ("ln", 512, _F), ("nb", 512, _F), ("lr", 8, _U), ("c1", 128, _F), ("c2", 128, _F), ("c3", 128, _F),
         ("ox", 512, _F), ("dd", 2048, _B), ("da", 2048, _B), ("db", 2048, _B), ("mt", 2048, _B), ("eh", 512, _H),
         ("ks", 128, _F), ("p8", 8, _F), ("pe", 128, _H), ("pm", 128, _H), ("l1", 8, _U), ("l2", 32, _U),
-        ("mn", 8, _F), ("y2", 8, _F), ("z2", 8, _F), ("wj", 8, _F), ("aa", 8, _F),
+        ("mn", 8, _F), ("y2", 8, _F), ("wj", 8, _F), ("aa", 8, _F),
         ("ah", 128, _I), ("al", 128, _I), ("ak", 128, _I), ("av", 128, _F), ("ap", 128, _F), ("as2", 128, _F), ("ac", 128, _F),
-        ("bg", 128, _F), ("bh", 128, _I), ("bl", 128, _I), ("bk", 128, _I), ("bi", 128, _I), ("bs", 128, _F), ("bp", 128, _F),
-        ("di", 128, _F), ("dq", 128, _F), ("sg", 128, _F), ("bd2", 128, _F), ("t2", 128, _F), ("m2", 128, _F), ("na", 128, _F),
-        ("e1", 128, _F)]:
+        ("ar", 128, _F), ("bg", 128, _F), ("bh", 128, _I), ("bl", 128, _I), ("bk", 128, _I), ("bi", 128, _I), ("bp", 128, _F),
+        ("di", 128, _F), ("dq", 128, _F), ("sg", 128, _F), ("t2", 128, _F), ("m2", 128, _F), ("m3", 128, _F), ("na", 128, _F),
+        ("nc", 128, _F), ("y3", 128, _F), ("y4", 128, _F), ("smv", 128, _F)]:
     SCRATCH[_n] = ("sbuf", [128, _w], _d)
 for _n in ("psU", "psK", "psD0", "psD1", "psL", "psA", "psV", "psW"):
     SCRATCH[_n] = ("psum", [128, 512], _F)
 SEMAPHORES = (["sV", "sA", "sP", "sG", "dent", "dsm", "dfe", "dy", "loc"]
               + ["%s%d" % (k, t) for k in ("ro", "re", "rn", "ra") for t in range(RO)])
+
+
+def plan(calls):
+    n = len(calls)
+    pre = [dict() for _ in calls]
+    wr, rd = {}, {}
+    for i, (q, c, r, w) in enumerate(calls):
+        for k in r:
+            if k in wr:
+                pre[i][wr[k]] = HOP
+            elif k[1:] in wr and k[0] == "~":
+                pre[i].setdefault(wr[k[1:]], 0)
+        for k in w:
+            for j in rd.get(k, []) + ([wr[k]] if k in wr else []):
+                if j != i:
+                    pre[i][j] = max(pre[i].get(j, 0), 0 if calls[j][0] == q else HOP)
+        for k in w:
+            wr[k], rd[k] = i, []
+        for k in r:
+            rd.setdefault(k, []).append(i)
+    post = [[] for _ in calls]
+    way = [0] * n
+    for i in range(n - 1, -1, -1):
+        way[i] += calls[i][1]
+        for j, h in pre[i].items():
+            post[j].append(i)
+            way[j] = max(way[j], way[i] + h)
+    banks = [set(k.split(":")[0] for k in r + w if k[:2] == "ps") for q, c, r, w in calls]
+    left = [len(p) for p in pre]
+    ready = [i for i in range(n) if not left[i]]
+    end, free, used, order = [0] * n, {}, {}, []
+
+    def earliest(i):
+        q = calls[i][0]
+        t = max([free.get(q, 0) if q != "R" else 0] + [end[j] + h for j, h in pre[i].items()])
+        return max([t] + [e + HOP for b in banks[i] for o, e in used.get(b, {}).items() if o != q])
+
+    while ready:
+        at = {i: earliest(i) for i in ready}
+        i = min(ready, key=lambda j: (at[j], -way[j]))
+        q = calls[i][0]
+        mine = [j for j in ready if calls[j][0] == q]
+        if q != "R":
+            fits = [j for j in mine if all(way[o] <= way[j] or at[j] + calls[j][1] <= at[o] + SLACK for o in mine)]
+            i = min(fits, key=lambda j: (at[j], -way[j]))
+        ready.remove(i)
+        end[i] = at[i] + calls[i][1]
+        free[q] = end[i]
+        for b in banks[i]:
+            used.setdefault(b, {})[q] = end[i]
+        order.append((at[i], len(order), i))
+        for j in post[i]:
+            left[j] -= 1
+            if not left[j]:
+                ready.append(j)
+    return [i for t, k, i in sorted(order)]
 
 
 def rank_program(g, core, T, topo):
@@ -51,6 +112,7 @@ def rank_program(g, core, T, topo):
     seen = {"V": {}, "A": {}, "P": {}, "G": {}, "S": {}}
     wr, rd, bank = {}, {}, {}
     v, a, pe = g.vector, g.scalar, g.tensor
+    calls, acts = [], []
 
     def wait(q, evs):
         evs = [e for e in evs if seen[q].get(e[0], 0) < e[1]]
@@ -88,14 +150,22 @@ def rank_program(g, core, T, topo):
             if k[:2] == "ps":
                 bank.setdefault(k.split(":")[0], {})[q] = ev
 
-    def op(q, fn, r, w):
-        wait(q, deps(q, r, w))
-        s = "s" + q
-        tot[s] = tot.get(s, 0) + 1
-        fn().then_inc(T.sem[s], 1)
-        clk = dict(seen[q])
-        clk[s] = tot[s]
-        note(q, r, w, (s, tot[s], clk))
+    def parts(keys):
+        return [p for k in keys for p in (["%s:%d" % (k, i) for i in range(4)] if k[:2] == "ps" and ":" not in k else [k])]
+
+    def op(q, fn, r, w, c):
+        r, w = parts(r), parts(w)
+
+        def issue():
+            wait(q, deps(q, r, w))
+            s = "s" + q
+            tot[s] = tot.get(s, 0) + 1
+            fn().then_inc(T.sem[s], 1)
+            clk = dict(seen[q])
+            clk[s] = tot[s]
+            note(q, r, w, (s, tot[s], clk))
+        calls.append((q, c, r, w))
+        acts.append(issue)
 
     def dma(q, out, in_, r, w, s):
         wait(q, deps("D" + q, r, w))
@@ -105,407 +175,402 @@ def rank_program(g, core, T, topo):
         clk[s] = tot[s]
         note("D", r, w, (s, tot[s], clk))
 
-    def joined(k, s):
-        wr[k] = [("D", (s, tot[s], {s: tot[s]}))]
+    def arrives(k, s, n, c, r):
+        def issue():
+            tot[s] = n
+            wr[k] = [("R", (s, n, {s: n}))]
+        calls.append(("R", c, r, [k]))
+        acts.append(issue)
 
-    def send(dst, out, in_, r, s):
-        wait("G", deps("G", r, []))
-        rid, pid = topo.addr(dst)[:2]
-        m = 0
-        for e in topo.engines(core, dst)[:NE]:
-            m |= 1 << e
-        g.remote_dma(out, in_, T.sem[s], T.sem["loc"], pid, rid, m)
-        tot["loc"] = tot.get("loc", 0) + NE
+    def send(dst, out, in_, r, s, k):
+        def issue():
+            wait("G", deps("G", r, []))
+            rid, pid = topo.addr(dst)[:2]
+            m = 0
+            for e in topo.engines(core, dst)[:NE]:
+                m |= 1 << e
+            g.remote_dma(out, in_, T.sem[s], T.sem["loc"], pid, rid, m)
+            tot["loc"] = tot.get("loc", 0) + NE
+        calls.append(("G", 300, r, ["sent" + s]))
+        acts.append(issue)
+        arrives(k, s, NE, (FLIGHT if k[:2] == "le" else LATE) - 2 * HOP, ["sent" + s])
 
-    def landed(k, s):
-        tot[s] = NE
-        wr[k] = [("R", (s, NE, {s: NE}))]
-
-    def ts(out, in0, s1, s2, o0, o1, r, w):
+    def ts(out, in0, s1, s2, o0, o1, r, w, c=128):
         if o1 is None:
-            op("V", lambda: v.tensor_scalar(out, in0, s1, None, o0), r, w)
+            op("V", lambda: v.tensor_scalar(out, in0, s1, None, o0), r, w, c)
         else:
-            op("V", lambda: v.tensor_scalar(out, in0, s1, s2, o0, o1), r, w)
+            op("V", lambda: v.tensor_scalar(out, in0, s1, s2, o0, o1), r, w, c)
 
-    def tt(out, i0, i1, o, r, w):
-        op("V", lambda: v.tensor_tensor(out, i0, i1, o), r, w)
+    def tt(out, i0, i1, o, r, w, c=128):
+        op("V", lambda: v.tensor_tensor(out, i0, i1, o), r, w, c)
 
-    def vc(out, in_, r, w):
-        op("V", lambda: v.tensor_copy(out, in_), r, w)
+    def vc(out, in_, r, w, c=128):
+        op("V", lambda: v.tensor_copy(out, in_), r, w, c)
 
-    def act(out, in_, f, r, w, bias=0.0, scale=1.0):
-        op("A", lambda: a.activation(out, in_, f, bias=bias, scale=scale), r, w)
+    def act(out, in_, f, r, w, bias=0.0, scale=1.0, c=128, acc=None):
+        op("A", lambda: a.activation(out, in_, f, bias=bias, scale=scale, accum_out=acc), r, w, c + 64)
 
-    def mm(out, l, rh, st, sp, r, w):
-        op("P", lambda: pe.matmul(out, l, rh, st, sp), r, w)
+    def mm(out, l, rh, st, sp, r, w, c=64):
+        op("P", lambda: pe.matmul(out, l, rh, st, sp), r, w, c)
 
-    def ms(ap, c, w, r=()):
-        op("V", lambda: v.memset(ap, c), list(r), w)
+    def ms(ap, x, w, r=(), c=64):
+        op("V", lambda: v.memset(ap, x), list(r), w, c)
 
-    def iota(out, pattern, base, w):
-        op("G", lambda: g.iota(out, pattern, base, 0, allow_small_or_imprecise_dtypes=True), [], w)
+    def iota(out, pattern, base, cm, w, n, whole=False):
+        if whole:
+            op("G", lambda: g.iota(out, pattern, base, cm), [], w, 160 + 2 * n)
+        else:
+            op("G", lambda: g.iota(out, pattern, base, cm, allow_small_or_imprecise_dtypes=True), [], w, 160 + 2 * n)
+
+    def pick(out, in_, pattern, o, base, cm, r, w):
+        op("G", lambda: g.affine_select(out, in_, pattern, o, 0.0, base, cm), r, w, 460)
+
+    def scan(out, mask, in_, r, w, c):
+        op("V", lambda: v.tensor_tensor_scan(out, mask, in_, 0.0, A.mult, A.max), r, w, c)
+
+    def least(out, in_, r, w, c):
+        op("V", lambda: v.tensor_reduce(out, in_, AxisListType.X, A.min, apply_absolute_value=True), r, w, c)
 
     def col(i):
         return T.pcol[:, i:i + 1]
 
-    dma("S", T.ents[:, 0:1024], T.ent[:, 0:1024], [], [], "dent")
-    dma("A", T.ents[:, 1024:2048], T.ent[:, 1024:2048], [], [], "dent")
-    joined("ents", "dent")
+    def gc(n):
+        return int(60 + GATHER * n)
+
     dma("S", T.wti[:, 0:1], T.wt[:, 0:1], [], [], "dsm")
     dma("A", T.kpi[:, 0:1], T.kap[:, 0:1], [], [], "dsm")
-    joined("wti", "dsm")
-    joined("kpi", "dsm")
+    dma("S", T.ents[:, 0:1024], T.ent[:, 0:1024], [], [], "dent")
+    dma("A", T.ents[:, 1024:2048], T.ent[:, 1024:2048], [], [], "dent")
     dma("S", T.fw[:, 0:2048], T.feat[:, 0:2048], [], [], "dfe")
     dma("A", T.fw[:, 2048:4096], T.feat[:, 2048:4096], [], [], "dfe")
-    joined("fw", "dfe")
+    for k, s in (("wti", "dsm"), ("kpi", "dsm"), ("ents", "dent"), ("fw", "dfe")):
+        arrives(k, s, 32, LOADED[k], [])
 
+    S = 64
     ms(T.ones[:], 1.0, ["ones"])
-    op("G", lambda: g.iota(T.pi[:, 0:1], [[1, 1]], 0, 1), [], ["pi"])
-    op("G", lambda: g.iota(T.sti[:], [[37, 64]], 0, 0), [], ["sti"])
-    iota(T.ramp[:], [[1, 240]], -112, ["ramp"])
-    op("G", lambda: g.affine_select(T.bd0[:], T.ones[:], [[-16, 8], [0, 16]], A.is_ge, 0.0, 0, 1), ["ones"], ["bd0"])
-    op("G", lambda: g.affine_select(T.bd[:], T.bd0[:], [[16, 8], [0, 16]], A.is_ge, 0.0, 15, -1), ["bd0"], ["bd"])
-    iota(T.r4[:], [[0, 32], [1, 4]], 0, ["r4"])
-    iota(T.r16[:], [[0, 8], [1, 16]], 0, ["r16"])
+    iota(T.pi[:, 0:1], [[1, 1]], 0, 1, ["pi"], 1, True)
+    iota(T.sti[:], [[37, 64]], 0, 0, ["sti"], 64, True)
+    iota(T.ramp[:], [[1, 240]], -112, 0, ["ramp"], 240)
+    pick(T.bd0[:], T.ones[:], [[-16, 8], [0, 16]], A.is_ge, 0, 1, ["ones"], ["bd0"])
+    pick(T.bd[:], T.bd0[:], [[16, 8], [0, 16]], A.is_ge, 15, -1, ["bd0"], ["bd"])
+    iota(T.r4[:], [[0, 32], [1, 4]], 0, 0, ["r4"], 128)
+    iota(T.r16[:], [[0, 8], [1, 16]], 0, 0, ["r16"], 128)
     R = T.ramp[:, 112:240]
-    ms(T.fm[:], 1.0, ["fm0"])
-    ms(T.fm[:, 0:2048:16], 0.0, ["fm"], ["fm0"])
+    for i in range(4):
+        ms(T.fm[:, 512 * i:512 * i + 512], 1.0, ["fm%d" % i], c=256)
+    ms(T.fm[:, 0:2048:16], 0.0, ["fm"], ["fm%d" % i for i in range(4)])
     ms(T.fw[:, 4096:4112], 0.0, ["fwz"])
     ms(T.uc[0:64, :], -32.0, ["uc0"])
     ms(T.uc[64:128, :], 1.0 / 128, ["uc"])
     ms(T.c2k[:], 2048.0, ["c2k"])
-    ms(T.onef[:], -1.0, ["onef"])
+    ms(T.half[:], 0.5, ["half"], c=128)
     ms(T.sa[:], 0.0, ["sa"])
-    ts(T.pj[:, 0:1], T.pi[:, 0:1], 15, None, A.bitwise_and, None, ["pi"], ["pj0"])
-    ts(T.pj[:, 1:2], T.pi[:, 0:1], 2, 3, A.arith_shift_right, A.bitwise_and, ["pi"], ["pj1"])
-    ts(T.pj[:, 2:3], T.pi[:, 0:1], 3, None, A.bitwise_and, None, ["pi"], ["pj2"])
-    ts(T.pj[:, 3:4], T.pi[:, 0:1], 4, None, A.arith_shift_right, None, ["pi"], ["pj3"])
-    ts(T.stj[:], T.sti[:], 63, None, A.bitwise_and, None, ["sti"], ["stj"])
-    vc(T.pcol[:, 0:4], T.pj[:, 0:4], ["pj0", "pj1", "pj2", "pj3"], ["pc"])
-    vc(col(4), T.pi[:, 0:1], ["pi"], ["pc4"])
-    ts(T.st[:, 0:64], T.stj[:], 4096.0, -2065.0 - OFF, A.mult, A.add, ["stj"], ["st"])
+    ts(T.pj[:, 0:1], T.pi[:, 0:1], 15, None, A.bitwise_and, None, ["pi"], ["pj0"], S)
+    ts(T.pj[:, 1:2], T.pi[:, 0:1], 2, 3, A.arith_shift_right, A.bitwise_and, ["pi"], ["pj1"], S)
+    ts(T.pj[:, 2:3], T.pi[:, 0:1], 3, None, A.bitwise_and, None, ["pi"], ["pj2"], S)
+    ts(T.pj[:, 3:4], T.pi[:, 0:1], 4, None, A.arith_shift_right, None, ["pi"], ["pj3"], S)
+    ts(T.stj[:], T.sti[:], 63, None, A.bitwise_and, None, ["sti"], ["stj"], S)
+    vc(T.pcol[:, 0:4], T.pj[:, 0:4], ["pj0", "pj1", "pj2", "pj3"], ["pc"], S)
+    vc(col(4), T.pi[:, 0:1], ["pi"], ["pc4"], S)
+    ts(T.st[:, 0:64], T.stj[:], 4096.0, -2065.0 - OFF, A.mult, A.add, ["stj"], ["st"], S)
     n = 64
     while n < 2048:
-        act(T.st[:, n:2 * n], T.st[:, 0:n], F.Copy, ["st"], ["st"])
-        n *= 2
-    ts(col(5), col(3), 4.0, col(2), A.mult, A.add, ["pc"], ["pc5"])
-    ts(col(8), col(0), 1024.5, None, A.add, None, ["pc"], ["pc8"])
-    ts(col(9), col(0), 16.0, -1023.5, A.mult, A.add, ["pc"], ["pc9"])
-    ts(T.zg[:], T.ramp[:, 112:120], col(3), None, A.is_equal, None, ["ramp", "pc"], ["zg"])
-    ts(T.mx[:], T.ramp[:, 112:116], col(1), None, A.is_equal, None, ["ramp", "pc"], ["mx"])
-    ts(T.cl[:], T.ramp[:, 112:144], 4.0, col(1), A.mult, A.add, ["ramp", "pc"], ["cl"])
-    vc(T.c8[:], T.ramp[:, 112:120], ["ramp"], ["c8"])
-    ts(T.sel[:], T.ramp[:, 112:144], col(5), None, A.is_equal, None, ["ramp", "pc5"], ["sel"])
-    ts(T.idb[:], R, col(4), None, A.is_equal, None, ["ramp", "pc4"], ["idb"])
-    ts(T.dmc[:], T.ramp[:, 112:120], 16.0, col(8), A.mult, A.add, ["ramp", "pc8"], ["dmc"])
-    ts(T.ls[:, 0:8], T.ramp[:, 112:120], 256.0, col(9), A.mult, A.add, ["ramp", "pc9"], ["ls0"])
-    ts(T.zp[:], T.zg[:], 32768.0, None, A.mult, None, ["zg"], ["zp"])
-    ts(T.zn[:], T.zg[:], -32768.0, None, A.mult, None, ["zg"], ["zn"])
-    ts(T.zh[:], T.zg[:], 16384.0, None, A.mult, None, ["zg"], ["zh"])
-    vc(T.cb[:], T.zg[:], ["zg"], ["cb"])
-    for t in range(1, RO):
-        ts(T.ls[:, 8 * t:8 * t + 8], T.ls[:, 0:8], float(t), None, A.add, None, ["ls0"], ["ls%d" % t])
-    vc(col(6), T.wti[:, 0:1], ["wti"], ["wcol"])
-    vc(col(7), T.kpi[:, 0:1], ["kpi"], ["kcol"])
-    ts(T.ka0[:], T.r4[:], col(1), None, A.is_equal, None, ["r4", "pc"], ["ka0"])
-    ts(T.wblk[:], T.bd[:], col(6), None, A.mult, None, ["bd", "wcol"], ["wblk"])
+        m = min(n, 512)
+        act(T.st[:, n:n + m], T.st[:, 0:m], F.Copy, ["st"], ["st"], c=m)
+        n += m
+    ts(col(5), col(3), 4.0, col(2), A.mult, A.add, ["pc"], ["pc5"], S)
+    ts(col(8), col(0), 0.5, None, A.add, None, ["pc"], ["pc8"], S)
+    ts(col(9), col(0), 16.0, float(SP), A.mult, A.add, ["pc"], ["pc9"], S)
+    ts(col(10), col(0), -8192.0, 4096.0, A.mult, A.add, ["pc"], ["pc10"], S)
+    ts(T.zg[:], T.ramp[:, 112:120], col(3), None, A.is_equal, None, ["ramp", "pc"], ["zg"], S)
+    ts(T.mx[:], T.ramp[:, 112:116], col(1), None, A.is_equal, None, ["ramp", "pc"], ["mx"], S)
+    ts(T.cl[:], T.ramp[:, 112:144], 4.0, col(1), A.mult, A.add, ["ramp", "pc"], ["cl"], S)
+    vc(T.c8[:], T.ramp[:, 112:120], ["ramp"], ["c8"], S)
+    ts(T.sel[:], T.ramp[:, 112:144], col(5), None, A.is_equal, None, ["ramp", "pc5"], ["sel"], S)
+    ts(T.idb[:], R, col(4), None, A.is_equal, None, ["ramp", "pc4"], ["idb"], S)
+    ts(T.spc[:], T.ramp[:, 112:120], 16.0, col(8), A.mult, A.add, ["ramp", "pc8"], ["spc"], S)
+    ts(T.ls[:], T.ramp[:, 112:120], 256.0, col(9), A.mult, A.add, ["ramp", "pc9"], ["ls"], S)
+    tt(T.am[:], T.ls[:], T.spc[:], A.subtract, ["ls", "spc"], ["am"], S)
+    tt(T.y2[:], T.ls[:], T.spc[:], A.add, ["ls", "spc"], ["y2"], S)
+    for t in range(RO):
+        ts(T.hd[:, 8 * t:8 * t + 8], T.am[:], t + 0.5, 0.5, A.add, A.mult, ["am"], ["hd%d" % t], S)
+        ts(T.md[:, 8 * t:8 * t + 8], T.y2[:], t - 0.5, 0.5, A.add, A.mult, ["y2"], ["md%d" % t], S)
+    ts(T.zp[:], T.zg[:], 32768.0, None, A.mult, None, ["zg"], ["zp"], S)
+    ts(T.zn[:], T.zg[:], -32768.0, None, A.mult, None, ["zg"], ["zn"], S)
+    ts(T.zh[:], T.zg[:], 16384.0, None, A.mult, None, ["zg"], ["zh"], S)
+    vc(T.cb[:], T.zg[:], ["zg"], ["cb"], S)
+    vc(col(6), T.wti[:, 0:1], ["wti"], ["wcol"], S)
+    vc(col(7), T.kpi[:, 0:1], ["kpi"], ["kcol"], S)
+    ts(T.ka0[:], T.r4[:], col(1), None, A.is_equal, None, ["r4", "pc"], ["ka0"], S)
+    ts(T.wblk[:], T.bd[:], col(6), None, A.mult, None, ["bd", "wcol"], ["wblk"], S)
     for x in range(4):
-        op("G", lambda: g.affine_select(T.w4[:, 128 * x:128 * x + 128], T.wblk[:], [[0, 8], [1, 4], [0, 4]], A.is_equal, 0.0, -x, 0),
-           ["wblk"], ["w4%d" % x])
-    ts(T.kr[:], T.ramp[:, 112:116], col(2), col(7), A.is_equal, A.mult, ["ramp", "pc", "kcol"], ["kr"])
-    tt(T.ka[:], T.ka0[:], T.bd[:], A.mult, ["ka0", "bd"], ["ka"])
-    mm(T.psL[:, 16:20], T.ka[:], T.kr[:], True, True, ["ka", "kr"], ["psL:k"])
+        pick(T.w4[:, 128 * x:128 * x + 128], T.wblk[:], [[0, 8], [1, 4], [0, 4]], A.is_equal, -x, 0, ["wblk"], ["w4%d" % x])
+    ts(T.kr[:], T.ramp[:, 112:116], col(2), col(7), A.is_equal, A.mult, ["ramp", "pc", "kcol"], ["kr"], S)
+    tt(T.ka[:], T.ka0[:], T.bd[:], A.mult, ["ka0", "bd"], ["ka"], 256)
+    mm(T.psL[:, 16:20], T.ka[:], T.kr[:], True, True, ["ka", "kr"], ["psL:1"])
     ts(T.pmk[:], T.r16[:], col(0), None, A.is_equal, None, ["r16", "pc"], ["pmk"])
-    ts(T.cm[:], T.r16[:], -16.0, 240.0, A.mult, A.add, ["r16"], ["cm"])
-    vc(T.kb[:], T.psL[:, 16:20], ["psL:k"], ["kb"])
-    ts(T.k16[:], T.psL[:, 16:20], 16.0, 2047.5, A.mult, A.add, ["psL:k"], ["k16"])
-    tt(T.kq[:], T.kb[:], T.psL[:, 16:20], A.mult, ["kb", "psL:k"], ["kq"])
-    ts(T.k8[:], T.kq[:], -8.0, -0.375, A.mult, A.add, ["kq"], ["k8"])
+    ts(T.cm[:], T.r16[:], -16.0, 240.0, A.mult, A.add, ["r16"], ["cm"], S)
+    vc(T.kb[:], T.psL[:, 16:20], ["psL:1"], ["kb"], S)
+    ts(T.k16[:], T.psL[:, 16:20], 16.0, 2047.5, A.mult, A.add, ["psL:1"], ["k16"], S)
+    tt(T.kq[:], T.kb[:], T.psL[:, 16:20], A.mult, ["kb", "psL:1"], ["kq"], S)
+    ts(T.k8[:], T.kq[:], -8.0, -0.375, A.mult, A.add, ["kq"], ["k8"], S)
+    ms(T.ri[:], 0.0, ["ri0"], c=292)
+    ms(T.mk[:], 1024.0 + SP, ["mk0"], c=292)
+    ms(T.rx[:, 0:128], -8192.0, ["rx0"])
+    ms(T.rx[:, 128:136], 1.0, ["rx"])
+    ts(T.ramp2[:], T.ramp[:, 0:128], 8192.0, None, A.mult, None, ["ramp"], ["ramp2"], S)
+    for c in range(8):
+        s, w = SEG[c], 16 * c + 16
+        ts(T.ri[:, s:s + w], T.ramp[:, 112:112 + w], col(4), 8192.0, A.is_equal, A.mult, ["ramp", "pc4", "ri0"], ["ri%d" % c], S)
+        ts(T.rn[:, s:s + w + 1], T.rx[:, 128 - w:129], T.zg[:, c:c + 1], None, A.mult, None, ["rx0", "rx", "zg"], ["rn%d" % c], S)
+        ts(T.mk[:, s:s + w], T.ramp2[:, 128 - w:128], col(10), T.spc[:, c:c + 1], A.add, A.max,
+           ["ramp2", "pc10", "spc", "mk0"], ["mk%d" % c], S)
 
-    def pair_constants():
-        for c in range(8):
-            s, w = slice(SEG[c], SEG[c + 1]), 16 * c + 16
-            ts(T.ri[:, s], T.ramp[:, 112:112 + w], col(4), 4096.0, A.is_equal, A.mult, ["ramp", "pc4"], ["ri"])
-            ts(T.rn[:, s], T.ones[:, 0:w], T.zg[:, c:c + 1], -4096.0, A.mult, A.mult, ["ones", "zg"], ["rn"])
-            ts(T.mk[:, s], T.ramp[:, 112 - 16 * c:128], col(0), 2.0 ** 24, A.is_ge, A.mult, ["ramp", "pc"], ["mk"])
-
-    banks = ["psK", "psD0", "psD1", "psW"]
+    PA, PV, PW = T.psA, T.psV, T.psW
+    P0, P1, P2, P3 = [slice(128 * i, 128 * i + 128) for i in range(4)]
+    TAB = T.tab[:, SP:W]
     CZ = -(MB + OFF - 2048.0)
 
     def first_lanes():
         e = T.ents[:, 0:2048:16]
-        ts(T.e1[:], e, -1024.5, MB, A.add, A.add, ["ents"], ["e1"])
-        ts(T.psV[:, 0:128], T.e1[:], CZ, None, A.add, None, ["e1"], ["psV:0"])
-        tt(T.so[:, 0:128], e, T.psV[:, 0:128], A.add, ["ents", "psV:0"], ["so0"])
+        ts(T.c1[:], e, -1024.5, MB, A.add, A.add, ["ents"], ["c1"])
+        ts(PV[:, P0], T.c1[:], CZ, None, A.add, None, ["c1"], ["psV:0"])
+        tt(T.so[:, 0:128], e, PV[:, P0], A.add, ["ents", "psV:0"], ["so0"])
 
     def first_table():
-        for i in range(4):
-            s = slice(512 * i, 512 * i + 512)
-            ts(T.cf[:, s], T.ents[:, s], -1024.5, MB, A.add, A.add, ["ents"], ["cf%d" % i])
-            act(T[banks[i]][:], T.cf[:, s], F.Identity, ["cf%d" % i], [banks[i]], bias=CZ)
-        for i in range(4):
-            s = slice(512 * i, 512 * i + 512)
-            tt(T.tab[:, s], T.ents[:, s], T[banks[i]][:], A.add, [banks[i], "ents"], ["tab"])
+        for i in range(8):
+            s, k = slice(256 * i, 256 * i + 256), ("psK", "psD0", "psD1", "psW")[i // 2]
+            p, pk = T[k][:, 256 * (i % 2):256 * (i % 2) + 256], ["%s:%d" % (k, 2 * (i % 2) + j) for j in range(2)]
+            ts(T.cf[:, s], T.ents[:, s], -1024.5, MB, A.add, A.add, ["ents"], ["cf%d" % i], 256)
+            act(p, T.cf[:, s], F.Identity, ["cf%d" % i], pk, bias=CZ, c=256)
+            tt(T.tab[:, SP + 256 * i:SP + 256 * i + 256], T.ents[:, s], p, A.add, pk + ["ents"], ["tab%d" % i], 256)
+        ms(T.tab[:, 0:16], 0.0, ["tab"], ["tab%d" % i for i in range(8)])
 
     def lane_list(t, dst):
         o = 128 * t
-        src, sk = (T.so[:, 0:128], "so0") if t == 0 else (T.tab[:, t:2048:16], "tab")
-        act(T.psA[:, 0:128], src, F.Identity, [sk], ["psA:0"], bias=-2048.75 / 16, scale=2.0 ** -16)
+        src, sk = (T.so[:, 0:128], "so0") if t == 0 else (T.tab[:, SP + t:W:16], "tab")
+        act(PA[:, P0], src, F.Identity, [sk], ["psA:0"], bias=-2048.75 / 16, scale=2.0 ** -16)
         if t:
             act(T.so[:, o:o + 128], src, F.Copy, [sk], ["so%d" % t])
-        send(dst, T.lo[:, o:o + 128], T.so[:, o:o + 128], ["so%d" % t], "ro%d" % t)
+        send(dst, T.lo[:, o:o + 128], T.so[:, o:o + 128], ["so%d" % t], "ro%d" % t, "lo%d" % t)
         ts(T.i1[:], src, -2033.0, None, A.add, None, [sk], ["i1"])
         ts(T.i3[:], T.i1[:], 16, None, A.bitwise_and, None, ["i1"], ["i3"])
-        tt(T.ly[:], T.i3[:], T.psA[:, 0:128], A.mult, ["i3", "psA:0"], ["ly"])
+        tt(T.ly[:], T.i3[:], PA[:, P0], A.mult, ["i3", "psA:0"], ["ly"])
         ts(T.lst[:], T.ly[:], M0 + 4096.0, -M0, A.add, A.add, ["ly"], ["lst"])
 
-    def gather_scalar(n0, n1, k):
-        op("A", lambda: a.activation(T.fg[:, 16 * n0:16 * n1], T.fw[:].indirect(T.lst[:, n0:n1]), F.Copy), ["lst", "fw", "fwz"], ["fg" + k])
+    def features(cuts):
+        for i in range(len(cuts) - 1):
+            n0, n1 = cuts[i:i + 2]
+            c = slice(16 * n0, 16 * n1)
+            r = ["lst", "fw", "fwz"]
+            if i:
+                act(T.fg[:, c], T.fw[:].indirect(T.lst[:, n0:n1]), F.Copy, r, ["fg%d" % i], c=gc(16 * (n1 - n0)) - 64)
+            else:
+                vc(T.fg[:, c], T.fw[:].indirect(T.lst[:, n0:n1]), r, ["fg%d" % i], gc(16 * (n1 - n0)))
+            scan(T.fs[:, c], T.fm[:, c], T.fg[:, c], ["fm", "fg%d" % i], ["fs%d" % i], 8 * (n1 - n0))
+        return ["fs%d" % i for i in range(len(cuts) - 1)]
 
-    def gather_vector(n0, n1, k):
-        op("V", lambda: v.tensor_copy(T.fg[:, 16 * n0:16 * n1], T.fw[:].indirect(T.lst[:, n0:n1])), ["lst", "fw", "fwz"], ["fg" + k])
-
-    def scan(n0, n1, k):
-        c = slice(16 * n0, 16 * n1)
-        op("V", lambda: v.tensor_tensor_scan(T.fs[:, c], T.fm[:, c], T.fg[:, c], 0.0, A.mult, A.max), ["fm", "fg" + k], ["fs" + k])
-
-    def cand(t, dst, ks):
+    def cand(t, dst, fs):
         o = 128 * t
         U = T.psU[:, 0:32]
+        mm(U, T.ones[:], T.uc[:], True, False, ["ones", "uc0", "uc"], ["psU"])
         for x in range(4):
-            mm(U, T.w4[:, 128 * x:128 * x + 128], T.fs[:, 16 * x + 15:2048:64], False, x == 3, ["w4%d" % x] + ["fs" + k for k in ks], ["psU"])
+            mm(U, T.w4[:, 128 * x:128 * x + 128], T.fs[:, 16 * x + 15:2048:64], False, x == 3, ["w4%d" % x] + fs, ["psU"])
         kc, kk = T.k8, "k8"
         if t:
-            kc, kk = T.kc[:, 4 * t:4 * t + 4], "kc"
-            ts(kc, T.k8[:], T.la[:, 12 * t - 4:12 * t - 3], None, A.add, None, ["k8", "la%d" % (t - 1)], ["kc"])
-        ts(T.ur[:], U, MN, -MN, A.add, A.add, ["psU"], ["ur"])
-        tt(T.uu[:], U, T.ur[:], A.subtract, ["psU", "ur"], ["uu"])
+            kc, kk = T.kc, "kc"
+            n, nk = T.la[:, 12 * t - 4:12 * t - 3], "la%d" % (t - 1)
+            ts(T.aa[:, 1:2], n, -15.5, M32, A.add, A.add, [nk], ["aa1"], S)
+            ts(T.aa[:, 2:3], T.aa[:, 1:2], -M32, -1.0, A.add, A.mult, ["aa1"], ["aa2"], S)
+            ts(kc[:], T.k8[:], n, T.aa[:, 2:3], A.add, A.add, ["k8", nk, "aa2"], ["kc"], S)
+        ts(T.ur[:], U, MN, -MN, A.add, A.add, ["psU"], ["ur"], S)
+        tt(T.uu[:], U, T.ur[:], A.subtract, ["psU", "ur"], ["uu"], S)
         for b in range(4):
             s = slice(32 * b, 32 * b + 32)
-            act(T.vq[:, s], T.uu[:], F.Square, ["uu", "k16"], ["vq%d" % b], bias=T.k16[:, b:b + 1])
-            c = 4 * t + b if t else b
-            ts(T.u5[:, s], T.vq[:, s], 0.03125, (T.kc if t else T.k8)[:, c:c + 1], A.mult, A.add, ["vq%d" % b, kk], ["u5%d" % b])
+            act(T.vq[:, s], T.uu[:], F.Square, ["uu", "k16"], ["vq%d" % b], bias=T.k16[:, b:b + 1], c=S)
+            ts(T.u5[:, s], T.vq[:, s], 0.03125, kc[:, b:b + 1], A.mult, A.add, ["vq%d" % b, kk], ["u5%d" % b], S)
         ts(T.u6[:], T.u5[:], 2047, None, A.bitwise_and, None, ["u5%d" % b for b in range(4)], ["u6"])
         vc(T.se[:, o:o + 128], T.u6[:], ["u6"], ["se%d" % t])
-        send(dst, T.le[:, o:o + 128], T.se[:, o:o + 128], ["se%d" % t], "re%d" % t)
+        send(dst, T.le[:, o:o + 128], T.se[:, o:o + 128], ["se%d" % t], "re%d" % t, "le%d" % t)
 
     def scatter(tab, lists, vals, r, off):
-        op("V", lambda: v.tensor_scalar(T[tab][:].indirect(lists), vals, 1.0, off, A.mult, A.add), r, [tab])
-
-    PA, PV, PW = T.psA, T.psV, T.psW
+        ts(T[tab][:].indirect(lists), vals, 1.0, off, A.mult, A.add, r, [tab], int(60 + SCATTER * 128))
 
     def expand(t):
         av, lk = T.lo[:, 128 * t:128 * t + 128], "lo%d" % t
         act(T.c1[:], av, F.Identity, [lk], ["c1"], bias=-8.5)
-        act(PA[:, 0:128], av, F.Identity, [lk], ["psA:0"], bias=OFF)
+        act(PA[:, P0], av, F.Identity, [lk], ["psA:0"], bias=OFF)
         act(T.c2[:], T.c1[:], F.Identity, ["c1"], ["c2"], bias=M16 + 16.0)
         act(T.c3[:], T.c2[:], F.Identity, ["c2"], ["c3"], bias=-M16 - 16.0)
-        act(T.ox[:], T.c3[:].indirect(T.cl[:]), F.Identity, ["c3", "cl"], ["ox"], bias=8.5)
+        act(T.ox[:], T.c3[:].indirect(T.cl[:]), F.Identity, ["c3", "cl"], ["ox"], bias=8.5, c=gc(512) - 64)
 
     def own_side(t):
-        th = 8.0 + t
-        tt(T.ah[:], T.st[:, t:2048:16], PA[:, 0:128], A.add, ["psA:0", "st"], ["ah"])
+        tt(T.ah[:], T.st[:, t:2048:16], PA[:, P0], A.add, ["psA:0", "st"], ["ah"])
         ts(T.al[:], T.ah[:], 31, None, A.bitwise_and, None, ["ah"], ["al"])
         ts(T.ak[:], T.ah[:], 15, 7, A.arith_shift_right, A.bitwise_and, ["ah"], ["ak"])
-        ts(PV[:, 0:128], T.al[:], th, 64.0, A.is_ge, A.mult, ["al"], ["psV:0"])
-        tt(T.av[:], T.ak[:], PV[:, 0:128], A.is_le, ["ak", "psV:0"], ["av"])
-        tt(T.as2[:], T.al[:], PV[:, 0:128], A.add, ["al", "psV:0"], ["as2"])
-        tt(T.ap[:], T.av[:], PA[:, 0:128], A.mult, ["av", "psA:0"], ["ap"])
-
-    def own_side_scalar(t):
+        ts(PV[:, P0], T.al[:], 8.0 + t, 64.0, A.is_ge, A.mult, ["al"], ["psV:0"])
+        tt(T.av[:], T.ak[:], PV[:, P0], A.is_le, ["ak", "psV:0"], ["av"])
+        tt(T.as2[:], T.al[:], PV[:, P0], A.add, ["al", "psV:0"], ["as2"])
+        tt(T.ap[:], T.av[:], PA[:, P0], A.mult, ["av", "psA:0"], ["ap"])
         act(T.ac[:], T.ap[:], F.Identity, ["ap"], ["ac"], bias=MN)
-        act(PA[:, 128:256], T.as2[:], F.Relu, ["as2"], ["psA:1"], bias=12.0 + t, scale=-1.0)
-        act(PA[:, 256:384], T.as2[:], F.Relu, ["as2"], ["psA:2"], bias=-1264.0, scale=16.0)
-        act(PA[:, 384:512], T.ac[:], F.Identity, ["ac"], ["psA:3"], bias=-MN)
+        act(T.ar[:], T.as2[:], F.Relu, ["as2"], ["ar"], bias=80 * 2.0 ** 25, scale=-2.0 ** 25)
+        act(PA[:, P1], T.as2[:], F.Relu, ["as2"], ["psA:1"], bias=12.0 + t, scale=-1.0)
+        act(PA[:, P3], T.ac[:], F.Identity, ["ac"], ["psA:3"], bias=-MN)
+        act(PA[:, P2], T.ar[:], F.Identity, ["ar"], ["psA:2"], bias=12.0 + t, scale=-1.0)
+
+    KEYS = ["psK:%s%d%d" % (k, i, x) for k in ("mt", "db") for i in range(4) for x in range(4)] + ["psK:e%d" % i for i in range(4)]
 
     def score(t):
         o = 128 * t
         K = T.psK
         lk = "le%d" % t
-        mm(K[:, 0:128], T.ones[:], T.cm[:], True, False, ["ones", "cm"], ["psK"])
-        for i in range(HA, 4):
-            mm(K[:, i:128:4], T.ones[:], T.c2k[:], False, False, ["ones", "c2k"], ["psK"])
+        left = [len(KEYS)]
 
-        def sums(i, tile, k, z, last=False):
+        def add(out, l, rh, r, k):
+            def fn():
+                left[0] -= 1
+                return pe.matmul(out, l, rh, False, left[0] == 0)
+            op("P", fn, r, [k], 64)
+
+        mm(K[:, P0], T.ones[:], T.cm[:], True, False, ["ones", "cm"], ["psK"], 128)
+        for i in range(HA, 4):
+            mm(K[:, i:128:4], T.ones[:], T.c2k[:], False, False, ["ones", "c2k"], ["psK"] + KEYS)
+
+        def sums(i, tile, k, z):
             for x in range(4):
-                mm(K[:, 4 * x + i:128:16], tile[:, 512 * i + x:512 * i + 512:4], T[z][:], False, last and x == 3, [k, z], ["psK"])
+                add(K[:, 4 * x + i:128:16], tile[:, 512 * i + x:512 * i + 512:4], T[z][:], [k, z], "psK:%s%d" % (k, x))
 
         for i in range(4):
             c = slice(512 * i, 512 * i + 512)
-            tt(T.dd[:, c], T.tab[:, 0:2048].indirect(T.le[:, o + 32 * i:o + 32 * i + 32]), T.ox[:], A.subtract, ["tab", lk, "ox"], ["dd%d" % i])
+            tt(T.dd[:, c], TAB.indirect(T.le[:, o + 32 * i:o + 32 * i + 32]), T.ox[:], A.subtract,
+               ["tab", lk, "ox", "~dd%d" % (i - 1), "~mt%d" % (i - 2)] + ["~eh%d" % x for x in range(4) if i == 2], ["dd%d" % i], gc(512))
+            for x in range(4 if i == 0 else 0):
+                ts(T.eh[:, x:512:4], T.le[:, o:o + 128], -1023.5, T.mx[:, x:x + 1], A.add, A.mult, [lk, "mx", "~dd0"], ["eh%d" % x], S)
             if i < HA:
-                act(T.da[:, c], T.dd[:, c], F.Abs, ["dd%d" % i], ["da%d" % i])
-                act(T.db[:, c], T.da[:, c], F.Sign, ["da%d" % i], ["db%d" % i], bias=-8.25)
-            if i == 0:
-                for x in range(4):
-                    ts(T.eh[:, x:512:4], T.le[:, o:o + 128], -1023.5, T.mx[:, x:x + 1], A.add, A.mult, [lk, "mx"], ["eh%d" % x])
-                for b in range(4):
-                    mm(K[:, b:128:4], T.eh[:, 128 * b:128 * b + 128], T.sel[:], False, False, ["sel"] + ["eh%d" % x for x in range(4)], ["psK"])
-            ts(T.mt[:, c], T.dd[:, c], MN + 4096.0, MN + 4096.0, A.add, A.is_equal, ["dd%d" % i], ["mt%d" % i])
-            if i and i - 1 < HA:
-                sums(i - 1, T.db, "db%d" % (i - 1), "zh")
+                act(T.da[:, c], T.dd[:, c], F.Abs, ["dd%d" % i], ["da%d" % i], c=512)
+                act(T.db[:, c], T.da[:, c], F.Sign, ["da%d" % i], ["db%d" % i], bias=-8.25, c=512)
+            else:
+                ts(T.db[:, c], T.dd[:, c], M16, M16, A.add, A.is_equal, ["dd%d" % i], ["db%d" % i], 256)
+            ts(T.mt[:, c], T.dd[:, c], MN + 4096.0, MN + 4096.0, A.add, A.is_equal, ["dd%d" % i], ["mt%d" % i], 256)
             sums(i, T.mt, "mt%d" % i, "zp")
-            if i >= HA:
-                ts(T.db[:, c], T.dd[:, c], M16, M16, A.add, A.is_equal, ["dd%d" % i], ["db%d" % i])
-                sums(i, T.db, "db%d" % i, "zn", i == 3)
-        if HA == 4:
-            sums(3, T.db, "db3", "zh", True)
+            sums(i, T.db, "db%d" % i, "zh" if i < HA else "zn")
+            add(K[:, i:128:4], T.eh[:, 128 * i:128 * i + 128], T.sel[:], ["sel"] + ["eh%d" % x for x in range(4)], "psK:e%d" % i)
 
-    DB = [("psD0", slice(0, SEG[SPLIT])), ("psD1", slice(SEG[SPLIT], SEG[8]))]
+    DB = [("psD0", 0, SPLIT), ("psD1", SPLIT, 8)]
 
     def partner(t):
-        for k, s in DB:
-            mm(T[k][:, 0:s.stop - s.start], T.idb[:], T.mk[:, s], True, False, ["idb", "mk"], [k])
-        op("V", lambda: v.tensor_tensor_scan(T.ks[:], T.fm[:, 0:128], T.psK[:, 0:128], 0.0, A.mult, A.max), ["fm", "psK"], ["ks"])
-        ts(PV[:, 128:136], T.ks[:, 15:128:16], MB, -MB, A.add, A.add, ["ks"], ["psV:1"])
-        tt(T.p8[:], T.ks[:, 15:128:16], PV[:, 128:136], A.subtract, ["ks", "psV:1"], ["p8"])
-        tt(T.pm[:], T.p8[:].indirect(T.c8[:]), T.pmk[:], A.mult, ["p8", "c8", "pmk"], ["pm"])
-        mm(T.psL[:, 0:8], T.pm[:], T.cb[:], True, True, ["pm", "cb"], ["psL"])
-        vc(T.pe[:], T.p8[:].indirect(T.c8[:]), ["p8", "c8"], ["pe"])
-        for k, s in DB:
-            mm(T[k][:, 0:s.stop - s.start], T.pm[:], T.rn[:, s], False, False, ["pm", "rn"], [k])
-        for k, s in DB:
-            mm(T[k][:, 0:s.stop - s.start], T.pe[:], T.ri[:, s], False, True, ["pe", "ri"], [k])
-        ts(T.l1[:], T.psL[:, 0:8], 1023.5, None, A.add, None, ["psL"], ["l1"])
-        ts(T.bg[:], T.tab[:, 0:2048].indirect(T.l1[:]), OFF, None, A.add, None, ["tab", "l1"], ["bg"])
-        tt(T.bh[:], T.st[:].indirect(T.l1[:]), T.bg[:], A.add, ["st", "l1", "bg"], ["bh"])
+        def pairs(l, lk, name, st, sp):
+            for k, c0, c1 in DB:
+                mm(T[k][:, 0:SEG[c1] - SEG[c0]], l, T[name][:, SEG[c0]:SEG[c1]], st, sp,
+                   [lk] + ["%s%d" % (name, c) for c in range(c0, c1)], [k], SEG[c1] - SEG[c0])
 
-    def winners(t, cs):
-        for c in cs:
-            k, s = DB[c >= SPLIT]
-            op("V", lambda: v.tensor_reduce(T.mn[:, c:c + 1], T[k][:, SEG[c] - s.start:SEG[c + 1] - s.start], AxisListType.X, A.min,
-                                            negate=True, apply_absolute_value=True), [k], ["mn%d" % c])
-
-    def lists(t, dst):
+        pairs(T.idb[:], "idb", "mk", True, False)
+        scan(T.ks[:], T.fm[:, 0:128], T.psK[:, P0], ["fm", "psK"] + KEYS, ["ks"], 128)
+        ts(PV[:, 128:136], T.ks[:, 15:128:16], MB, -MB, A.add, A.add, ["ks"], ["psV:1"], S)
+        tt(T.p8[:], T.ks[:, 15:128:16], PV[:, 128:136], A.subtract, ["ks", "psV:1"], ["p8"], S)
+        tt(T.pm[:], T.p8[:].indirect(T.c8[:]), T.pmk[:], A.mult, ["p8", "c8", "pmk"], ["pm"], gc(128))
+        mm(T.psL[:, 0:8], T.pm[:], T.cb[:], True, True, ["pm", "cb"], ["psL:0"])
+        vc(T.pe[:], T.p8[:].indirect(T.c8[:]), ["p8", "c8"], ["pe"], gc(128))
+        pairs(T.pm[:], "pm", "rn", False, False)
+        pairs(T.pe[:], "pe", "ri", False, True)
+        ts(T.l1[:], T.psL[:, 0:8], 1023.5, None, A.add, None, ["psL:0"], ["l1"], S)
+        ts(T.bg[:], TAB.indirect(T.l1[:]), OFF, None, A.add, None, ["tab", "l1"], ["bg"], gc(128))
+        tt(T.bh[:], T.st[:].indirect(T.l1[:]), T.bg[:], A.add, ["st", "l1", "bg"], ["bh"], gc(128))
+        for k, c0, c1 in DB:
+            for c in range(c0, c1):
+                least(T.mn[:, c:c + 1], T[k][:, SEG[c] - SEG[c0]:SEG[c + 1] - SEG[c0]], [k], ["mn%d" % c], max(S, SEG[c + 1] - SEG[c]))
         mk = ["mn%d" % c for c in range(8)]
+        ts(T.l2[:, 8 * t:8 * t + 8], T.mn[:], -0.5, None, A.add, None, mk, ["l2%d" % t], S)
+        return mk
+
+    def merged(t, dst, mk):
         o = 12 * t
-        tt(T.y2[:], T.mn[:], T.dmc[:], A.add, mk + ["dmc"], ["y2"])
+        act(T.wj[:], T.mn[:], F.Sign, mk, ["wj", "aa0"], bias=-SP - 0.25, c=S, acc=T.aa[:, 0:1])
         if t < RO - 1:
-            op("A", lambda: a.activation(T.wj[:], T.mn[:], F.Sign, accum_out=T.aa[:, 0:1]), mk, ["wj", "aa0"])
-            mm(T.psU[:, 64:65], T.onef[:], T.aa[:, 0:1], True, True, ["onef", "aa0"], ["psU"])
-            pa = T.psU[:, 64:65]
-            act(T.aa[:, 1:2], pa, F.Identity, ["psU"], ["aa1"], bias=-15.5)
-            act(T.aa[:, 2:3], T.aa[:, 1:2], F.Identity, ["aa1"], ["aa2"], bias=M32)
-            act(T.aa[:, 3:4], T.aa[:, 2:3], F.Identity, ["aa2"], ["aa3"], bias=M32, scale=-1.0)
-            act(T.sa[:, o + 8:o + 9], pa, F.Identity, ["psU", "aa3", "sa"], ["sb%d" % t], bias=T.aa[:, 3:4])
-        tt(T.sa[:, o:o + 8], T.y2[:], T.ls[:, 8 * t:8 * t + 8], A.max, ["y2", "ls%d" % t, "sa"], ["sa%d" % t])
-        send(dst, T.la[:, o:o + 12], T.sa[:, o:o + 12], ["sa", "sa%d" % t, "sb%d" % t], "ra%d" % t)
-        tt(T.z2[:], T.y2[:], T.psL[:, 0:8], A.max, ["y2", "psL"], ["z2"])
-        ts(T.l2[:, 8 * t:8 * t + 8], T.z2[:], 1023.5, None, A.add, None, ["z2"], ["l2%d" % t])
+            mm(T.psL[:, 32:33], T.half[:], T.aa[:, 0:1], True, True, ["half", "aa0"], ["psL:2"], 256)
+            act(T.sa[:, o + 8:o + 9], T.psL[:, 32:33], F.Copy, ["psL:2", "sa"], ["sb%d" % t], c=S)
+        tt(T.y2[:], T.wj[:], T.hd[:, 8 * t:8 * t + 8], A.mult, ["wj", "hd%d" % t], ["y2"], S)
+        tt(T.sa[:, o:o + 8], T.y2[:], T.md[:, 8 * t:8 * t + 8], A.add, ["y2", "md%d" % t, "sa"], ["sa%d" % t], S)
+        send(dst, T.la[:, o:o + 12], T.sa[:, o:o + 12], ["sa", "sa%d" % t, "sb%d" % t], "ra%d" % t, "la%d" % t)
 
-    def to_numbers(out, y, r, w):
-        ts(T.e1[:], y, 0.5, MB, A.mult, A.add, r, ["e1"])
-        ts(PV[:, 128:256], T.e1[:], -MB, None, A.add, None, ["e1"], ["psV:1"])
-        tt(out, y, PV[:, 128:256], A.subtract, r + ["psV:1"], w)
-
-    def lane_new(t, dst):
-        o = 128 * t
-        last = t == RO - 1
-        tt(PV[:, 128:256], T.ap[:], PW[:, 0:128], A.is_lt, ["ap", "psW:0"], ["psV:1"])
-        tt(T.m2[:], T.sg[:], PV[:, 128:256], A.max, ["sg", "psV:1"], ["m2"])
-        tt(PV[:, 256:384], T.m2[:], PW[:, 384:512], A.mult, ["m2", "psW:3"], ["psV:2"])
-        tt(T.na[:] if last else T.sn[:, o:o + 128], T.ap[:], PV[:, 256:384], A.max, ["ap", "psV:2"], ["na" if last else "sn%d" % t])
-        if last:
-            to_numbers(T.sn[:, o:o + 128], T.na[:], ["na"], ["sn%d" % t])
-        send(dst, T.ln[:, o:o + 128], T.sn[:, o:o + 128], ["sn%d" % t], "rn%d" % t)
+    def to_numbers(out, y, e, p, r, w):
+        ts(T[e][:], y, 0.5, MB, A.mult, A.add, r, [e])
+        ts(PW[:, 128 * p:128 * p + 128], T[e][:], -MB, None, A.add, None, [e], ["psW:%d" % p])
+        tt(out, y, PW[:, 128 * p:128 * p + 128], A.subtract, r + ["psW:%d" % p], w)
 
     def meet(t, dst):
-        th = 8.0 + t
         o = 128 * t
         last = t == RO - 1
-        ts(T.bl[:], T.bh[:], 31, None, A.bitwise_and, None, ["bh"], ["bl"])
-        ts(T.bk[:], T.bh[:], 15, 7, A.arith_shift_right, A.bitwise_and, ["bh"], ["bk"])
-        ts(PW[:, 0:128], T.bl[:], th, 64.0, A.is_ge, A.mult, ["bl"], ["psW:0"])
-        ts(T.bi[:], T.bh[:], 16, None, A.bitwise_and, None, ["bh"], ["bi"])
-        tt(PW[:, 128:256], T.bk[:], PW[:, 0:128], A.is_le, ["bk", "psW:0"], ["psW:1"])
-        tt(T.bs[:], T.bl[:], PW[:, 0:128], A.add, ["bl", "psW:0"], ["bs"])
-        act(T.bd2[:], T.bs[:], F.Relu, ["bs"], ["bd2"], bias=12.0 + t, scale=-1.0)
-        tt(T.bp[:], T.bg[:], PW[:, 128:256], A.mult, ["bg", "psW:1"], ["bp"])
-        tt(PW[:, 256:384], T.bi[:], PA[:, 128:256], A.min, ["bi", "psA:1"], ["psW:2"])
-        tt(T.di[:], T.bp[:], PA[:, 384:512], A.subtract, ["bp", "psA:3"], ["di"])
+        tt(T.di[:], T.bg[:], PA[:, P3], A.subtract, ["bg", "psA:3"], ["di"])
         act(T.dq[:], T.di[:], F.Square, ["di"], ["dq"], scale=1.0 / 2048)
         act(T.sg[:], T.dq[:], F.Sign, ["dq"], ["sg"], bias=1.0, scale=-1.0)
-        tt(PW[:, 128:256], T.bd2[:], PA[:, 256:384], A.min, ["bd2", "psA:2"], ["psW:1"])
-        winners(t, range(0, 3))
-        tt(PW[:, 256:384], T.ap[:], PW[:, 256:384], A.add, ["ap", "psW:2"], ["psW:2"])
-        tt(T.t2[:], T.bp[:], PW[:, 128:256], A.add, ["bp", "psW:1"], ["t2"])
-        tt(PV[:, 128:256], T.bp[:], PV[:, 0:128], A.is_lt, ["bp", "psV:0"], ["psV:1"])
-        tt(PW[:, 384:512], T.t2[:], PW[:, 256:384], A.max, ["t2", "psW:2"], ["psW:3"])
-        winners(t, range(3, 8))
-
-        def site_new():
-            tt(T.t2[:], T.sg[:], PV[:, 384:512] if last else PV[:, 128:256], A.max, ["sg", "psV:3" if last else "psV:1"], ["t2"])
-            tt(PV[:, 256:384], T.t2[:], PW[:, 384:512], A.mult, ["t2", "psW:3"], ["psV:2"])
-            tt(T.na[:] if last else T.nb[:, o:o + 128], T.bp[:], PV[:, 256:384], A.max, ["bp", "psV:2"], ["na" if last else "nb%d" % t])
-
-        if last:
-            lists(t, dst)
-            lane_new(t, dst)
-            tt(PV[:, 384:512], T.bp[:], PV[:, 0:128], A.is_lt, ["bp", "psV:0"], ["psV:3"])
-            site_new()
-            to_numbers(T.nb[:, o:o + 128], T.na[:], ["na"], ["nb%d" % t])
-        else:
-            lists(t, dst)
-            site_new()
+        ts(T.bl[:], T.bh[:], 31, None, A.bitwise_and, None, ["bh"], ["bl"])
+        ts(T.bk[:], T.bh[:], 15, 7, A.arith_shift_right, A.bitwise_and, ["bh"], ["bk"])
+        ts(T.bi[:], T.bh[:], 16, None, A.bitwise_and, None, ["bh"], ["bi"])
+        ts(PW[:, P0], T.bl[:], 8.0 + t, 64.0, A.is_ge, A.mult, ["bl"], ["psW:0"])
+        tt(T.y3[:], PA[:, P2], T.bl[:], A.subtract, ["psA:2", "bl"], ["y3"])
+        tt(PW[:, P2], T.bi[:], PA[:, P1], A.min, ["bi", "psA:1"], ["psW:2"])
+        tt(PW[:, P1], T.bk[:], PW[:, P0], A.is_le, ["bk", "psW:0"], ["psW:1"])
+        tt(PV[:, P3], T.y3[:], PW[:, P0], A.subtract, ["y3", "psW:0"], ["psV:3"])
+        tt(T.y4[:], T.bg[:], PV[:, P3], A.add, ["bg", "psV:3"], ["y4"])
+        tt(PW[:, P2], T.ap[:], PW[:, P2], A.add, ["ap", "psW:2"], ["psW:2"])
+        tt(T.t2[:], T.y4[:], PW[:, P1], A.mult, ["y4", "psW:1"], ["t2"])
+        tt(T.bp[:], T.bg[:], PW[:, P1], A.mult, ["bg", "psW:1"], ["bp"])
+        tt(T.smv[:], T.sg[:], PW[:, P1], A.mult, ["sg", "psW:1"], ["smv"])
+        tt(PW[:, P3], T.t2[:], PW[:, P2], A.max, ["t2", "psW:2"], ["psW:3"])
+        tt(PV[:, P1], T.bp[:], PV[:, P0], A.is_lt, ["bp", "psV:0"], ["psV:1"])
+        tt(T.m2[:], T.smv[:], PV[:, P1], A.max, ["smv", "psV:1"], ["m2"])
+        tt(PV[:, P1], T.m2[:], PW[:, P3], A.mult, ["m2", "psW:3"], ["psV:1"])
+        tt(T.nc[:] if last else T.nb[:, o:o + 128], T.bp[:], PV[:, P1], A.max, ["bp", "psV:1"], ["nc" if last else "nb%d" % t])
+        if not last:
             scatter("tab", T.l2[:, 8 * t:8 * t + 8], T.nb[:, o:o + 128], ["l2%d" % t, "nb%d" % t], -OFF)
+        tt(PV[:, P2], T.ap[:], PW[:, P0], A.is_lt, ["ap", "psW:0"], ["psV:2"])
+        tt(PV[:, P3], T.bp[:], PW[:, P3], A.max, ["bp", "psW:3"], ["psV:3"])
+        tt(T.m3[:], T.smv[:], PV[:, P2], A.max, ["smv", "psV:2"], ["m3"])
+        tt(PV[:, P2], T.m3[:], PV[:, P3], A.mult, ["m3", "psV:3"], ["psV:2"])
+        tt(T.na[:] if last else T.sn[:, o:o + 128], T.ap[:], PV[:, P2], A.max, ["ap", "psV:2"], ["na" if last else "sn%d" % t])
+        if last:
+            to_numbers(T.sn[:, o:o + 128], T.na[:], "c1", 0, ["na"], ["sn%d" % t])
+            to_numbers(T.nb[:, o:o + 128], T.nc[:], "c2", 1, ["nc"], ["nb%d" % t])
+        send(dst, T.ln[:, o:o + 128], T.sn[:, o:o + 128], ["sn%d" % t], "rn%d" % t, "ln%d" % t)
 
     def back(t):
         o = 128 * t
         tab, off = ("tab", -OFF) if t < RO - 1 else ("fin", 0.0)
-        ts(T.lr[:], T.la[:, 12 * t:12 * t + 8], 1023.5, None, A.add, None, ["la%d" % t], ["lr"])
-        scatter(tab, T.lr[:], T.ln[:, o:o + 128], ["lr", "ln%d" % t, tab], off)
+        vc(T.lr[:], T.la[:, 12 * t:12 * t + 8], ["la%d" % t], ["lr"], S)
+        scatter(tab, T.lr[:], T.ln[:, o:o + 128], ["lr", "ln%d" % t, "~se%d" % (t + 1), tab], off)
         scatter(tab, T.l2[:, 8 * t:8 * t + 8], T.nb[:, o:o + 128], ["l2%d" % t, "nb%d" % t, tab], off)
 
-    last_banks = ["psK", "psU", "psD0", "psD1"]
-
-    def last_table(step):
-        for i in range(4):
-            s = slice(512 * i, 512 * i + 512)
-            if step == 0:
-                act(T.cf[:, s], T.tab[:, s], F.Identity, ["tab"], ["cf%d" % i], bias=MB, scale=0.5)
-            elif step == 1:
-                act(T[last_banks[i]][:], T.cf[:, s], F.Identity, ["cf%d" % i], [last_banks[i]], bias=-MB - OFF / 2)
-            else:
-                tt(T.fin[:, s], T.tab[:, s], T[last_banks[i]][:], A.subtract, ["tab", last_banks[i]], ["fin"])
+    def last_table():
+        for i in range(8):
+            s, k = slice(SP + 256 * i, SP + 256 * i + 256), ("psK", "psU", "psD0", "psD1")[i // 2]
+            p, pk = T[k][:, 256 * (i % 2):256 * (i % 2) + 256], ["%s:%d" % (k, 2 * (i % 2) + j) for j in range(2)]
+            cf = T.cf[:, 256 * i:256 * i + 256]
+            act(cf, T.tab[:, s], F.Identity, ["tab"], ["cf%d" % i], bias=MB, scale=0.5, c=256)
+            act(p, cf, F.Identity, ["cf%d" % i], pk, bias=-MB - OFF / 2, c=256)
+            tt(T.fin[:, s], T.tab[:, s], p, A.subtract, ["tab"] + pk, ["fin%d" % i], 256)
+        ms(T.fin[:, 0:16], 0.0, ["fin"], ["fin%d" % i for i in range(8)])
 
     first_lanes()
+    first_table()
     for t in range(RO):
         callee = T.cores[(rank + 1 + t % 7) % N]
         caller = T.cores[(rank - 1 - t % 7) % N]
-        for k, s in (("lo", "ro"), ("le", "re"), ("ln", "rn"), ("la", "ra")):
-            landed("%s%d" % (k, t), "%s%d" % (s, t))
         lane_list(t, callee)
-        mm(T.psU[:, 0:32], T.ones[:], T.uc[:], True, False, ["ones", "uc0", "uc"], ["psU"])
         vs = VS if t else VS0
-        mid = (vs + 128) // 4 * 2
-        if t == 0:
-            first_table()
-        gather_scalar(vs, mid, "A")
-        gather_scalar(mid, 128, "B")
-        if t:
-            lane_new(t - 1, prev)
-        gather_vector(0, vs, "V")
-        scan(0, vs, "V")
-        scan(vs, mid, "A")
-        scan(mid, 128, "B")
-        cand(t, callee, "VAB")
+        cand(t, callee, features([0, vs, (vs + 128) // 4 * 2, 128]))
         expand(t)
         own_side(t)
-        own_side_scalar(t)
         if t:
             back(t - 1)
-        else:
-            pair_constants()
         score(t)
-        if t == RO - 1:
-            last_table(0)
-        partner(t)
+        merged(t, caller, partner(t))
         meet(t, caller)
-        prev = caller
-    last_table(1)
-    last_table(2)
+    last_table()
     back(RO - 1)
-    dma("S", T.yent[:, 0:1024], T.fin[:, 0:1024], ["fin"], [], "dy")
-    dma("A", T.yent[:, 1024:2048], T.fin[:, 1024:2048], ["fin"], [], "dy")
+    for i in plan(calls):
+        acts[i]()
+    dma("S", T.yent[:, 0:1024], T.fin[:, SP:SP + 1024], ["fin"], [], "dy")
+    dma("A", T.yent[:, 1024:2048], T.fin[:, SP + 1024:W], ["fin"], [], "dy")
     for s in tot:
         wait("G", [(s, tot[s], {})])

@@ -9,12 +9,13 @@ SP = 128
 W = SP + 2048
 NE = 8
 VS, VS0 = 56, 56
-HA = 2
+GA = (2, 3)
+HA = (0,)
 SEG = [8 * c * (c + 1) + c for c in range(9)]
-SPLIT = 6
-HOP, FLIGHT, LATE, SLACK = 240, 2700, 4000, 120
+SPLIT = (0, 4, 6, 8)
+HOP, FLIGHT, LATE, SLACK, ROOM = 260, 2700, 4000, 40, 100
 GATHER, SCATTER = 1.5, 3.8
-LOADED = {"wti": 2400, "kpi": 2400, "ents": 5600, "fw": 9400}
+LOADED = {"wti": 4200, "kpi": 4200, "ents": 4000, "fw": 7000}
 
 _F, _B, _I, _H, _U = "float32", "bfloat16", "int32", "float16", "uint16"
 SCRATCH = {}
@@ -23,16 +24,16 @@ for _n, _w, _d in [
         ("wti", 4, _I), ("kpi", 4, _I), ("pi", 4, _I), ("pj", 4, _I), ("pcol", 16, _F), ("sti", 64, _I), ("stj", 64, _I),
         ("ones", 128, _B), ("half", 128, _F), ("bd0", 128, _B), ("bd", 128, _B), ("wblk", 128, _B), ("w4", 512, _B),
         ("ramp", 240, _B), ("r16", 128, _B), ("r4", 128, _B), ("cm", 128, _B), ("idb", 128, _B), ("ka0", 128, _B), ("ka", 128, _B),
-        ("kr", 4, _B), ("kb", 4, _F), ("kq", 4, _F), ("k16", 4, _F), ("k8", 4, _F), ("kc", 4, _F), ("uc", 32, _B), ("c2k", 32, _B),
+        ("kr", 4, _B), ("kb", 8, _F), ("k16", 4, _F), ("k8", 4, _F), ("kc", 4, _F), ("uc", 32, _B), ("c2k", 128, _B),
         ("mx", 4, _F), ("zg", 8, _F), ("zp", 8, _B), ("zn", 8, _B), ("zh", 8, _B), ("cb", 8, _H), ("sel", 32, _H), ("cl", 32, _U),
         ("c8", 8, _U), ("pmk", 128, _F), ("ri", 584, _H), ("rn", 584, _H), ("mk", 584, _B), ("spc", 8, _F), ("ls", 8, _F),
         ("hd", 32, _F), ("md", 32, _F), ("rx", 136, _B), ("ramp2", 128, _B), ("am", 8, _F), ("fm", 2048, _B),
         ("i1", 128, _I), ("i3", 128, _I), ("ly", 128, _F), ("lst", 128, _U), ("fg", 2048, _B), ("fs", 2048, _B),
         ("ur", 32, _F), ("uu", 32, _F), ("vq", 128, _F), ("u5", 128, _I), ("u6", 128, _I),
         ("se", 512, _U), ("le", 512, _U), ("so", 512, _F), ("lo", 512, _F), ("sa", 48, _F), ("la", 48, _F),
-        ("sn", 512, _F), ("ln", 512, _F), ("nb", 512, _F), ("lr", 8, _U), ("c1", 128, _F), ("c2", 128, _F), ("c3", 128, _F),
+        ("sn", 520, _F), ("ln", 520, _F), ("nb", 512, _F), ("lr", 8, _U), ("c1", 128, _F), ("c2", 128, _F), ("c3", 128, _F),
         ("ox", 512, _F), ("dd", 2048, _B), ("da", 2048, _B), ("db", 2048, _B), ("mt", 2048, _B), ("eh", 512, _H),
-        ("ks", 128, _F), ("p8", 8, _F), ("pe", 128, _H), ("pm", 128, _H), ("l1", 8, _U), ("l2", 32, _U),
+        ("ks", 128, _F), ("kh", 128, _H), ("p8", 8, _F), ("pe", 128, _H), ("pm", 128, _H), ("l1", 8, _U), ("l2", 32, _U),
         ("mn", 8, _F), ("y2", 8, _F), ("wj", 8, _F), ("aa", 8, _F),
         ("ah", 128, _I), ("al", 128, _I), ("ak", 128, _I), ("av", 128, _F), ("ap", 128, _F), ("as2", 128, _F), ("ac", 128, _F),
         ("ar", 128, _F), ("bg", 128, _F), ("bh", 128, _I), ("bl", 128, _I), ("bk", 128, _I), ("bi", 128, _I), ("bp", 128, _F),
@@ -58,7 +59,7 @@ def plan(calls):
         for k in w:
             for j in rd.get(k, []) + ([wr[k]] if k in wr else []):
                 if j != i:
-                    pre[i][j] = max(pre[i].get(j, 0), 0 if calls[j][0] == q else HOP)
+                    pre[i][j] = max(pre[i].get(j, 0), 0 if calls[j][0] == q == "P" else HOP)
         for k in w:
             wr[k], rd[k] = i, []
         for k in r:
@@ -86,7 +87,9 @@ def plan(calls):
         q = calls[i][0]
         mine = [j for j in ready if calls[j][0] == q]
         if q != "R":
-            fits = [j for j in mine if all(way[o] <= way[j] or at[j] + calls[j][1] <= at[o] + SLACK for o in mine)]
+            last = max(at[o] + way[o] for o in ready) + SLACK
+            fits = [j for j in mine
+                    if all(way[o] <= way[j] or at[j] + calls[j][1] <= max(at[o], min(at[o] + ROOM, last - way[o])) for o in mine)]
             i = min(fits, key=lambda j: (at[j], -way[j]))
         ready.remove(i)
         end[i] = at[i] + calls[i][1]
@@ -133,8 +136,7 @@ def rank_program(g, core, T, topo):
         for k in r:
             evs += [e for o, e in wr.get(k, [])]
         for k in w:
-            evs += [e for o, e in wr.get(k, []) if o != q]
-            evs += [e for o, e in rd.get(k, []) if o != q]
+            evs += [e for o, e in wr.get(k, []) + rd.get(k, []) if o != q or q != "P"]
         for k in list(r) + list(w):
             if k[:2] == "ps":
                 evs += [e for o, e in bank.get(k.split(":")[0], {}).items() if o != q]
@@ -237,10 +239,10 @@ def rank_program(g, core, T, topo):
     def gc(n):
         return int(60 + GATHER * n)
 
-    dma("S", T.wti[:, 0:1], T.wt[:, 0:1], [], [], "dsm")
-    dma("A", T.kpi[:, 0:1], T.kap[:, 0:1], [], [], "dsm")
     dma("S", T.ents[:, 0:1024], T.ent[:, 0:1024], [], [], "dent")
     dma("A", T.ents[:, 1024:2048], T.ent[:, 1024:2048], [], [], "dent")
+    dma("S", T.wti[:, 0:1], T.wt[:, 0:1], [], [], "dsm")
+    dma("A", T.kpi[:, 0:1], T.kap[:, 0:1], [], [], "dsm")
     dma("S", T.fw[:, 0:2048], T.feat[:, 0:2048], [], [], "dfe")
     dma("A", T.fw[:, 2048:4096], T.feat[:, 2048:4096], [], [], "dfe")
     for k, s in (("wti", "dsm"), ("kpi", "dsm"), ("ents", "dent"), ("fw", "dfe")):
@@ -256,13 +258,16 @@ def rank_program(g, core, T, topo):
     iota(T.r4[:], [[0, 32], [1, 4]], 0, 0, ["r4"], 128)
     iota(T.r16[:], [[0, 8], [1, 16]], 0, 0, ["r16"], 128)
     R = T.ramp[:, 112:240]
-    for i in range(4):
-        ms(T.fm[:, 512 * i:512 * i + 512], 1.0, ["fm%d" % i], c=256)
-    ms(T.fm[:, 0:2048:16], 0.0, ["fm"], ["fm%d" % i for i in range(4)])
+    ms(T.fm[:, 1:256], 1.0, ["fm0"], c=128)
+    ms(T.fm[:, 0:256:16], 0.0, ["fm"], ["fm0"])
+    vc(T.fm[:, 256:512], T.fm[:, 0:256], ["fm"], ["fm"])
+    for n in (512, 1024, 1536):
+        act(T.fm[:, n:n + 512], T.fm[:, 0:512], F.Copy, ["fm"], ["fm%d" % n], c=512)
     ms(T.fw[:, 4096:4112], 0.0, ["fwz"])
     ms(T.uc[0:64, :], -32.0, ["uc0"])
     ms(T.uc[64:128, :], 1.0 / 128, ["uc"])
-    ms(T.c2k[:], 2048.0, ["c2k"])
+    for b in range(4):
+        ms(T.c2k[:, b:128:4], 256.0 if b in HA else 288.0, ["c2k"], ["c2k"])
     ms(T.half[:], 0.5, ["half"], c=128)
     ms(T.sa[:], 0.0, ["sa"])
     ts(T.pj[:, 0:1], T.pi[:, 0:1], 15, None, A.bitwise_and, None, ["pi"], ["pj0"], S)
@@ -273,11 +278,11 @@ def rank_program(g, core, T, topo):
     vc(T.pcol[:, 0:4], T.pj[:, 0:4], ["pj0", "pj1", "pj2", "pj3"], ["pc"], S)
     vc(col(4), T.pi[:, 0:1], ["pi"], ["pc4"], S)
     ts(T.st[:, 0:64], T.stj[:], 4096.0, -2065.0 - OFF, A.mult, A.add, ["stj"], ["st"], S)
-    n = 64
-    while n < 2048:
-        m = min(n, 512)
-        act(T.st[:, n:n + m], T.st[:, 0:m], F.Copy, ["st"], ["st"], c=m)
-        n += m
+    for n in (64, 128, 256):
+        vc(T.st[:, n:2 * n], T.st[:, 0:n], ["st"], ["st"], n)
+    for n in (512, 1024, 1536):
+        act(T.st[:, n:n + 512], T.st[:, 0:512], F.Copy, ["st"], ["st%d" % n], c=512)
+    ST = ["st", "st512", "st1024", "st1536"]
     ts(col(5), col(3), 4.0, col(2), A.mult, A.add, ["pc"], ["pc5"], S)
     ts(col(8), col(0), 0.5, None, A.add, None, ["pc"], ["pc8"], S)
     ts(col(9), col(0), 16.0, float(SP), A.mult, A.add, ["pc"], ["pc9"], S)
@@ -286,7 +291,7 @@ def rank_program(g, core, T, topo):
     ts(T.mx[:], T.ramp[:, 112:116], col(1), None, A.is_equal, None, ["ramp", "pc"], ["mx"], S)
     ts(T.cl[:], T.ramp[:, 112:144], 4.0, col(1), A.mult, A.add, ["ramp", "pc"], ["cl"], S)
     vc(T.c8[:], T.ramp[:, 112:120], ["ramp"], ["c8"], S)
-    ts(T.sel[:], T.ramp[:, 112:144], col(5), None, A.is_equal, None, ["ramp", "pc5"], ["sel"], S)
+    ts(T.sel[:], T.ramp[:, 112:144], col(5), 1.0 / 64, A.is_equal, A.mult, ["ramp", "pc5"], ["sel"], S)
     ts(T.idb[:], R, col(4), None, A.is_equal, None, ["ramp", "pc4"], ["idb"], S)
     ts(T.spc[:], T.ramp[:, 112:120], 16.0, col(8), A.mult, A.add, ["ramp", "pc8"], ["spc"], S)
     ts(T.ls[:], T.ramp[:, 112:120], 256.0, col(9), A.mult, A.add, ["ramp", "pc9"], ["ls"], S)
@@ -295,9 +300,9 @@ def rank_program(g, core, T, topo):
     for t in range(RO):
         ts(T.hd[:, 8 * t:8 * t + 8], T.am[:], t + 0.5, 0.5, A.add, A.mult, ["am"], ["hd%d" % t], S)
         ts(T.md[:, 8 * t:8 * t + 8], T.y2[:], t - 0.5, 0.5, A.add, A.mult, ["y2"], ["md%d" % t], S)
-    ts(T.zp[:], T.zg[:], 32768.0, None, A.mult, None, ["zg"], ["zp"], S)
-    ts(T.zn[:], T.zg[:], -32768.0, None, A.mult, None, ["zg"], ["zn"], S)
-    ts(T.zh[:], T.zg[:], 16384.0, None, A.mult, None, ["zg"], ["zh"], S)
+    ts(T.zp[:], T.zg[:], 512.0, None, A.mult, None, ["zg"], ["zp"], S)
+    ts(T.zn[:], T.zg[:], -512.0, None, A.mult, None, ["zg"], ["zn"], S)
+    ts(T.zh[:], T.zg[:], 256.0, None, A.mult, None, ["zg"], ["zh"], S)
     vc(T.cb[:], T.zg[:], ["zg"], ["cb"], S)
     vc(col(6), T.wti[:, 0:1], ["wti"], ["wcol"], S)
     vc(col(7), T.kpi[:, 0:1], ["kpi"], ["kcol"], S)
@@ -308,12 +313,12 @@ def rank_program(g, core, T, topo):
     ts(T.kr[:], T.ramp[:, 112:116], col(2), col(7), A.is_equal, A.mult, ["ramp", "pc", "kcol"], ["kr"], S)
     tt(T.ka[:], T.ka0[:], T.bd[:], A.mult, ["ka0", "bd"], ["ka"], 256)
     mm(T.psL[:, 16:20], T.ka[:], T.kr[:], True, True, ["ka", "kr"], ["psL:1"])
-    ts(T.pmk[:], T.r16[:], col(0), None, A.is_equal, None, ["r16", "pc"], ["pmk"])
-    ts(T.cm[:], T.r16[:], -16.0, 240.0, A.mult, A.add, ["r16"], ["cm"], S)
-    vc(T.kb[:], T.psL[:, 16:20], ["psL:1"], ["kb"], S)
+    ts(T.pmk[:], T.r16[:], col(0), 64.0, A.is_equal, A.mult, ["r16", "pc"], ["pmk"])
+    ts(T.cm[:], T.r16[:], -0.25, 3.75, A.mult, A.add, ["r16"], ["cm"], S)
+    vc(T.kb[:, 0:4], T.psL[:, 16:20], ["psL:1"], ["kb"], S)
     ts(T.k16[:], T.psL[:, 16:20], 16.0, 2047.5, A.mult, A.add, ["psL:1"], ["k16"], S)
-    tt(T.kq[:], T.kb[:], T.psL[:, 16:20], A.mult, ["kb", "psL:1"], ["kq"], S)
-    ts(T.k8[:], T.kq[:], -8.0, -0.375, A.mult, A.add, ["kq"], ["k8"], S)
+    tt(T.kb[:, 4:8], T.kb[:, 0:4], T.psL[:, 16:20], A.mult, ["kb", "psL:1"], ["kq"], S)
+    ts(T.k8[:], T.kb[:, 4:8], -8.0, -0.375, A.mult, A.add, ["kq"], ["k8"], S)
     ms(T.ri[:], 0.0, ["ri0"], c=292)
     ms(T.mk[:], 1024.0 + SP, ["mk0"], c=292)
     ms(T.rx[:, 0:128], -8192.0, ["rx0"])
@@ -367,7 +372,7 @@ def rank_program(g, core, T, topo):
                 act(T.fg[:, c], T.fw[:].indirect(T.lst[:, n0:n1]), F.Copy, r, ["fg%d" % i], c=gc(16 * (n1 - n0)) - 64)
             else:
                 vc(T.fg[:, c], T.fw[:].indirect(T.lst[:, n0:n1]), r, ["fg%d" % i], gc(16 * (n1 - n0)))
-            scan(T.fs[:, c], T.fm[:, c], T.fg[:, c], ["fm", "fg%d" % i], ["fs%d" % i], 8 * (n1 - n0))
+            scan(T.fs[:, c], T.fm[:, c], T.fg[:, c], ["fm", "fm512", "fm1024", "fm1536", "fg%d" % i], ["fs%d" % i], 8 * (n1 - n0))
         return ["fs%d" % i for i in range(len(cuts) - 1)]
 
     def cand(t, dst, fs):
@@ -403,9 +408,11 @@ def rank_program(g, core, T, topo):
         act(T.c2[:], T.c1[:], F.Identity, ["c1"], ["c2"], bias=M16 + 16.0)
         act(T.c3[:], T.c2[:], F.Identity, ["c2"], ["c3"], bias=-M16 - 16.0)
         act(T.ox[:], T.c3[:].indirect(T.cl[:]), F.Identity, ["c3", "cl"], ["ox"], bias=8.5, c=gc(512) - 64)
+        if GA:
+            act(PW[:], T.ox[:], F.Copy, ["ox"], ["psW"], c=512)
 
     def own_side(t):
-        tt(T.ah[:], T.st[:, t:2048:16], PA[:, P0], A.add, ["psA:0", "st"], ["ah"])
+        tt(T.ah[:], T.st[:, t:2048:16], PA[:, P0], A.add, ["psA:0"] + ST, ["ah"])
         ts(T.al[:], T.ah[:], 31, None, A.bitwise_and, None, ["ah"], ["al"])
         ts(T.ak[:], T.ah[:], 15, 7, A.arith_shift_right, A.bitwise_and, ["ah"], ["ak"])
         ts(PV[:, P0], T.al[:], 8.0 + t, 64.0, A.is_ge, A.mult, ["al"], ["psV:0"])
@@ -416,7 +423,7 @@ def rank_program(g, core, T, topo):
         act(T.ar[:], T.as2[:], F.Relu, ["as2"], ["ar"], bias=80 * 2.0 ** 25, scale=-2.0 ** 25)
         act(PA[:, P1], T.as2[:], F.Relu, ["as2"], ["psA:1"], bias=12.0 + t, scale=-1.0)
         act(PA[:, P3], T.ac[:], F.Identity, ["ac"], ["psA:3"], bias=-MN)
-        act(PA[:, P2], T.ar[:], F.Identity, ["ar"], ["psA:2"], bias=12.0 + t, scale=-1.0)
+        act(PA[:, P2], T.ar[:], F.Identity, ["ar"], ["psA:2"], bias=OFF + 13.0 + t, scale=-1.0)
 
     KEYS = ["psK:%s%d%d" % (k, i, x) for k in ("mt", "db") for i in range(4) for x in range(4)] + ["psK:e%d" % i for i in range(4)]
 
@@ -433,8 +440,7 @@ def rank_program(g, core, T, topo):
             op("P", fn, r, [k], 64)
 
         mm(K[:, P0], T.ones[:], T.cm[:], True, False, ["ones", "cm"], ["psK"], 128)
-        for i in range(HA, 4):
-            mm(K[:, i:128:4], T.ones[:], T.c2k[:], False, False, ["ones", "c2k"], ["psK"] + KEYS)
+        mm(K[:, P0], T.ones[:], T.c2k[:], False, False, ["ones", "c2k"], ["psK"] + KEYS, 128)
 
         def sums(i, tile, k, z):
             for x in range(4):
@@ -442,40 +448,51 @@ def rank_program(g, core, T, topo):
 
         for i in range(4):
             c = slice(512 * i, 512 * i + 512)
-            tt(T.dd[:, c], TAB.indirect(T.le[:, o + 32 * i:o + 32 * i + 32]), T.ox[:], A.subtract,
-               ["tab", lk, "ox", "~dd%d" % (i - 1), "~mt%d" % (i - 2)] + ["~eh%d" % x for x in range(4) if i == 2], ["dd%d" % i], gc(512))
-            for x in range(4 if i == 0 else 0):
-                ts(T.eh[:, x:512:4], T.le[:, o:o + 128], -1023.5, T.mx[:, x:x + 1], A.add, A.mult, [lk, "mx", "~dd0"], ["eh%d" % x], S)
-            if i < HA:
+            cands = TAB.indirect(T.le[:, o + 32 * i:o + 32 * i + 32])
+            turn = ["~dd%d" % (i - 1), "~mt%d" % (i - 2)] + ["~eh%d" % x for x in range(4 if i == 2 else 0)]
+            if i in GA:
+                ck = ["cf%d" % (2 * i), "cf%d" % (2 * i + 1)]
+                act(T.cf[:, c], cands, F.Copy, ["tab", lk] + ["~cf%d" % (2 * j) for j in GA if j < i], ck, c=gc(512) - 64)
+                tt(T.dd[:, c], T.cf[:, c], PW[:], A.subtract, ck + ["psW"] + turn, ["dd%d" % i], 512)
+            else:
+                tt(T.dd[:, c], cands, T.ox[:], A.subtract, ["tab", lk, "ox"] + turn, ["dd%d" % i], gc(512))
+            if i in HA:
                 act(T.da[:, c], T.dd[:, c], F.Abs, ["dd%d" % i], ["da%d" % i], c=512)
                 act(T.db[:, c], T.da[:, c], F.Sign, ["da%d" % i], ["db%d" % i], bias=-8.25, c=512)
             else:
                 ts(T.db[:, c], T.dd[:, c], M16, M16, A.add, A.is_equal, ["dd%d" % i], ["db%d" % i], 256)
             ts(T.mt[:, c], T.dd[:, c], MN + 4096.0, MN + 4096.0, A.add, A.is_equal, ["dd%d" % i], ["mt%d" % i], 256)
             sums(i, T.mt, "mt%d" % i, "zp")
-            sums(i, T.db, "db%d" % i, "zh" if i < HA else "zn")
+            sums(i, T.db, "db%d" % i, "zh" if i in HA else "zn")
+            for x in range(4 if i == 0 else 0):
+                ts(T.eh[:, x:512:4], T.le[:, o:o + 128], -1023.5, T.mx[:, x:x + 1], A.add, A.mult, [lk, "mx", "~dd0"], ["eh%d" % x], S)
             add(K[:, i:128:4], T.eh[:, 128 * i:128 * i + 128], T.sel[:], ["sel"] + ["eh%d" % x for x in range(4)], "psK:e%d" % i)
 
-    DB = [("psD0", 0, SPLIT), ("psD1", SPLIT, 8)]
+    DB = [(k, SPLIT[i], SPLIT[i + 1]) for i, k in enumerate(("psD0", "psD1", "psU")[:len(SPLIT) - 1])]
 
     def partner(t):
-        def pairs(l, lk, name, st, sp):
-            for k, c0, c1 in DB:
-                mm(T[k][:, 0:SEG[c1] - SEG[c0]], l, T[name][:, SEG[c0]:SEG[c1]], st, sp,
-                   [lk] + ["%s%d" % (name, c) for c in range(c0, c1)], [k], SEG[c1] - SEG[c0])
+        def pairs(i, l, lk, name, st, sp, after=()):
+            k, c0, c1 = DB[i]
+            mm(T[k][:, 0:SEG[c1] - SEG[c0]], l, T[name][:, SEG[c0]:SEG[c1]], st, sp,
+               [lk] + ["%s%d" % (name, c) for c in range(c0, c1)] + list(after), [k], SEG[c1] - SEG[c0])
 
-        pairs(T.idb[:], "idb", "mk", True, False)
+        for i in range(len(DB)):
+            pairs(i, T.idb[:], "idb", "mk", True, False)
         scan(T.ks[:], T.fm[:, 0:128], T.psK[:, P0], ["fm", "psK"] + KEYS, ["ks"], 128)
-        ts(PV[:, 128:136], T.ks[:, 15:128:16], MB, -MB, A.add, A.add, ["ks"], ["psV:1"], S)
-        tt(T.p8[:], T.ks[:, 15:128:16], PV[:, 128:136], A.subtract, ["ks", "psV:1"], ["p8"], S)
+        scan(T.kh[:], T.fm[:, 0:128], T.psK[:, P0], ["fm", "psK"] + KEYS, ["kh"], 128)
+        tt(T.p8[:], T.ks[:, 15:128:16], T.kh[:, 15:128:16], A.subtract, ["ks", "kh"], ["p8"], S)
         tt(T.pm[:], T.p8[:].indirect(T.c8[:]), T.pmk[:], A.mult, ["p8", "c8", "pmk"], ["pm"], gc(128))
         mm(T.psL[:, 0:8], T.pm[:], T.cb[:], True, True, ["pm", "cb"], ["psL:0"])
-        vc(T.pe[:], T.p8[:].indirect(T.c8[:]), ["p8", "c8"], ["pe"], gc(128))
-        pairs(T.pm[:], "pm", "rn", False, False)
-        pairs(T.pe[:], "pe", "ri", False, True)
+        ts(T.pe[:], T.p8[:].indirect(T.c8[:]), 64.0, None, A.mult, None, ["p8", "c8"], ["pe"], gc(128))
+        after = "~psL:0"
+        for i in range(len(DB)):
+            pairs(i, T.pm[:], "pm", "rn", False, False, [after])
+            pairs(i, T.pe[:], "pe", "ri", False, True)
+            after = "~%s:0" % DB[i][0]
         ts(T.l1[:], T.psL[:, 0:8], 1023.5, None, A.add, None, ["psL:0"], ["l1"], S)
         ts(T.bg[:], TAB.indirect(T.l1[:]), OFF, None, A.add, None, ["tab", "l1"], ["bg"], gc(128))
-        tt(T.bh[:], T.st[:].indirect(T.l1[:]), T.bg[:], A.add, ["st", "l1", "bg"], ["bh"], gc(128))
+        act(T.c1[:], TAB.indirect(T.l1[:]), F.Identity, ["tab", "l1"], ["c1"], bias=-8.5, c=gc(128) - 64)
+        tt(T.bh[:], T.st[:].indirect(T.l1[:]), T.bg[:], A.add, ST + ["l1", "bg"], ["bh"], gc(128))
         for k, c0, c1 in DB:
             for c in range(c0, c1):
                 least(T.mn[:, c:c + 1], T[k][:, SEG[c] - SEG[c0]:SEG[c + 1] - SEG[c0]], [k], ["mn%d" % c], max(S, SEG[c + 1] - SEG[c]))
@@ -490,6 +507,9 @@ def rank_program(g, core, T, topo):
             mm(T.psL[:, 32:33], T.half[:], T.aa[:, 0:1], True, True, ["half", "aa0"], ["psL:2"], 256)
             act(T.sa[:, o + 8:o + 9], T.psL[:, 32:33], F.Copy, ["psL:2", "sa"], ["sb%d" % t], c=S)
         tt(T.y2[:], T.wj[:], T.hd[:, 8 * t:8 * t + 8], A.mult, ["wj", "hd%d" % t], ["y2"], S)
+        if t == RO - 1:
+            tt(T.sn[:, 512:520], T.y2[:], T.md[:, 8 * t:8 * t + 8], A.add, ["y2", "md%d" % t], ["sa%d" % t], S)
+            return
         tt(T.sa[:, o:o + 8], T.y2[:], T.md[:, 8 * t:8 * t + 8], A.add, ["y2", "md%d" % t, "sa"], ["sa%d" % t], S)
         send(dst, T.la[:, o:o + 12], T.sa[:, o:o + 12], ["sa", "sa%d" % t, "sb%d" % t], "ra%d" % t, "la%d" % t)
 
@@ -508,13 +528,14 @@ def rank_program(g, core, T, topo):
         ts(T.bk[:], T.bh[:], 15, 7, A.arith_shift_right, A.bitwise_and, ["bh"], ["bk"])
         ts(T.bi[:], T.bh[:], 16, None, A.bitwise_and, None, ["bh"], ["bi"])
         ts(PW[:, P0], T.bl[:], 8.0 + t, 64.0, A.is_ge, A.mult, ["bl"], ["psW:0"])
-        tt(T.y3[:], PA[:, P2], T.bl[:], A.subtract, ["psA:2", "bl"], ["y3"])
+        act(T.c2[:], T.c1[:], F.Identity, ["c1"], ["c2"], bias=M16)
+        act(T.y3[:], T.c2[:], F.Identity, ["c2"], ["y3"], bias=-M16)
         tt(PW[:, P2], T.bi[:], PA[:, P1], A.min, ["bi", "psA:1"], ["psW:2"])
         tt(PW[:, P1], T.bk[:], PW[:, P0], A.is_le, ["bk", "psW:0"], ["psW:1"])
-        tt(PV[:, P3], T.y3[:], PW[:, P0], A.subtract, ["y3", "psW:0"], ["psV:3"])
-        tt(T.y4[:], T.bg[:], PV[:, P3], A.add, ["bg", "psV:3"], ["y4"])
+        tt(PV[:, P2], T.bk[:], PW[:, P0], A.is_equal, ["bk", "psW:0"], ["psV:2"])
+        tt(T.y4[:], T.y3[:], PA[:, P2], A.add, ["y3", "psA:2"], ["y4"])
         tt(PW[:, P2], T.ap[:], PW[:, P2], A.add, ["ap", "psW:2"], ["psW:2"])
-        tt(T.t2[:], T.y4[:], PW[:, P1], A.mult, ["y4", "psW:1"], ["t2"])
+        tt(T.t2[:], T.y4[:], PV[:, P2], A.mult, ["y4", "psV:2"], ["t2"])
         tt(T.bp[:], T.bg[:], PW[:, P1], A.mult, ["bg", "psW:1"], ["bp"])
         tt(T.smv[:], T.sg[:], PW[:, P1], A.mult, ["sg", "psW:1"], ["smv"])
         tt(PW[:, P3], T.t2[:], PW[:, P2], A.max, ["t2", "psW:2"], ["psW:3"])
@@ -527,17 +548,27 @@ def rank_program(g, core, T, topo):
         tt(PV[:, P2], T.ap[:], PW[:, P0], A.is_lt, ["ap", "psW:0"], ["psV:2"])
         tt(PV[:, P3], T.bp[:], PW[:, P3], A.max, ["bp", "psW:3"], ["psV:3"])
         tt(T.m3[:], T.smv[:], PV[:, P2], A.max, ["smv", "psV:2"], ["m3"])
+        if last:
+            act(T.ac[:], T.bg[:], F.Identity, ["bg"], ["ac"], bias=MB, scale=0.5)
+            act(T.ar[:], T.ac[:], F.Identity, ["ac"], ["ar"], bias=-MB)
+            act(T.av[:], PA[:, P3], F.Identity, ["psA:3"], ["av"], scale=0.5)
+            tt(PW[:, P2], T.ar[:], PV[:, P2], A.mult, ["ar", "psV:2"], ["psW:2"])
+            tt(PW[:, P2], T.av[:], PW[:, P2], A.max, ["av", "psW:2"], ["psW:2"])
         tt(PV[:, P2], T.m3[:], PV[:, P3], A.mult, ["m3", "psV:3"], ["psV:2"])
         tt(T.na[:] if last else T.sn[:, o:o + 128], T.ap[:], PV[:, P2], A.max, ["ap", "psV:2"], ["na" if last else "sn%d" % t])
         if last:
-            to_numbers(T.sn[:, o:o + 128], T.na[:], "c1", 0, ["na"], ["sn%d" % t])
+            tt(T.sn[:, o:o + 128], T.na[:], PW[:, P2], A.subtract, ["na", "psW:2"], ["sn%d" % t])
             to_numbers(T.nb[:, o:o + 128], T.nc[:], "c2", 1, ["nc"], ["nb%d" % t])
-        send(dst, T.ln[:, o:o + 128], T.sn[:, o:o + 128], ["sn%d" % t], "rn%d" % t, "ln%d" % t)
+        n = 136 if last else 128
+        send(dst, T.ln[:, o:o + n], T.sn[:, o:o + n], ["sn%d" % t] + (["sa%d" % t] if last else []), "rn%d" % t, "ln%d" % t)
 
     def back(t):
         o = 128 * t
         tab, off = ("tab", -OFF) if t < RO - 1 else ("fin", 0.0)
-        vc(T.lr[:], T.la[:, 12 * t:12 * t + 8], ["la%d" % t], ["lr"], S)
+        if t < RO - 1:
+            vc(T.lr[:], T.la[:, 12 * t:12 * t + 8], ["la%d" % t], ["lr"], S)
+        else:
+            vc(T.lr[:], T.ln[:, 512:520], ["ln%d" % t], ["lr"], S)
         scatter(tab, T.lr[:], T.ln[:, o:o + 128], ["lr", "ln%d" % t, "~se%d" % (t + 1), tab], off)
         scatter(tab, T.l2[:, 8 * t:8 * t + 8], T.nb[:, o:o + 128], ["l2%d" % t, "nb%d" % t, tab], off)
 

@@ -7,32 +7,37 @@ M16, M32, MB, MN = M0 * 16, M0 * 32, M0 * 2048, M0 * 4096
 OFF = 2.0 ** 23
 SP = 128
 W = SP + 2048
+F2 = 4112
 NE = 8
-VS, VS0 = 56, 56
+CUTS = (0, 56, 96, 128)
 GA = (2, 3)
-HA = (0,)
+TA = (0,)
+LH = 2
+STEPS = ("dd0", "dd1", "dd2", "mt1", "db1", "mt2", "db2", "dd3", "eh3", "in3")
 SEG = [8 * c * (c + 1) + c for c in range(9)]
 SPLIT = (0, 4, 6, 8)
-HOP, FLIGHT, LATE, SLACK, ROOM = 260, 2700, 4000, 40, 100
+HOP, SLACK, ROOM = 260, 40, 100
+MORE = {"lo0": 2000, "la3": 800}
+FLIGHT = {"le": 2200, "lo": 3300, "la": 3600, "ln": 4000, "lh": 4600}
 GATHER, SCATTER = 1.5, 3.8
 LOADED = {"wti": 4200, "kpi": 4200, "ents": 4000, "fw": 7000}
 
 _F, _B, _I, _H, _U = "float32", "bfloat16", "int32", "float16", "uint16"
 SCRATCH = {}
 for _n, _w, _d in [
-        ("ents", 2048, _I), ("tab", W, _F), ("fin", W, _F), ("st", 2048, _F), ("fw", 4112, _B), ("cf", 2048, _F),
-        ("wti", 4, _I), ("kpi", 4, _I), ("pi", 4, _I), ("pj", 4, _I), ("pcol", 16, _F), ("sti", 64, _I), ("stj", 64, _I),
-        ("ones", 128, _B), ("half", 128, _F), ("bd0", 128, _B), ("bd", 128, _B), ("wblk", 128, _B), ("w4", 512, _B),
-        ("ramp", 240, _B), ("r16", 128, _B), ("r4", 128, _B), ("cm", 128, _B), ("idb", 128, _B), ("ka0", 128, _B), ("ka", 128, _B),
+        ("ents", 2048, _I), ("tab", W, _F), ("fin", W, _F), ("st", 2048, _F), ("fw", F2 + 8192, _B), ("cf", 2048, _F),
+        ("wti", 4, _I), ("kpi", 4, _I), ("pj", 8, _I), ("zl", 8, _F), ("pcol", 20, _F), ("sti", 64, _I), ("stj", 64, _I),
+        ("ones", 128, _B), ("half", 128, _F), ("idf", 128, _F), ("bd0", 128, _B), ("bd", 128, _B), ("w4", 512, _B),
+        ("ramp", 240, _B), ("r16", 128, _B), ("r4", 128, _B), ("cm", 128, _B), ("idb", 128, _B), ("ka", 128, _B),
         ("kr", 4, _B), ("kb", 8, _F), ("k16", 4, _F), ("k8", 4, _F), ("kc", 4, _F), ("uc", 32, _B), ("c2k", 128, _B),
-        ("mx", 4, _F), ("zg", 8, _F), ("zp", 8, _B), ("zn", 8, _B), ("zh", 8, _B), ("cb", 8, _H), ("sel", 32, _H), ("cl", 32, _U),
+        ("mx", 4, _F), ("zg", 8, _F), ("zz", 24, _B), ("cb", 8, _H), ("sel", 32, _H), ("cl", 32, _U),
         ("c8", 8, _U), ("pmk", 128, _F), ("ri", 584, _H), ("rn", 584, _H), ("mk", 584, _B), ("spc", 8, _F), ("ls", 8, _F),
         ("hd", 32, _F), ("md", 32, _F), ("rx", 136, _B), ("ramp2", 128, _B), ("am", 8, _F), ("fm", 2048, _B),
         ("i1", 128, _I), ("i3", 128, _I), ("ly", 128, _F), ("lst", 128, _U), ("fg", 2048, _B), ("fs", 2048, _B),
         ("ur", 32, _F), ("uu", 32, _F), ("vq", 128, _F), ("u5", 128, _I), ("u6", 128, _I),
         ("se", 512, _U), ("le", 512, _U), ("so", 512, _F), ("lo", 512, _F), ("sa", 48, _F), ("la", 48, _F),
-        ("sn", 520, _F), ("ln", 520, _F), ("nb", 512, _F), ("lr", 8, _U), ("c1", 128, _F), ("c2", 128, _F), ("c3", 128, _F),
-        ("ox", 512, _F), ("dd", 2048, _B), ("da", 2048, _B), ("db", 2048, _B), ("mt", 2048, _B), ("eh", 512, _H),
+        ("sn", 512, _F), ("ln", 512, _F), ("nb", 512, _F), ("lr", 8, _U), ("c1", 128, _F), ("c2", 128, _F), ("c3", 128, _F),
+        ("ox", 512, _F), ("dd", 2048, _B), ("da", 2048, _B), ("db", 2048, _B), ("mt", 2048, _B), ("eh", 512, _H), ("sh", 2048, _H), ("lh", 2048, _H),
         ("ks", 128, _F), ("kh", 128, _H), ("p8", 8, _F), ("pe", 128, _H), ("pm", 128, _H), ("l1", 8, _U), ("l2", 32, _U),
         ("mn", 8, _F), ("y2", 8, _F), ("wj", 8, _F), ("aa", 8, _F),
         ("ah", 128, _I), ("al", 128, _I), ("ak", 128, _I), ("av", 128, _F), ("ap", 128, _F), ("as2", 128, _F), ("ac", 128, _F),
@@ -43,7 +48,7 @@ for _n, _w, _d in [
 for _n in ("psU", "psK", "psD0", "psD1", "psL", "psA", "psV", "psW"):
     SCRATCH[_n] = ("psum", [128, 512], _F)
 SEMAPHORES = (["sV", "sA", "sP", "sG", "dent", "dsm", "dfe", "dy", "loc"]
-              + ["%s%d" % (k, t) for k in ("ro", "re", "rn", "ra") for t in range(RO)])
+              + ["%s%d" % (k, t) for k in ("ro", "re", "rn", "ra", "rh") for t in range(RO)])
 
 
 def plan(calls):
@@ -195,7 +200,7 @@ def rank_program(g, core, T, topo):
             tot["loc"] = tot.get("loc", 0) + NE
         calls.append(("G", 300, r, ["sent" + s]))
         acts.append(issue)
-        arrives(k, s, NE, (FLIGHT if k[:2] == "le" else LATE) - 2 * HOP, ["sent" + s])
+        arrives(k, s, NE, FLIGHT[k[:2]] - 2 * HOP + MORE.get(k, 0), ["sent" + s])
 
     def ts(out, in0, s1, s2, o0, o1, r, w, c=128):
         if o1 is None:
@@ -218,11 +223,11 @@ def rank_program(g, core, T, topo):
     def ms(ap, x, w, r=(), c=64):
         op("V", lambda: v.memset(ap, x), list(r), w, c)
 
-    def iota(out, pattern, base, cm, w, n, whole=False):
+    def iota(out, pattern, base, cm, w, n, whole=False, r=()):
         if whole:
-            op("G", lambda: g.iota(out, pattern, base, cm), [], w, 160 + 2 * n)
+            op("G", lambda: g.iota(out, pattern, base, cm), r, w, 160 + 2 * n)
         else:
-            op("G", lambda: g.iota(out, pattern, base, cm, allow_small_or_imprecise_dtypes=True), [], w, 160 + 2 * n)
+            op("G", lambda: g.iota(out, pattern, base, cm, allow_small_or_imprecise_dtypes=True), r, w, 160 + 2 * n)
 
     def pick(out, in_, pattern, o, base, cm, r, w):
         op("G", lambda: g.affine_select(out, in_, pattern, o, 0.0, base, cm), r, w, 460)
@@ -250,10 +255,11 @@ def rank_program(g, core, T, topo):
 
     S = 64
     ms(T.ones[:], 1.0, ["ones"])
-    iota(T.pi[:, 0:1], [[1, 1]], 0, 1, ["pi"], 1, True)
-    iota(T.sti[:], [[37, 64]], 0, 0, ["sti"], 64, True)
-    iota(T.ramp[:], [[1, 240]], -112, 0, ["ramp"], 240)
-    pick(T.bd0[:], T.ones[:], [[-16, 8], [0, 16]], A.is_ge, 0, 1, ["ones"], ["bd0"])
+    PI = T.pj[:, 7:8]
+    iota(PI, [[1, 1]], 0, 1, ["pi"], 1, True)
+    iota(T.sti[:], [[37, 64]], 0, 0, ["sti"], 64, True, ["~pi"])
+    iota(T.ramp[:], [[1, 240]], -112, 0, ["ramp"], 240, False, ["~pi"])
+    pick(T.bd0[:], T.ones[:], [[-16, 8], [0, 16]], A.is_ge, 0, 1, ["ones", "~ramp", "~sti"], ["bd0"])
     pick(T.bd[:], T.bd0[:], [[16, 8], [0, 16]], A.is_ge, 15, -1, ["bd0"], ["bd"])
     iota(T.r4[:], [[0, 32], [1, 4]], 0, 0, ["r4"], 128)
     iota(T.r16[:], [[0, 8], [1, 16]], 0, 0, ["r16"], 128)
@@ -267,32 +273,33 @@ def rank_program(g, core, T, topo):
     ms(T.uc[0:64, :], -32.0, ["uc0"])
     ms(T.uc[64:128, :], 1.0 / 128, ["uc"])
     for b in range(4):
-        ms(T.c2k[:, b:128:4], 256.0 if b in HA else 288.0, ["c2k"], ["c2k"])
+        ms(T.c2k[:, b:128:4], 256.0 + 32.0 * (b in TA), ["c2k"], ["c2k"])
     ms(T.half[:], 0.5, ["half"], c=128)
     ms(T.sa[:], 0.0, ["sa"])
-    ts(T.pj[:, 0:1], T.pi[:, 0:1], 15, None, A.bitwise_and, None, ["pi"], ["pj0"], S)
-    ts(T.pj[:, 1:2], T.pi[:, 0:1], 2, 3, A.arith_shift_right, A.bitwise_and, ["pi"], ["pj1"], S)
-    ts(T.pj[:, 2:3], T.pi[:, 0:1], 3, None, A.bitwise_and, None, ["pi"], ["pj2"], S)
-    ts(T.pj[:, 3:4], T.pi[:, 0:1], 4, None, A.arith_shift_right, None, ["pi"], ["pj3"], S)
+    for i, (sh, m) in enumerate(((0, 15), (2, 3), (0, 3), (4, 7), (2, 31), (2, 15), (6, 1))):
+        ts(T.pj[:, i:i + 1], PI, sh, m, A.arith_shift_right, A.bitwise_and, ["pi"], ["pj%d" % i], S)
     ts(T.stj[:], T.sti[:], 63, None, A.bitwise_and, None, ["sti"], ["stj"], S)
-    vc(T.pcol[:, 0:4], T.pj[:, 0:4], ["pj0", "pj1", "pj2", "pj3"], ["pc"], S)
-    vc(col(4), T.pi[:, 0:1], ["pi"], ["pc4"], S)
+    vc(T.pcol[:, 0:8], T.pj[:], ["pi"] + ["pj%d" % i for i in range(7)], ["pc"], S)
+    ts(col(11), col(2), 32.0, col(4), A.mult, A.add, ["pc"], ["pc11"], S)
+    ts(col(12), col(2), 2.0, col(6), A.mult, A.add, ["pc"], ["pc12"], S)
     ts(T.st[:, 0:64], T.stj[:], 4096.0, -2065.0 - OFF, A.mult, A.add, ["stj"], ["st"], S)
     for n in (64, 128, 256):
-        vc(T.st[:, n:2 * n], T.st[:, 0:n], ["st"], ["st"], n)
+        act(T.st[:, n:2 * n], T.st[:, 0:n], F.Copy, ["st"], ["st"], c=n)
     for n in (512, 1024, 1536):
         act(T.st[:, n:n + 512], T.st[:, 0:512], F.Copy, ["st"], ["st%d" % n], c=512)
     ST = ["st", "st512", "st1024", "st1536"]
-    ts(col(5), col(3), 4.0, col(2), A.mult, A.add, ["pc"], ["pc5"], S)
+    ts(col(13), col(3), 4.0, col(2), A.mult, A.add, ["pc"], ["pc13"], S)
+    ts(col(14), col(1), 32.0, None, A.mult, None, ["pc"], ["pc14"], S)
+    ts(T.zl[:], T.ramp[:, 112:120], col(12), None, A.is_equal, None, ["ramp", "pc12"], ["zl"], S)
     ts(col(8), col(0), 0.5, None, A.add, None, ["pc"], ["pc8"], S)
     ts(col(9), col(0), 16.0, float(SP), A.mult, A.add, ["pc"], ["pc9"], S)
     ts(col(10), col(0), -8192.0, 4096.0, A.mult, A.add, ["pc"], ["pc10"], S)
     ts(T.zg[:], T.ramp[:, 112:120], col(3), None, A.is_equal, None, ["ramp", "pc"], ["zg"], S)
     ts(T.mx[:], T.ramp[:, 112:116], col(1), None, A.is_equal, None, ["ramp", "pc"], ["mx"], S)
-    ts(T.cl[:], T.ramp[:, 112:144], 4.0, col(1), A.mult, A.add, ["ramp", "pc"], ["cl"], S)
+    ts(T.cl[:], T.ramp[:, 112:144], col(14), None, A.add, None, ["ramp", "pc14"], ["cl"], S)
     vc(T.c8[:], T.ramp[:, 112:120], ["ramp"], ["c8"], S)
-    ts(T.sel[:], T.ramp[:, 112:144], col(5), 1.0 / 64, A.is_equal, A.mult, ["ramp", "pc5"], ["sel"], S)
-    ts(T.idb[:], R, col(4), None, A.is_equal, None, ["ramp", "pc4"], ["idb"], S)
+    ts(T.sel[:], T.ramp[:, 112:144], col(13), 1.0 / 64, A.is_equal, A.mult, ["ramp", "pc13"], ["sel"], S)
+    ts(T.idb[:], R, col(7), None, A.is_equal, None, ["ramp", "pc"], ["idb"], S)
     ts(T.spc[:], T.ramp[:, 112:120], 16.0, col(8), A.mult, A.add, ["ramp", "pc8"], ["spc"], S)
     ts(T.ls[:], T.ramp[:, 112:120], 256.0, col(9), A.mult, A.add, ["ramp", "pc9"], ["ls"], S)
     tt(T.am[:], T.ls[:], T.spc[:], A.subtract, ["ls", "spc"], ["am"], S)
@@ -300,20 +307,22 @@ def rank_program(g, core, T, topo):
     for t in range(RO):
         ts(T.hd[:, 8 * t:8 * t + 8], T.am[:], t + 0.5, 0.5, A.add, A.mult, ["am"], ["hd%d" % t], S)
         ts(T.md[:, 8 * t:8 * t + 8], T.y2[:], t - 0.5, 0.5, A.add, A.mult, ["y2"], ["md%d" % t], S)
-    ts(T.zp[:], T.zg[:], 512.0, None, A.mult, None, ["zg"], ["zp"], S)
-    ts(T.zn[:], T.zg[:], -512.0, None, A.mult, None, ["zg"], ["zn"], S)
-    ts(T.zh[:], T.zg[:], 256.0, None, A.mult, None, ["zg"], ["zh"], S)
-    vc(T.cb[:], T.zg[:], ["zg"], ["cb"], S)
-    vc(col(6), T.wti[:, 0:1], ["wti"], ["wcol"], S)
-    vc(col(7), T.kpi[:, 0:1], ["kpi"], ["kcol"], S)
-    ts(T.ka0[:], T.r4[:], col(1), None, A.is_equal, None, ["r4", "pc"], ["ka0"], S)
-    ts(T.wblk[:], T.bd[:], col(6), None, A.mult, None, ["bd", "wcol"], ["wblk"], S)
+    Z = {}
+    for i, (k, x) in enumerate((("zp", 512.0), ("zn", -512.0), ("zh", 256.0))):
+        Z[k] = T.zz[:, 8 * i:8 * i + 8]
+        ts(Z[k], T.zg[:], x, None, A.mult, None, ["zg"], [k], S)
+    vc(T.cb[:], T.zl[:], ["zl"], ["cb"], S)
+    vc(col(16), T.wti[:, 0:1], ["wti"], ["wcol"], S)
+    vc(col(17), T.kpi[:, 0:1], ["kpi"], ["kcol"], S)
+    ts(T.bd0[:], T.r4[:], col(1), None, A.is_equal, None, ["r4", "pc"], ["bd0"], S)
     for x in range(4):
-        pick(T.w4[:, 128 * x:128 * x + 128], T.wblk[:], [[0, 8], [1, 4], [0, 4]], A.is_equal, -x, 0, ["wblk"], ["w4%d" % x])
-    ts(T.kr[:], T.ramp[:, 112:116], col(2), col(7), A.is_equal, A.mult, ["ramp", "pc", "kcol"], ["kr"], S)
-    tt(T.ka[:], T.ka0[:], T.bd[:], A.mult, ["ka0", "bd"], ["ka"], 256)
+        w4 = T.w4[:, 128 * x:128 * x + 128]
+        pick(w4, T.bd[:], [[0, 8], [1, 4], [0, 4]], A.is_equal, -x, 0, ["bd", "~r4", "~r16"], ["w4%d" % x])
+        ts(w4, w4, col(16), None, A.mult, None, ["w4%d" % x, "wcol"], ["w4%d" % x], S)
+    ts(T.kr[:], T.ramp[:, 112:116], col(2), col(17), A.is_equal, A.mult, ["ramp", "pc", "kcol"], ["kr"], S)
+    tt(T.ka[:], T.bd0[:], T.bd[:], A.mult, ["bd0", "bd"], ["ka"], 256)
     mm(T.psL[:, 16:20], T.ka[:], T.kr[:], True, True, ["ka", "kr"], ["psL:1"])
-    ts(T.pmk[:], T.r16[:], col(0), 64.0, A.is_equal, A.mult, ["r16", "pc"], ["pmk"])
+    ts(T.pmk[:], T.r16[:], col(5), 64.0, A.is_equal, A.mult, ["r16", "pc"], ["pmk"])
     ts(T.cm[:], T.r16[:], -0.25, 3.75, A.mult, A.add, ["r16"], ["cm"], S)
     vc(T.kb[:, 0:4], T.psL[:, 16:20], ["psL:1"], ["kb"], S)
     ts(T.k16[:], T.psL[:, 16:20], 16.0, 2047.5, A.mult, A.add, ["psL:1"], ["k16"], S)
@@ -326,12 +335,13 @@ def rank_program(g, core, T, topo):
     ts(T.ramp2[:], T.ramp[:, 0:128], 8192.0, None, A.mult, None, ["ramp"], ["ramp2"], S)
     for c in range(8):
         s, w = SEG[c], 16 * c + 16
-        ts(T.ri[:, s:s + w], T.ramp[:, 112:112 + w], col(4), 8192.0, A.is_equal, A.mult, ["ramp", "pc4", "ri0"], ["ri%d" % c], S)
-        ts(T.rn[:, s:s + w + 1], T.rx[:, 128 - w:129], T.zg[:, c:c + 1], None, A.mult, None, ["rx0", "rx", "zg"], ["rn%d" % c], S)
+        ts(T.ri[:, s:s + w], T.ramp[:, 112:112 + w], col(11), 8192.0, A.is_equal, A.mult, ["ramp", "pc11", "ri0"], ["ri%d" % c], S)
+        ts(T.rn[:, s:s + w + 1], T.rx[:, 128 - w:129], T.zl[:, c:c + 1], None, A.mult, None, ["rx0", "rx", "zl"], ["rn%d" % c], S)
         ts(T.mk[:, s:s + w], T.ramp2[:, 128 - w:128], col(10), T.spc[:, c:c + 1], A.add, A.max,
            ["ramp2", "pc10", "spc", "mk0"], ["mk%d" % c], S)
 
-    PA, PV, PW = T.psA, T.psV, T.psW
+    ts(T.idf[:], R, col(7), None, A.is_equal, None, ["ramp", "pc"], ["idf"])
+    PA, PV, PW, PL = T.psA, T.psV, T.psW, T.psL
     P0, P1, P2, P3 = [slice(128 * i, 128 * i + 128) for i in range(4)]
     TAB = T.tab[:, SP:W]
     CZ = -(MB + OFF - 2048.0)
@@ -354,25 +364,44 @@ def rank_program(g, core, T, topo):
     def lane_list(t, dst):
         o = 128 * t
         src, sk = (T.so[:, 0:128], "so0") if t == 0 else (T.tab[:, SP + t:W:16], "tab")
-        act(PA[:, P0], src, F.Identity, [sk], ["psA:0"], bias=-2048.75 / 16, scale=2.0 ** -16)
         if t:
             act(T.so[:, o:o + 128], src, F.Copy, [sk], ["so%d" % t])
         send(dst, T.lo[:, o:o + 128], T.so[:, o:o + 128], ["so%d" % t], "ro%d" % t, "lo%d" % t)
-        ts(T.i1[:], src, -2033.0, None, A.add, None, [sk], ["i1"])
+        if t:
+            ts(T.i1[:], src, -2033.0, None, A.add, None, [sk], ["i1"])
+            ts(T.i3[:], T.i1[:], 16 - 4096, None, A.bitwise_and, None, ["i1"], ["i3"])
+            ts(T.lst[:], T.i3[:], 2.0 ** -11, 4096.496, A.mult, A.add, ["i3"], ["lst"])
+            return
+        e = T.ents[:, 0:2048:16]
+        ts(T.i1[:], e, 15.0, None, A.add, None, ["ents"], ["i1"])
+        ts(PA[:, P0], e, 2.0 ** -15, -4096.5 / 16, A.mult, A.add, ["ents"], ["psA:0"])
         ts(T.i3[:], T.i1[:], 16, None, A.bitwise_and, None, ["i1"], ["i3"])
         tt(T.ly[:], T.i3[:], PA[:, P0], A.mult, ["i3", "psA:0"], ["ly"])
         ts(T.lst[:], T.ly[:], M0 + 4096.0, -M0, A.add, A.add, ["ly"], ["lst"])
 
-    def features(cuts):
+    def spread_features():
+        for i in range(16):
+            s = F2 + 512 * i
+            iota(T.fw[:, s:s + 512:2], [[0, 256]], 0, 0, ["f2z%d" % i], 256)
+            act(T.fw[:, s + 1:s + 512:2], T.fw[:, 256 * i:256 * i + 256], F.Copy, ["fw", "~sentre0"], ["f2%d" % i], c=256)
+
+    def features(t, cuts):
+        win, wk = T.fw[:, 0:F2], ["fw", "fwz"]
+        if t:
+            win, wk = T.fw[:, F2:F2 + 8192], ["f2%s%d" % (k, i) for k in ("", "z") for i in range(16)]
         for i in range(len(cuts) - 1):
             n0, n1 = cuts[i:i + 2]
             c = slice(16 * n0, 16 * n1)
-            r = ["lst", "fw", "fwz"]
+            r = ["lst"] + wk + ["~fg%d" % (i - 1)] * (i > 1)
             if i:
-                act(T.fg[:, c], T.fw[:].indirect(T.lst[:, n0:n1]), F.Copy, r, ["fg%d" % i], c=gc(16 * (n1 - n0)) - 64)
+                act(T.fg[:, c], win.indirect(T.lst[:, n0:n1]), F.Copy, r, ["fg%d" % i], c=gc(16 * (n1 - n0)) - 64)
             else:
-                vc(T.fg[:, c], T.fw[:].indirect(T.lst[:, n0:n1]), r, ["fg%d" % i], gc(16 * (n1 - n0)))
-            scan(T.fs[:, c], T.fm[:, c], T.fg[:, c], ["fm", "fm512", "fm1024", "fm1536", "fg%d" % i], ["fs%d" % i], 8 * (n1 - n0))
+                vc(T.fg[:, c], win.indirect(T.lst[:, n0:n1]), r, ["fg%d" % i], gc(16 * (n1 - n0)))
+        prev = "~fg0"
+        for i in [1, 0] + list(range(2, len(cuts) - 1)):
+            c = slice(16 * cuts[i], 16 * cuts[i + 1])
+            scan(T.fs[:, c], T.fm[:, c], T.fg[:, c], ["fm", "fm512", "fm1024", "fm1536", "fg%d" % i, prev], ["fs%d" % i], (c.stop - c.start) // 2)
+            prev = "~fs%d" % i
         return ["fs%d" % i for i in range(len(cuts) - 1)]
 
     def cand(t, dst, fs):
@@ -380,7 +409,8 @@ def rank_program(g, core, T, topo):
         U = T.psU[:, 0:32]
         mm(U, T.ones[:], T.uc[:], True, False, ["ones", "uc0", "uc"], ["psU"])
         for x in range(4):
-            mm(U, T.w4[:, 128 * x:128 * x + 128], T.fs[:, 16 * x + 15:2048:64], False, x == 3, ["w4%d" % x] + fs, ["psU"])
+            mm(U, T.w4[:, 128 * x:128 * x + 128], T.fs[:, 512 * x + 15:512 * x + 512:16], False, x == 3,
+               ["w4%d" % x] + [k for i, k in enumerate(fs) if CUTS[i] < 32 * x + 32 and CUTS[i + 1] > 32 * x], ["psU"])
         kc, kk = T.k8, "k8"
         if t:
             kc, kk = T.kc, "kc"
@@ -397,6 +427,12 @@ def rank_program(g, core, T, topo):
         ts(T.u6[:], T.u5[:], 2047, None, A.bitwise_and, None, ["u5%d" % b for b in range(4)], ["u6"])
         vc(T.se[:, o:o + 128], T.u6[:], ["u6"], ["se%d" % t])
         send(dst, T.le[:, o:o + 128], T.se[:, o:o + 128], ["se%d" % t], "re%d" % t, "le%d" % t)
+        n = 128 * LH
+        for x in range(4):
+            ts(T.sh[:, n * t + x:n * t + n:4], T.se[:, o:o + n // 4], -1023.5, T.mx[:, x:x + 1], A.add, A.mult,
+               ["se%d" % t, "mx"], ["sh%d%d" % (t, x)], S)
+        send(dst, T.lh[:, n * t:n * t + n], T.sh[:, n * t:n * t + n], ["sh%d%d" % (t, x) for x in range(4)] + ["~sentre%d" % t],
+             "rh%d" % t, "lh%d" % t)
 
     def scatter(tab, lists, vals, r, off):
         ts(T[tab][:].indirect(lists), vals, 1.0, off, A.mult, A.add, r, [tab], int(60 + SCATTER * 128))
@@ -421,17 +457,20 @@ def rank_program(g, core, T, topo):
         tt(T.ap[:], T.av[:], PA[:, P0], A.mult, ["av", "psA:0"], ["ap"])
         act(T.ac[:], T.ap[:], F.Identity, ["ap"], ["ac"], bias=MN)
         act(T.ar[:], T.as2[:], F.Relu, ["as2"], ["ar"], bias=80 * 2.0 ** 25, scale=-2.0 ** 25)
-        act(PA[:, P1], T.as2[:], F.Relu, ["as2"], ["psA:1"], bias=12.0 + t, scale=-1.0)
-        act(PA[:, P3], T.ac[:], F.Identity, ["ac"], ["psA:3"], bias=-MN)
-        act(PA[:, P2], T.ar[:], F.Identity, ["ar"], ["psA:2"], bias=OFF + 13.0 + t, scale=-1.0)
+        act(PL[:, P1], T.as2[:], F.Relu, ["as2"], ["psL:a"], bias=12.0 + t, scale=-1.0)
+        act(T.di[:], T.ac[:], F.Identity, ["ac"], ["di"], bias=MN, scale=-1.0)
+        mm(PA[:, P3], T.idf[:], T.di[:], True, False, ["idf", "di"], ["psA:3"], 512)
+        act(PL[:, P2], T.ar[:], F.Identity, ["ar"], ["psL:b"], bias=OFF + 13.0 + t, scale=-1.0)
 
-    KEYS = ["psK:%s%d%d" % (k, i, x) for k in ("mt", "db") for i in range(4) for x in range(4)] + ["psK:e%d" % i for i in range(4)]
+    KEYS = (["psK:%s%d%d" % (k, i, x) for i in range(4) for k in ("mt", "db")[:1 if i in TA else 2] for x in range(4)]
+            + ["psK:e%d" % i for i in range(4)])
 
     def score(t):
         o = 128 * t
         K = T.psK
         lk = "le%d" % t
         left = [len(KEYS)]
+        EH = ["eh%d" % x for x in range(4)]
 
         def add(out, l, rh, r, k):
             def fn():
@@ -442,31 +481,47 @@ def rank_program(g, core, T, topo):
         mm(K[:, P0], T.ones[:], T.cm[:], True, False, ["ones", "cm"], ["psK"], 128)
         mm(K[:, P0], T.ones[:], T.c2k[:], False, False, ["ones", "c2k"], ["psK"] + KEYS, 128)
 
-        def sums(i, tile, k, z):
+        def sums(i, tile, k, z, r=None):
             for x in range(4):
-                add(K[:, 4 * x + i:128:16], tile[:, 512 * i + x:512 * i + 512:4], T[z][:], [k, z], "psK:%s%d" % (k, x))
+                add(K[:, 4 * x + i:128:16], tile[:, 512 * i + x:512 * i + 512:4], Z[z], (r or [k]) + [z], "psK:%s%d" % (k, x))
 
-        for i in range(4):
+        for i in GA:
+            act(T.cf[:, 512 * i:512 * i + 512], TAB.indirect(T.le[:, o + 32 * i:o + 32 * i + 32]), F.Copy,
+                ["tab", lk, "~cf%d" % (2 * i - 2)], ["cf%d" % (2 * i), "cf%d" % (2 * i + 1)], c=gc(512) - 64)
+        tests = {"mt": (MN + 4096.0, "zp"), "db": (M16, "zn")}
+        prev = "~"
+        for step in STEPS:
+            k, i = step[:2], int(step[2])
             c = slice(512 * i, 512 * i + 512)
-            cands = TAB.indirect(T.le[:, o + 32 * i:o + 32 * i + 32])
-            turn = ["~dd%d" % (i - 1), "~mt%d" % (i - 2)] + ["~eh%d" % x for x in range(4 if i == 2 else 0)]
-            if i in GA:
-                ck = ["cf%d" % (2 * i), "cf%d" % (2 * i + 1)]
-                act(T.cf[:, c], cands, F.Copy, ["tab", lk] + ["~cf%d" % (2 * j) for j in GA if j < i], ck, c=gc(512) - 64)
-                tt(T.dd[:, c], T.cf[:, c], PW[:], A.subtract, ck + ["psW"] + turn, ["dd%d" % i], 512)
+            if k == "dd" and i in GA:
+                tt(T.dd[:, c], T.cf[:, c], PW[:], A.subtract, ["cf%d" % (2 * i), "cf%d" % (2 * i + 1), "psW", prev], [step], 512)
+            elif k == "dd":
+                tt(T.dd[:, c], TAB.indirect(T.le[:, o + 32 * i:o + 32 * i + 32]), T.ox[:], A.subtract, ["tab", lk, "ox", prev], [step], gc(512))
+            elif k in tests:
+                ts(T[k][:, c], T.dd[:, c], tests[k][0], tests[k][0], A.add, A.is_equal, ["dd%d" % i, prev], [step], 256)
+                sums(i, T[k], step, tests[k][1])
+            elif k == "eh":
+                for x in range(4):
+                    ts(T.eh[:, 128 * LH + x:512:4], T.le[:, o + 32 * LH:o + 128], -1023.5, T.mx[:, x:x + 1], A.add, A.mult,
+                       [lk, "mx", prev], [EH[x]], S)
+                    prev = "~" + EH[x]
+                for b in range(4):
+                    src, sk = (T.lh[:, 128 * (LH * t + b):128 * (LH * t + b + 1)], ["lh%d" % t]) if b < LH else (T.eh[:, 128 * b:128 * b + 128], EH)
+                    add(K[:, b:128:4], src, T.sel[:], ["sel"] + sk, "psK:e%d" % b)
             else:
-                tt(T.dd[:, c], cands, T.ox[:], A.subtract, ["tab", lk, "ox"] + turn, ["dd%d" % i], gc(512))
-            if i in HA:
-                act(T.da[:, c], T.dd[:, c], F.Abs, ["dd%d" % i], ["da%d" % i], c=512)
-                act(T.db[:, c], T.da[:, c], F.Sign, ["da%d" % i], ["db%d" % i], bias=-8.25, c=512)
-            else:
-                ts(T.db[:, c], T.dd[:, c], M16, M16, A.add, A.is_equal, ["dd%d" % i], ["db%d" % i], 256)
-            ts(T.mt[:, c], T.dd[:, c], MN + 4096.0, MN + 4096.0, A.add, A.is_equal, ["dd%d" % i], ["mt%d" % i], 256)
-            sums(i, T.mt, "mt%d" % i, "zp")
-            sums(i, T.db, "db%d" % i, "zh" if i in HA else "zn")
-            for x in range(4 if i == 0 else 0):
-                ts(T.eh[:, x:512:4], T.le[:, o:o + 128], -1023.5, T.mx[:, x:x + 1], A.add, A.mult, [lk, "mx", "~dd0"], ["eh%d" % x], S)
-            add(K[:, i:128:4], T.eh[:, 128 * i:128 * i + 128], T.sel[:], ["sel"] + ["eh%d" % x for x in range(4)], "psK:e%d" % i)
+                for x in range(4):
+                    c4 = slice(c.start + x, c.stop, 4)
+                    for k, (m, z) in tests.items():
+                        ts(T[k][:, c4], T.dd[:, c4], m, m, A.add, A.is_equal, ["dd%d" % i, prev], ["%s%d%d" % (k, i, x)], S)
+                        add(K[:, 4 * x + i:128:16], T[k][:, c4], Z[z], ["%s%d%d" % (k, i, x), z], "psK:%s%d%d" % (k, i, x))
+            prev = "~" + step
+            if k == "dd" and i in TA:
+                for h in (2 * i, 2 * i + 1):
+                    c2 = slice(256 * h, 256 * h + 256)
+                    act(T.da[:, c2], T.dd[:, c2], F.Abs, [step] + ["~cf%d" % (2 * j) for j in GA], ["da%d" % h], c=256)
+                    act(T.cf[:, c2], T.da[:, c2], F.Abs, ["da%d" % h], ["cf%d" % h], bias=-1026.25, c=256)
+                    act(T.mt[:, c2], T.cf[:, c2], F.Sign, ["cf%d" % h], ["ma%d" % h], bias=1018.0, scale=-1.0, c=256)
+                sums(i, T.mt, "mt%d" % i, "zh", ["ma%d" % h for h in (2 * i, 2 * i + 1)])
 
     DB = [(k, SPLIT[i], SPLIT[i + 1]) for i, k in enumerate(("psD0", "psD1", "psU")[:len(SPLIT) - 1])]
 
@@ -507,22 +562,14 @@ def rank_program(g, core, T, topo):
             mm(T.psL[:, 32:33], T.half[:], T.aa[:, 0:1], True, True, ["half", "aa0"], ["psL:2"], 256)
             act(T.sa[:, o + 8:o + 9], T.psL[:, 32:33], F.Copy, ["psL:2", "sa"], ["sb%d" % t], c=S)
         tt(T.y2[:], T.wj[:], T.hd[:, 8 * t:8 * t + 8], A.mult, ["wj", "hd%d" % t], ["y2"], S)
-        if t == RO - 1:
-            tt(T.sn[:, 512:520], T.y2[:], T.md[:, 8 * t:8 * t + 8], A.add, ["y2", "md%d" % t], ["sa%d" % t], S)
-            return
         tt(T.sa[:, o:o + 8], T.y2[:], T.md[:, 8 * t:8 * t + 8], A.add, ["y2", "md%d" % t, "sa"], ["sa%d" % t], S)
         send(dst, T.la[:, o:o + 12], T.sa[:, o:o + 12], ["sa", "sa%d" % t, "sb%d" % t], "ra%d" % t, "la%d" % t)
-
-    def to_numbers(out, y, e, p, r, w):
-        ts(T[e][:], y, 0.5, MB, A.mult, A.add, r, [e])
-        ts(PW[:, 128 * p:128 * p + 128], T[e][:], -MB, None, A.add, None, [e], ["psW:%d" % p])
-        tt(out, y, PW[:, 128 * p:128 * p + 128], A.subtract, r + ["psW:%d" % p], w)
 
     def meet(t, dst):
         o = 128 * t
         last = t == RO - 1
-        tt(T.di[:], T.bg[:], PA[:, P3], A.subtract, ["bg", "psA:3"], ["di"])
-        act(T.dq[:], T.di[:], F.Square, ["di"], ["dq"], scale=1.0 / 2048)
+        mm(PA[:, P3], T.idf[:], T.bg[:], False, True, ["idf", "bg", "~psU:0"], ["psA:3"], 512)
+        act(T.dq[:], PA[:, P3], F.Square, ["psA:3"], ["dq"], bias=0.5, scale=1.0 / 2048)
         act(T.sg[:], T.dq[:], F.Sign, ["dq"], ["sg"], bias=1.0, scale=-1.0)
         ts(T.bl[:], T.bh[:], 31, None, A.bitwise_and, None, ["bh"], ["bl"])
         ts(T.bk[:], T.bh[:], 15, 7, A.arith_shift_right, A.bitwise_and, ["bh"], ["bk"])
@@ -530,45 +577,47 @@ def rank_program(g, core, T, topo):
         ts(PW[:, P0], T.bl[:], 8.0 + t, 64.0, A.is_ge, A.mult, ["bl"], ["psW:0"])
         act(T.c2[:], T.c1[:], F.Identity, ["c1"], ["c2"], bias=M16)
         act(T.y3[:], T.c2[:], F.Identity, ["c2"], ["y3"], bias=-M16)
-        tt(PW[:, P2], T.bi[:], PA[:, P1], A.min, ["bi", "psA:1"], ["psW:2"])
+        if last:
+            tt(PL[:, P1], T.av[:], PL[:, P1], A.mult, ["av", "psL:a"], ["psL:a"])
+        tt(PW[:, P2], T.bi[:], PL[:, P1], A.min, ["bi", "psL:a"], ["psW:2"])
         tt(PW[:, P1], T.bk[:], PW[:, P0], A.is_le, ["bk", "psW:0"], ["psW:1"])
-        tt(PV[:, P2], T.bk[:], PW[:, P0], A.is_equal, ["bk", "psW:0"], ["psV:2"])
-        tt(T.y4[:], T.y3[:], PA[:, P2], A.add, ["y3", "psA:2"], ["y4"])
-        tt(PW[:, P2], T.ap[:], PW[:, P2], A.add, ["ap", "psW:2"], ["psW:2"])
-        tt(T.t2[:], T.y4[:], PV[:, P2], A.mult, ["y4", "psV:2"], ["t2"])
-        tt(T.bp[:], T.bg[:], PW[:, P1], A.mult, ["bg", "psW:1"], ["bp"])
+        tt(PW[:, P3], T.bk[:], PW[:, P0], A.is_equal, ["bk", "psW:0"], ["psW:3"])
+        lane, site, wake = "ap", "bg", (PL[:, P2], "psL:b")
+        if last:
+            lane, site, wake = "na", "nc", (PV[:, P3], "psV:3")
+            act(T.ly[:], T.di[:], F.Identity, ["di"], ["ly"], scale=0.5)
+            tt(T.na[:], T.ap[:], T.ly[:], A.add, ["ap", "ly"], ["na"], 256)
+            tt(PV[:, P3], T.ly[:], PL[:, P2], A.add, ["ly", "psL:b"], ["psV:3"])
+            act(T.ac[:], T.bg[:], F.Identity, ["bg"], ["ac"], bias=MB, scale=0.5)
+            act(PA[:, P1], T.ac[:], F.Identity, ["ac"], ["psA:1"], bias=-MB)
+            tt(T.nc[:], T.bg[:], PA[:, P1], A.subtract, ["bg", "psA:1"], ["nc"])
+        tt(T.y4[:], T.y3[:], wake[0], A.add, ["y3", wake[1]], ["y4"])
+        tt(PW[:, P2], T[lane][:], PW[:, P2], A.add, [lane, "psW:2"], ["psW:2"])
+        tt(T.t2[:], T.y4[:], PW[:, P3], A.mult, ["y4", "psW:3"], ["t2"])
+        tt(T.bp[:], T[site][:], PW[:, P1], A.mult, [site, "psW:1"], ["bp"])
         tt(T.smv[:], T.sg[:], PW[:, P1], A.mult, ["sg", "psW:1"], ["smv"])
         tt(PW[:, P3], T.t2[:], PW[:, P2], A.max, ["t2", "psW:2"], ["psW:3"])
-        tt(PV[:, P1], T.bp[:], PV[:, P0], A.is_lt, ["bp", "psV:0"], ["psV:1"])
+        if last:
+            ts(PL[:, P3], T.al[:], 8.0 + t, None, A.is_ge, None, ["al"], ["psL:c"])
+            tt(PV[:, P1], T.bp[:], PL[:, P3], A.is_lt, ["bp", "psL:c"], ["psV:1"])
+        else:
+            tt(PV[:, P1], T.bp[:], PV[:, P0], A.is_lt, ["bp", "psV:0"], ["psV:1"])
         tt(T.m2[:], T.smv[:], PV[:, P1], A.max, ["smv", "psV:1"], ["m2"])
         tt(PV[:, P1], T.m2[:], PW[:, P3], A.mult, ["m2", "psW:3"], ["psV:1"])
-        tt(T.nc[:] if last else T.nb[:, o:o + 128], T.bp[:], PV[:, P1], A.max, ["bp", "psV:1"], ["nc" if last else "nb%d" % t])
+        tt(T.nb[:, o:o + 128], T.bp[:], PV[:, P1], A.max, ["bp", "psV:1"], ["nb%d" % t])
         if not last:
             scatter("tab", T.l2[:, 8 * t:8 * t + 8], T.nb[:, o:o + 128], ["l2%d" % t, "nb%d" % t], -OFF)
         tt(PV[:, P2], T.ap[:], PW[:, P0], A.is_lt, ["ap", "psW:0"], ["psV:2"])
         tt(PV[:, P3], T.bp[:], PW[:, P3], A.max, ["bp", "psW:3"], ["psV:3"])
         tt(T.m3[:], T.smv[:], PV[:, P2], A.max, ["smv", "psV:2"], ["m3"])
-        if last:
-            act(T.ac[:], T.bg[:], F.Identity, ["bg"], ["ac"], bias=MB, scale=0.5)
-            act(T.ar[:], T.ac[:], F.Identity, ["ac"], ["ar"], bias=-MB)
-            act(T.av[:], PA[:, P3], F.Identity, ["psA:3"], ["av"], scale=0.5)
-            tt(PW[:, P2], T.ar[:], PV[:, P2], A.mult, ["ar", "psV:2"], ["psW:2"])
-            tt(PW[:, P2], T.av[:], PW[:, P2], A.max, ["av", "psW:2"], ["psW:2"])
         tt(PV[:, P2], T.m3[:], PV[:, P3], A.mult, ["m3", "psV:3"], ["psV:2"])
-        tt(T.na[:] if last else T.sn[:, o:o + 128], T.ap[:], PV[:, P2], A.max, ["ap", "psV:2"], ["na" if last else "sn%d" % t])
-        if last:
-            tt(T.sn[:, o:o + 128], T.na[:], PW[:, P2], A.subtract, ["na", "psW:2"], ["sn%d" % t])
-            to_numbers(T.nb[:, o:o + 128], T.nc[:], "c2", 1, ["nc"], ["nb%d" % t])
-        n = 136 if last else 128
-        send(dst, T.ln[:, o:o + n], T.sn[:, o:o + n], ["sn%d" % t] + (["sa%d" % t] if last else []), "rn%d" % t, "ln%d" % t)
+        tt(T.sn[:, o:o + 128], T[lane][:], PV[:, P2], A.max, [lane, "psV:2"], ["sn%d" % t])
+        send(dst, T.ln[:, o:o + 128], T.sn[:, o:o + 128], ["sn%d" % t], "rn%d" % t, "ln%d" % t)
 
     def back(t):
         o = 128 * t
         tab, off = ("tab", -OFF) if t < RO - 1 else ("fin", 0.0)
-        if t < RO - 1:
-            vc(T.lr[:], T.la[:, 12 * t:12 * t + 8], ["la%d" % t], ["lr"], S)
-        else:
-            vc(T.lr[:], T.ln[:, 512:520], ["ln%d" % t], ["lr"], S)
+        vc(T.lr[:], T.la[:, 12 * t:12 * t + 8], ["la%d" % t], ["lr"], S)
         scatter(tab, T.lr[:], T.ln[:, o:o + 128], ["lr", "ln%d" % t, "~se%d" % (t + 1), tab], off)
         scatter(tab, T.l2[:, 8 * t:8 * t + 8], T.nb[:, o:o + 128], ["l2%d" % t, "nb%d" % t, tab], off)
 
@@ -588,8 +637,9 @@ def rank_program(g, core, T, topo):
         callee = T.cores[(rank + 1 + t % 7) % N]
         caller = T.cores[(rank - 1 - t % 7) % N]
         lane_list(t, callee)
-        vs = VS if t else VS0
-        cand(t, callee, features([0, vs, (vs + 128) // 4 * 2, 128]))
+        cand(t, callee, features(t, CUTS))
+        if t == 0:
+            spread_features()
         expand(t)
         own_side(t)
         if t:

@@ -5,20 +5,23 @@ RO = 4
 M0 = 1.5 * 2.0 ** 23
 M16, M32, MB, MN = M0 * 16, M0 * 32, M0 * 2048, M0 * 4096
 OFF = 2.0 ** 23
-SP = 128
+SP = 256
 W = SP + 2048
 F2 = 4112
 NE = 8
 CUTS = (0, 56, 96, 128)
 GA = (2, 3)
 TA = (0,)
-LH = 2
-STEPS = ("dd0", "dd1", "dd2", "mt1", "db1", "mt2", "db2", "dd3", "eh3", "in3")
+AM = 6
+SCALAR = ("bz", "xa2", "dq", "xb6", "xb7")
+EARLY = 2
+STEPS = ("dd0", "eh0", "dd1", "dd2", "mt1", "db1", "mt2", "db2", "in3")
+LAST = (0, 1, 2, 4, 3, 5, 6, 7)
 SEG = [8 * c * (c + 1) + c for c in range(9)]
 SPLIT = (0, 4, 6, 8)
 HOP, SLACK, ROOM = 260, 40, 100
 MORE = {"lo0": 2000, "la3": 800}
-FLIGHT = {"le": 2200, "lo": 3300, "la": 3600, "ln": 4000, "lh": 4600}
+FLIGHT = {"lu": 2100, "lo": 3300, "la": 3600, "ln": 4000}
 GATHER, SCATTER = 1.5, 3.8
 LOADED = {"wti": 4200, "kpi": 4200, "ents": 4000, "fw": 7000}
 
@@ -29,26 +32,26 @@ for _n, _w, _d in [
         ("wti", 4, _I), ("kpi", 4, _I), ("pj", 8, _I), ("zl", 8, _F), ("pcol", 20, _F), ("sti", 64, _I), ("stj", 64, _I),
         ("ones", 128, _B), ("half", 128, _F), ("idf", 128, _F), ("bd0", 128, _B), ("bd", 128, _B), ("w4", 512, _B),
         ("ramp", 240, _B), ("r16", 128, _B), ("r4", 128, _B), ("cm", 128, _B), ("idb", 128, _B), ("ka", 128, _B),
-        ("kr", 4, _B), ("kb", 8, _F), ("k16", 4, _F), ("k8", 4, _F), ("kc", 4, _F), ("uc", 32, _B), ("c2k", 128, _B),
-        ("mx", 4, _F), ("zg", 8, _F), ("zz", 24, _B), ("cb", 8, _H), ("sel", 32, _H), ("cl", 32, _U),
-        ("c8", 8, _U), ("pmk", 128, _F), ("ri", 584, _H), ("rn", 584, _H), ("mk", 584, _B), ("spc", 8, _F), ("ls", 8, _F),
-        ("hd", 32, _F), ("md", 32, _F), ("rx", 136, _B), ("ramp2", 128, _B), ("am", 8, _F), ("fm", 2048, _B),
+        ("kr", 4, _B), ("k8", 4, _F), ("uc", 32, _B), ("c2k", 128, _B),
+        ("mx", 4, _B), ("zg", 8, _F), ("zz", 24, _B), ("cb", 8, _H), ("sel", 32, _H), ("cl", 32, _U),
+        ("c8", 8, _U), ("pmk", 128, _F), ("ri", 128, _H), ("rn", 584, _H), ("mk", 584, _B), ("spc", 8, _F), ("ls", 8, _F),
+        ("rx", 136, _B), ("ramp2", 128, _B), ("fm", 2048, _B),
         ("i1", 128, _I), ("i3", 128, _I), ("ly", 128, _F), ("lst", 128, _U), ("fg", 2048, _B), ("fs", 2048, _B),
-        ("ur", 32, _F), ("uu", 32, _F), ("vq", 128, _F), ("u5", 128, _I), ("u6", 128, _I),
-        ("se", 512, _U), ("le", 512, _U), ("so", 512, _F), ("lo", 512, _F), ("sa", 48, _F), ("la", 48, _F),
-        ("sn", 512, _F), ("ln", 512, _F), ("nb", 512, _F), ("lr", 8, _U), ("c1", 128, _F), ("c2", 128, _F), ("c3", 128, _F),
-        ("ox", 512, _F), ("dd", 2048, _B), ("da", 2048, _B), ("db", 2048, _B), ("mt", 2048, _B), ("eh", 512, _H), ("sh", 2048, _H), ("lh", 2048, _H),
+        ("ur", 32, _F), ("vq", 32, _F), ("u5", 128, _I), ("u6", 128, _I),
+        ("su", 160, _F), ("lu", 160, _F), ("le", 128, _U), ("lw", 1152, _F), ("lo", 512, _F), ("sa", 48, _F), ("la", 48, _F),
+        ("sn", 512, _F), ("nb", 128, _F), ("nr", 128, _F), ("sg", 128, _F), ("lr", 8, _U), ("c1", 128, _F), ("c2", 128, _F), ("c3", 128, _F),
+        ("ox", 512, _F), ("dd", 2048, _B), ("da", 2048, _B), ("db", 2048, _B), ("mt", 2048, _B), ("eh", 512, _H),
         ("ks", 128, _F), ("kh", 128, _H), ("p8", 8, _F), ("pe", 128, _H), ("pm", 128, _H), ("l1", 8, _U), ("l2", 32, _U),
-        ("mn", 8, _F), ("y2", 8, _F), ("wj", 8, _F), ("aa", 8, _F),
+        ("mn", 8, _F), ("xa", 584, _F), ("xb", 584, _F), ("xc", 16, _F), ("bj", 128, _I), ("wj", 8, _F), ("aa", 8, _F),
         ("ah", 128, _I), ("al", 128, _I), ("ak", 128, _I), ("av", 128, _F), ("ap", 128, _F), ("as2", 128, _F), ("ac", 128, _F),
-        ("ar", 128, _F), ("bg", 128, _F), ("bh", 128, _I), ("bl", 128, _I), ("bk", 128, _I), ("bi", 128, _I), ("bp", 128, _F),
-        ("di", 128, _F), ("dq", 128, _F), ("sg", 128, _F), ("t2", 128, _F), ("m2", 128, _F), ("m3", 128, _F), ("na", 128, _F),
-        ("nc", 128, _F), ("y3", 128, _F), ("y4", 128, _F), ("smv", 128, _F)]:
+        ("ao", 128, _F), ("bg", 128, _F), ("bs", 128, _F), ("bh", 128, _I), ("bl", 128, _I), ("bk", 128, _I), ("bi", 128, _I),
+        ("idn", 128, _F), ("ay", 128, _F), ("az", 128, _F), ("bz", 128, _F), ("bn", 128, _F), ("wq", 128, _F), ("dq", 128, _F),
+        ("dz", 128, _F), ("f2", 128, _F), ("t2", 128, _F), ("m3", 128, _F), ("na", 128, _F), ("r0", 128, _F), ("sx", 128, _F)]:
     SCRATCH[_n] = ("sbuf", [128, _w], _d)
 for _n in ("psU", "psK", "psD0", "psD1", "psL", "psA", "psV", "psW"):
     SCRATCH[_n] = ("psum", [128, 512], _F)
 SEMAPHORES = (["sV", "sA", "sP", "sG", "dent", "dsm", "dfe", "dy", "loc"]
-              + ["%s%d" % (k, t) for k in ("ro", "re", "rn", "ra", "rh") for t in range(RO)])
+              + ["%s%d" % (k, t) for k in ("ro", "re", "rn", "ra") for t in range(RO)])
 
 
 def plan(calls):
@@ -93,8 +96,9 @@ def plan(calls):
         mine = [j for j in ready if calls[j][0] == q]
         if q != "R":
             last = max(at[o] + way[o] for o in ready) + SLACK
+            due = {o: max([0] + [end[j] + h for j, h in pre[o].items()]) for o in mine}
             fits = [j for j in mine
-                    if all(way[o] <= way[j] or at[j] + calls[j][1] <= max(at[o], min(at[o] + ROOM, last - way[o])) for o in mine)]
+                    if all(way[o] <= way[j] or at[j] + calls[j][1] <= max(at[o], min(due[o] + ROOM, last - way[o])) for o in mine)]
             i = min(fits, key=lambda j: (at[j], -way[j]))
         ready.remove(i)
         end[i] = at[i] + calls[i][1]
@@ -274,7 +278,7 @@ def rank_program(g, core, T, topo):
     ms(T.uc[64:128, :], 1.0 / 128, ["uc"])
     for b in range(4):
         ms(T.c2k[:, b:128:4], 256.0 + 32.0 * (b in TA), ["c2k"], ["c2k"])
-    ms(T.half[:], 0.5, ["half"], c=128)
+    ms(T.half[:], 1.0, ["half"], c=128)
     ms(T.sa[:], 0.0, ["sa"])
     for i, (sh, m) in enumerate(((0, 15), (2, 3), (0, 3), (4, 7), (2, 31), (2, 15), (6, 1))):
         ts(T.pj[:, i:i + 1], PI, sh, m, A.arith_shift_right, A.bitwise_and, ["pi"], ["pj%d" % i], S)
@@ -282,7 +286,7 @@ def rank_program(g, core, T, topo):
     vc(T.pcol[:, 0:8], T.pj[:], ["pi"] + ["pj%d" % i for i in range(7)], ["pc"], S)
     ts(col(11), col(2), 32.0, col(4), A.mult, A.add, ["pc"], ["pc11"], S)
     ts(col(12), col(2), 2.0, col(6), A.mult, A.add, ["pc"], ["pc12"], S)
-    ts(T.st[:, 0:64], T.stj[:], 4096.0, -2065.0 - OFF, A.mult, A.add, ["stj"], ["st"], S)
+    ts(T.st[:, 0:64], T.stj[:], 4096.0, -2065.0, A.mult, A.add, ["stj"], ["st"], S)
     for n in (64, 128, 256):
         act(T.st[:, n:2 * n], T.st[:, 0:n], F.Copy, ["st"], ["st"], c=n)
     for n in (512, 1024, 1536):
@@ -292,7 +296,6 @@ def rank_program(g, core, T, topo):
     ts(col(14), col(1), 32.0, None, A.mult, None, ["pc"], ["pc14"], S)
     ts(T.zl[:], T.ramp[:, 112:120], col(12), None, A.is_equal, None, ["ramp", "pc12"], ["zl"], S)
     ts(col(8), col(0), 0.5, None, A.add, None, ["pc"], ["pc8"], S)
-    ts(col(9), col(0), 16.0, float(SP), A.mult, A.add, ["pc"], ["pc9"], S)
     ts(col(10), col(0), -8192.0, 4096.0, A.mult, A.add, ["pc"], ["pc10"], S)
     ts(T.zg[:], T.ramp[:, 112:120], col(3), None, A.is_equal, None, ["ramp", "pc"], ["zg"], S)
     ts(T.mx[:], T.ramp[:, 112:116], col(1), None, A.is_equal, None, ["ramp", "pc"], ["mx"], S)
@@ -301,12 +304,7 @@ def rank_program(g, core, T, topo):
     ts(T.sel[:], T.ramp[:, 112:144], col(13), 1.0 / 64, A.is_equal, A.mult, ["ramp", "pc13"], ["sel"], S)
     ts(T.idb[:], R, col(7), None, A.is_equal, None, ["ramp", "pc"], ["idb"], S)
     ts(T.spc[:], T.ramp[:, 112:120], 16.0, col(8), A.mult, A.add, ["ramp", "pc8"], ["spc"], S)
-    ts(T.ls[:], T.ramp[:, 112:120], 256.0, col(9), A.mult, A.add, ["ramp", "pc9"], ["ls"], S)
-    tt(T.am[:], T.ls[:], T.spc[:], A.subtract, ["ls", "spc"], ["am"], S)
-    tt(T.y2[:], T.ls[:], T.spc[:], A.add, ["ls", "spc"], ["y2"], S)
-    for t in range(RO):
-        ts(T.hd[:, 8 * t:8 * t + 8], T.am[:], t + 0.5, 0.5, A.add, A.mult, ["am"], ["hd%d" % t], S)
-        ts(T.md[:, 8 * t:8 * t + 8], T.y2[:], t - 0.5, 0.5, A.add, A.mult, ["y2"], ["md%d" % t], S)
+    ts(T.ls[:], T.spc[:], 128.0, None, A.add, None, ["spc"], ["ls"], S)
     Z = {}
     for i, (k, x) in enumerate((("zp", 512.0), ("zn", -512.0), ("zh", 256.0))):
         Z[k] = T.zz[:, 8 * i:8 * i + 8]
@@ -324,23 +322,23 @@ def rank_program(g, core, T, topo):
     mm(T.psL[:, 16:20], T.ka[:], T.kr[:], True, True, ["ka", "kr"], ["psL:1"])
     ts(T.pmk[:], T.r16[:], col(5), 64.0, A.is_equal, A.mult, ["r16", "pc"], ["pmk"])
     ts(T.cm[:], T.r16[:], -0.25, 3.75, A.mult, A.add, ["r16"], ["cm"], S)
-    vc(T.kb[:, 0:4], T.psL[:, 16:20], ["psL:1"], ["kb"], S)
-    ts(T.k16[:], T.psL[:, 16:20], 16.0, 2047.5, A.mult, A.add, ["psL:1"], ["k16"], S)
-    tt(T.kb[:, 4:8], T.kb[:, 0:4], T.psL[:, 16:20], A.mult, ["kb", "psL:1"], ["kq"], S)
-    ts(T.k8[:], T.kb[:, 4:8], -8.0, -0.375, A.mult, A.add, ["kq"], ["k8"], S)
-    ms(T.ri[:], 0.0, ["ri0"], c=292)
+    for t in range(RO):
+        ts(T.su[:, 40 * t + 32:40 * t + 36], T.psL[:, 16:20], 2.0, None, A.mult, None, ["psL:1"], ["k16%d" % t], S)
+    ts(T.k8[:], T.psL[:, 16:20], 4095.0, -0.25, A.mult, A.add, ["psL:1"], ["k8"], S)
+    ts(T.su[:, 36:40], T.psL[:, 16:20], 4095.0, -0.25, A.mult, A.add, ["psL:1"], ["kc0"], S)
+    ts(T.ri[:], R, col(11), 8192.0, A.is_equal, A.mult, ["ramp", "pc11"], ["ri"], S)
     ms(T.mk[:], 1024.0 + SP, ["mk0"], c=292)
     ms(T.rx[:, 0:128], -8192.0, ["rx0"])
     ms(T.rx[:, 128:136], 1.0, ["rx"])
     ts(T.ramp2[:], T.ramp[:, 0:128], 8192.0, None, A.mult, None, ["ramp"], ["ramp2"], S)
     for c in range(8):
         s, w = SEG[c], 16 * c + 16
-        ts(T.ri[:, s:s + w], T.ramp[:, 112:112 + w], col(11), 8192.0, A.is_equal, A.mult, ["ramp", "pc11", "ri0"], ["ri%d" % c], S)
         ts(T.rn[:, s:s + w + 1], T.rx[:, 128 - w:129], T.zl[:, c:c + 1], None, A.mult, None, ["rx0", "rx", "zl"], ["rn%d" % c], S)
         ts(T.mk[:, s:s + w], T.ramp2[:, 128 - w:128], col(10), T.spc[:, c:c + 1], A.add, A.max,
            ["ramp2", "pc10", "spc", "mk0"], ["mk%d" % c], S)
 
     ts(T.idf[:], R, col(7), None, A.is_equal, None, ["ramp", "pc"], ["idf"])
+    act(T.idn[:], T.idf[:], F.Identity, ["idf"], ["idn"], scale=-1.0)
     PA, PV, PW, PL = T.psA, T.psV, T.psW, T.psL
     P0, P1, P2, P3 = [slice(128 * i, 128 * i + 128) for i in range(4)]
     TAB = T.tab[:, SP:W]
@@ -350,7 +348,7 @@ def rank_program(g, core, T, topo):
         e = T.ents[:, 0:2048:16]
         ts(T.c1[:], e, -1024.5, MB, A.add, A.add, ["ents"], ["c1"])
         ts(PV[:, P0], T.c1[:], CZ, None, A.add, None, ["c1"], ["psV:0"])
-        tt(T.so[:, 0:128], e, PV[:, P0], A.add, ["ents", "psV:0"], ["so0"])
+        tt(T.lw[:, 0:128], e, PV[:, P0], A.add, ["ents", "psV:0"], ["so0"])
 
     def first_table():
         for i in range(8):
@@ -363,10 +361,11 @@ def rank_program(g, core, T, topo):
 
     def lane_list(t, dst):
         o = 128 * t
-        src, sk = (T.so[:, 0:128], "so0") if t == 0 else (T.tab[:, SP + t:W:16], "tab")
+        so = T.lw[:, 2 * o:2 * o + 128] if t < RO - 1 else T.lw[:, 1024:1152]
+        src, sk = (so, "so0") if t == 0 else (T.tab[:, SP + t:W:16], "tab")
         if t:
-            act(T.so[:, o:o + 128], src, F.Copy, [sk], ["so%d" % t])
-        send(dst, T.lo[:, o:o + 128], T.so[:, o:o + 128], ["so%d" % t], "ro%d" % t, "lo%d" % t)
+            act(so, src, F.Copy, [sk], ["so%d" % t])
+        send(dst, T.lo[:, o:o + 128], so, ["so%d" % t], "ro%d" % t, "lo%d" % t)
         if t:
             ts(T.i1[:], src, -2033.0, None, A.add, None, [sk], ["i1"])
             ts(T.i3[:], T.i1[:], 16 - 4096, None, A.bitwise_and, None, ["i1"], ["i3"])
@@ -405,70 +404,79 @@ def rank_program(g, core, T, topo):
         return ["fs%d" % i for i in range(len(cuts) - 1)]
 
     def cand(t, dst, fs):
-        o = 128 * t
         U = T.psU[:, 0:32]
         mm(U, T.ones[:], T.uc[:], True, False, ["ones", "uc0", "uc"], ["psU"])
         for x in range(4):
             mm(U, T.w4[:, 128 * x:128 * x + 128], T.fs[:, 512 * x + 15:512 * x + 512:16], False, x == 3,
                ["w4%d" % x] + [k for i, k in enumerate(fs) if CUTS[i] < 32 * x + 32 and CUTS[i + 1] > 32 * x], ["psU"])
-        kc, kk = T.k8, "k8"
+        o = 40 * t
         if t:
-            kc, kk = T.kc, "kc"
             n, nk = T.la[:, 12 * t - 4:12 * t - 3], "la%d" % (t - 1)
-            ts(T.aa[:, 1:2], n, -15.5, M32, A.add, A.add, [nk], ["aa1"], S)
-            ts(T.aa[:, 2:3], T.aa[:, 1:2], -M32, -1.0, A.add, A.mult, ["aa1"], ["aa2"], S)
-            ts(kc[:], T.k8[:], n, T.aa[:, 2:3], A.add, A.add, ["k8", nk, "aa2"], ["kc"], S)
+            ts(T.aa[:, 1:2], n, -31.0, M32 * 2, A.add, A.add, [nk], ["aa1"], S)
+            ts(T.aa[:, 2:3], T.aa[:, 1:2], -M32 * 2, -1.0, A.add, A.mult, ["aa1"], ["aa2"], S)
+            ts(T.su[:, o + 36:o + 40], T.k8[:], n, T.aa[:, 2:3], A.add, A.add, ["k8", nk, "aa2"], ["kc%d" % t], S)
         ts(T.ur[:], U, MN, -MN, A.add, A.add, ["psU"], ["ur"], S)
-        tt(T.uu[:], U, T.ur[:], A.subtract, ["psU", "ur"], ["uu"], S)
-        for b in range(4):
-            s = slice(32 * b, 32 * b + 32)
-            act(T.vq[:, s], T.uu[:], F.Square, ["uu", "k16"], ["vq%d" % b], bias=T.k16[:, b:b + 1], c=S)
-            ts(T.u5[:, s], T.vq[:, s], 0.03125, kc[:, b:b + 1], A.mult, A.add, ["vq%d" % b, kk], ["u5%d" % b], S)
-        ts(T.u6[:], T.u5[:], 2047, None, A.bitwise_and, None, ["u5%d" % b for b in range(4)], ["u6"])
-        vc(T.se[:, o:o + 128], T.u6[:], ["u6"], ["se%d" % t])
-        send(dst, T.le[:, o:o + 128], T.se[:, o:o + 128], ["se%d" % t], "re%d" % t, "le%d" % t)
-        n = 128 * LH
-        for x in range(4):
-            ts(T.sh[:, n * t + x:n * t + n:4], T.se[:, o:o + n // 4], -1023.5, T.mx[:, x:x + 1], A.add, A.mult,
-               ["se%d" % t, "mx"], ["sh%d%d" % (t, x)], S)
-        send(dst, T.lh[:, n * t:n * t + n], T.sh[:, n * t:n * t + n], ["sh%d%d" % (t, x) for x in range(4)] + ["~sentre%d" % t],
-             "rh%d" % t, "lh%d" % t)
+        tt(T.su[:, o:o + 32], U, T.ur[:], A.subtract, ["psU", "ur"], ["se%d" % t], S)
+        send(dst, T.lu[:, o:o + 40], T.su[:, o:o + 40], ["se%d" % t, "k16%d" % t, "kc%d" % t], "re%d" % t, "lu%d" % t)
 
-    def scatter(tab, lists, vals, r, off):
-        ts(T[tab][:].indirect(lists), vals, 1.0, off, A.mult, A.add, r, [tab], int(60 + SCATTER * 128))
+    def cand_list(t):
+        o, lk = 40 * t, "lu%d" % t
+        u = T.lu[:, o:o + 32]
+        act(T.vq[:], u, F.Square, [lk, "~ox"], ["vq"], bias=2047.5 / 4, scale=0.25, c=S)
+        act(PW[:], T.ox[:], F.Copy, ["ox", "~vq"], ["psW"], c=512)
+        for b in range(4):
+            ts(PL[:, 256 + 32 * b:288 + 32 * b], u, T.lu[:, o + 32 + b:o + 33 + b], T.lu[:, o + 36 + b:o + 37 + b], A.mult, A.add,
+               [lk], ["psL:b%d" % b], S)
+        for b in range(4):
+            tt(T.u5[:, 32 * b:32 * b + 32], T.vq[:], PL[:, 256 + 32 * b:288 + 32 * b], A.add, ["vq", "psL:b%d" % b, "~psL:b3"], ["u5%d" % b], S)
+        ts(T.u6[:], T.u5[:], 1, 2047, A.arith_shift_right, A.bitwise_and, ["u5%d" % b for b in range(4)], ["u6"])
+        vc(T.le[:], T.u6[:], ["u6"], ["le"])
+        for x in range(EARLY):
+            ts(T.eh[:, x:512:4], T.u6[:], -1023.5, T.mx[:, x:x + 1], A.add, A.mult, ["u6", "mx", "~le"], ["eh%d" % x])
+
+    def scatter(tab, t):
+        tt(T[tab][:].indirect(T.l2[:, 8 * t:8 * t + 8]), T.nb[:], T.nr[:], A.add, ["l2%d" % t, "nb", "nr", tab], [tab],
+           int(60 + SCATTER * 128))
 
     def expand(t):
         av, lk = T.lo[:, 128 * t:128 * t + 128], "lo%d" % t
         act(T.c1[:], av, F.Identity, [lk], ["c1"], bias=-8.5)
         act(PA[:, P0], av, F.Identity, [lk], ["psA:0"], bias=OFF)
+        act(PL[:, P1], T.st[:, t:2048:16], F.Copy, ST, ["psL:a"])
         act(T.c2[:], T.c1[:], F.Identity, ["c1"], ["c2"], bias=M16 + 16.0)
         act(T.c3[:], T.c2[:], F.Identity, ["c2"], ["c3"], bias=-M16 - 16.0)
         act(T.ox[:], T.c3[:].indirect(T.cl[:]), F.Identity, ["c3", "cl"], ["ox"], bias=8.5, c=gc(512) - 64)
-        if GA:
-            act(PW[:], T.ox[:], F.Copy, ["ox"], ["psW"], c=512)
 
     def own_side(t):
-        tt(T.ah[:], T.st[:, t:2048:16], PA[:, P0], A.add, ["psA:0"] + ST, ["ah"])
+        tt(T.ah[:], T.lo[:, 128 * t:128 * t + 128], PL[:, P1], A.add, ["lo%d" % t, "psL:a"], ["ah"])
         ts(T.al[:], T.ah[:], 31, None, A.bitwise_and, None, ["ah"], ["al"])
         ts(T.ak[:], T.ah[:], 15, 7, A.arith_shift_right, A.bitwise_and, ["ah"], ["ak"])
         ts(PV[:, P0], T.al[:], 8.0 + t, 64.0, A.is_ge, A.mult, ["al"], ["psV:0"])
         tt(T.av[:], T.ak[:], PV[:, P0], A.is_le, ["ak", "psV:0"], ["av"])
         tt(T.as2[:], T.al[:], PV[:, P0], A.add, ["al", "psV:0"], ["as2"])
         tt(T.ap[:], T.av[:], PA[:, P0], A.mult, ["av", "psA:0"], ["ap"])
-        act(T.ac[:], T.ap[:], F.Identity, ["ap"], ["ac"], bias=MN)
-        act(T.ar[:], T.as2[:], F.Relu, ["as2"], ["ar"], bias=80 * 2.0 ** 25, scale=-2.0 ** 25)
-        act(PL[:, P1], T.as2[:], F.Relu, ["as2"], ["psL:a"], bias=12.0 + t, scale=-1.0)
-        act(T.di[:], T.ac[:], F.Identity, ["ac"], ["di"], bias=MN, scale=-1.0)
-        mm(PA[:, P3], T.idf[:], T.di[:], True, False, ["idf", "di"], ["psA:3"], 512)
-        act(PL[:, P2], T.ar[:], F.Identity, ["ar"], ["psL:b"], bias=OFF + 13.0 + t, scale=-1.0)
+
+    def own_rest(t):
+        act(T.ay[:], T.ap[:], F.Identity, ["ap"] + ["~ma1"] * (t < RO - 1), ["ay"], bias=-OFF)
+        mm(PA[:, P1], T.idn[:], T.ay[:], True, False, ["idn", "ay"] + ["~" + k for k in KEYS], ["psA:1"], 512)
+        act(PV[:, P2], T.as2[:], F.Relu, ["as2", "~ay"], ["psV:2"], bias=(12.0 + t) / 16, scale=-1.0 / 16)
+        act(T.sg[:], T.as2[:], F.Sign, ["as2", "~ay"], ["sg"], bias=-79.5)
+        act(PV[:, P3], T.sg[:], F.Identity, ["sg"], ["psV:3"], scale=8.0 + t)
+        lane, lk, off = T.ap, "ap", -OFF
+        if t == RO - 1:
+            lane, lk, off = T.na, "na", 0.0
+            act(T.ac[:], T.ap[:], F.Identity, ["ap", "~ay"], ["ac"], bias=MN)
+            act(PA[:, P2], T.ac[:], F.Identity, ["ac"], ["psA:2"], bias=MN / 2, scale=-0.5)
+            tt(T.na[:], T.ap[:], PA[:, P2], A.add, ["ap", "psA:2"], ["na"])
+        tt(T.ao[:], lane[:], PV[:, P0], A.mult, [lk, "psV:0"], ["ao"])
+        act(T.az[:], T.ao[:], F.Identity, ["ao", "~ay"], ["az"], bias=off, scale=1.0 / 64)
 
     KEYS = (["psK:%s%d%d" % (k, i, x) for i in range(4) for k in ("mt", "db")[:1 if i in TA else 2] for x in range(4)]
             + ["psK:e%d" % i for i in range(4)])
 
     def score(t):
-        o = 128 * t
         K = T.psK
-        lk = "le%d" % t
+        lk = "le"
         left = [len(KEYS)]
         EH = ["eh%d" % x for x in range(4)]
 
@@ -486,34 +494,40 @@ def rank_program(g, core, T, topo):
                 add(K[:, 4 * x + i:128:16], tile[:, 512 * i + x:512 * i + 512:4], Z[z], (r or [k]) + [z], "psK:%s%d" % (k, x))
 
         for i in GA:
-            act(T.cf[:, 512 * i:512 * i + 512], TAB.indirect(T.le[:, o + 32 * i:o + 32 * i + 32]), F.Copy,
+            act(T.cf[:, 512 * i:512 * i + 512], TAB.indirect(T.le[:, 32 * i:32 * i + 32]), F.Copy,
                 ["tab", lk, "~cf%d" % (2 * i - 2)], ["cf%d" % (2 * i), "cf%d" % (2 * i + 1)], c=gc(512) - 64)
         tests = {"mt": (MN + 4096.0, "zp"), "db": (M16, "zn")}
-        prev = "~"
+        prev = "~eh%d" % (EARLY - 1)
         for step in STEPS:
             k, i = step[:2], int(step[2])
             c = slice(512 * i, 512 * i + 512)
             if k == "dd" and i in GA:
                 tt(T.dd[:, c], T.cf[:, c], PW[:], A.subtract, ["cf%d" % (2 * i), "cf%d" % (2 * i + 1), "psW", prev], [step], 512)
             elif k == "dd":
-                tt(T.dd[:, c], TAB.indirect(T.le[:, o + 32 * i:o + 32 * i + 32]), T.ox[:], A.subtract, ["tab", lk, "ox", prev], [step], gc(512))
+                tt(T.dd[:, c], TAB.indirect(T.le[:, 32 * i:32 * i + 32]), T.ox[:], A.subtract, ["tab", lk, "ox", prev], [step], gc(512))
             elif k in tests:
                 ts(T[k][:, c], T.dd[:, c], tests[k][0], tests[k][0], A.add, A.is_equal, ["dd%d" % i, prev], [step], 256)
                 sums(i, T[k], step, tests[k][1])
             elif k == "eh":
-                for x in range(4):
-                    ts(T.eh[:, 128 * LH + x:512:4], T.le[:, o + 32 * LH:o + 128], -1023.5, T.mx[:, x:x + 1], A.add, A.mult,
-                       [lk, "mx", prev], [EH[x]], S)
+                for x in range(EARLY, 4):
+                    ts(T.eh[:, x:512:4], T.le[:], -1023.5, T.mx[:, x:x + 1], A.add, A.mult, [lk, "mx", prev], [EH[x]], S)
                     prev = "~" + EH[x]
                 for b in range(4):
-                    src, sk = (T.lh[:, 128 * (LH * t + b):128 * (LH * t + b + 1)], ["lh%d" % t]) if b < LH else (T.eh[:, 128 * b:128 * b + 128], EH)
-                    add(K[:, b:128:4], src, T.sel[:], ["sel"] + sk, "psK:e%d" % b)
+                    add(K[:, b:128:4], T.eh[:, 128 * b:128 * b + 128], T.sel[:], ["sel"] + EH, "psK:e%d" % b)
+                step = EH[3]
             else:
-                for x in range(4):
+                for j in LAST:
+                    x = j % 4
                     c4 = slice(c.start + x, c.stop, 4)
+                    if j < 4:
+                        tt(T.dd[:, c4], T.cf[:, c4], PW[:, x:512:4], A.subtract, ["cf%d" % (2 * i), "cf%d" % (2 * i + 1), "psW", prev],
+                           ["dd%d%d" % (i, x)])
+                        prev = "~dd%d%d" % (i, x)
+                        continue
                     for k, (m, z) in tests.items():
-                        ts(T[k][:, c4], T.dd[:, c4], m, m, A.add, A.is_equal, ["dd%d" % i, prev], ["%s%d%d" % (k, i, x)], S)
+                        ts(T[k][:, c4], T.dd[:, c4], m, m, A.add, A.is_equal, ["dd%d%d" % (i, x), prev], ["%s%d%d" % (k, i, x)], S)
                         add(K[:, 4 * x + i:128:16], T[k][:, c4], Z[z], ["%s%d%d" % (k, i, x), z], "psK:%s%d%d" % (k, i, x))
+                        prev = "~%s%d%d" % (k, i, x)
             prev = "~" + step
             if k == "dd" and i in TA:
                 for h in (2 * i, 2 * i + 1):
@@ -542,84 +556,140 @@ def rank_program(g, core, T, topo):
         after = "~psL:0"
         for i in range(len(DB)):
             pairs(i, T.pm[:], "pm", "rn", False, False, [after])
-            pairs(i, T.pe[:], "pe", "ri", False, True)
+            k, c0, c1 = DB[i]
+            for c in range(c0, c1):
+                s, w = SEG[c] - SEG[c0], 16 * c + 16
+                mm(T[k][:, s:s + w], T.pe[:], T.ri[:, 0:w], False, c == c1 - 1, ["pe", "ri"], [k], max(S, w))
             after = "~%s:0" % DB[i][0]
         ts(T.l1[:], T.psL[:, 0:8], 1023.5, None, A.add, None, ["psL:0"], ["l1"], S)
-        ts(T.bg[:], TAB.indirect(T.l1[:]), OFF, None, A.add, None, ["tab", "l1"], ["bg"], gc(128))
-        act(T.c1[:], TAB.indirect(T.l1[:]), F.Identity, ["tab", "l1"], ["c1"], bias=-8.5, c=gc(128) - 64)
-        tt(T.bh[:], T.st[:].indirect(T.l1[:]), T.bg[:], A.add, ST + ["l1", "bg"], ["bh"], gc(128))
+        act(T.bs[:], T.st[:].indirect(T.l1[:]), F.Copy, ST + ["l1"], ["bs"], c=gc(128) - 64)
+        act(T.bg[:], TAB.indirect(T.l1[:]), F.Copy, ["tab", "l1", "~bs"], ["bg"], c=gc(128) - 64)
+        ts(T.bh[:], TAB.indirect(T.l1[:]), -2065.0, None, A.add, None, ["tab", "l1"], ["bh"], gc(128))
+        mm(PA[:, P1], T.idf[:], T.bg[:], False, True, ["idf", "bg", "~psU:0"], ["psA:1"], 512)
+        prev = "~bg"
+        for step in SCALAR:
+            if step == "dq":
+                act(T.dq[:], PA[:, P1], F.Square, ["psA:1", prev], [step], scale=1.0 / 2048)
+            elif step == "bz":
+                act(T.bz[:], T.bg[:], F.Sign, ["bg", prev], [step], bias=OFF)
+            elif step[1] == "a":
+                k, c0, c1 = DB[int(step[2])]
+                act(T.xa[:, SEG[c0]:SEG[c1]], T[k][:, 0:SEG[c1] - SEG[c0]], F.Abs, [k, prev], [step], c=SEG[c1] - SEG[c0])
+            else:
+                c = int(step[2])
+                s = slice(SEG[c], SEG[c + 1])
+                act(T.xb[:, s], T.xa[:, s], F.Relu, ["xa%d" % i for i in range(3) if SPLIT[i] <= c < SPLIT[i + 1]] + [prev], [step],
+                    bias=4096.0, scale=-1.0, c=SEG[c + 1] - SEG[c] + 24, acc=T.xc[:, c:c + 1])
+            prev = "~" + step
         for k, c0, c1 in DB:
-            for c in range(c0, c1):
-                least(T.mn[:, c:c + 1], T[k][:, SEG[c] - SEG[c0]:SEG[c + 1] - SEG[c0]], [k], ["mn%d" % c], max(S, SEG[c + 1] - SEG[c]))
+            for c in range(c0, min(c1, AM)):
+                least(T.mn[:, c:c + 1], T[k][:, SEG[c] - SEG[c0]:SEG[c + 1] - SEG[c0]], [k, "~bh"], ["mn%d" % c], max(S, SEG[c + 1] - SEG[c]))
+        act(T.xc[:, 8 + AM:16], T.xc[:, AM:8], F.Identity, ["xb%d" % c for c in range(AM, 8)], ["xc"], bias=4096.0, scale=-1.0, c=S)
+        tt(T.mn[:, AM:8], T.xc[:, 8 + AM:16], T.spc[:, AM:8], A.max, ["xc", "spc"], ["mn%d" % c for c in range(AM, 8)], S)
         mk = ["mn%d" % c for c in range(8)]
         ts(T.l2[:, 8 * t:8 * t + 8], T.mn[:], -0.5, None, A.add, None, mk, ["l2%d" % t], S)
         return mk
 
     def merged(t, dst, mk):
         o = 12 * t
-        act(T.wj[:], T.mn[:], F.Sign, mk, ["wj", "aa0"], bias=-SP - 0.25, c=S, acc=T.aa[:, 0:1])
         if t < RO - 1:
+            act(T.wj[:], T.mn[:], F.Sign, mk, ["wj", "aa0"], bias=-SP + 0.75, c=S, acc=T.aa[:, 0:1])
             mm(T.psL[:, 32:33], T.half[:], T.aa[:, 0:1], True, True, ["half", "aa0"], ["psL:2"], 256)
             act(T.sa[:, o + 8:o + 9], T.psL[:, 32:33], F.Copy, ["psL:2", "sa"], ["sb%d" % t], c=S)
-        tt(T.y2[:], T.wj[:], T.hd[:, 8 * t:8 * t + 8], A.mult, ["wj", "hd%d" % t], ["y2"], S)
-        tt(T.sa[:, o:o + 8], T.y2[:], T.md[:, 8 * t:8 * t + 8], A.add, ["y2", "md%d" % t, "sa"], ["sa%d" % t], S)
+        tt(T.sa[:, o:o + 8], T.mn[:], T.ls[:], A.min, mk + ["ls", "sa"], ["sa%d" % t], S)
         send(dst, T.la[:, o:o + 12], T.sa[:, o:o + 12], ["sa", "sa%d" % t, "sb%d" % t], "ra%d" % t, "la%d" % t)
 
     def meet(t, dst):
         o = 128 * t
         last = t == RO - 1
-        mm(PA[:, P3], T.idf[:], T.bg[:], False, True, ["idf", "bg", "~psU:0"], ["psA:3"], 512)
-        act(T.dq[:], PA[:, P3], F.Square, ["psA:3"], ["dq"], bias=0.5, scale=1.0 / 2048)
-        act(T.sg[:], T.dq[:], F.Sign, ["dq"], ["sg"], bias=1.0, scale=-1.0)
-        ts(T.bl[:], T.bh[:], 31, None, A.bitwise_and, None, ["bh"], ["bl"])
-        ts(T.bk[:], T.bh[:], 15, 7, A.arith_shift_right, A.bitwise_and, ["bh"], ["bk"])
-        ts(T.bi[:], T.bh[:], 16, None, A.bitwise_and, None, ["bh"], ["bi"])
-        ts(PW[:, P0], T.bl[:], 8.0 + t, 64.0, A.is_ge, A.mult, ["bl"], ["psW:0"])
-        act(T.c2[:], T.c1[:], F.Identity, ["c1"], ["c2"], bias=M16)
-        act(T.y3[:], T.c2[:], F.Identity, ["c2"], ["y3"], bias=-M16)
+        PK = T.psK
         if last:
-            tt(PL[:, P1], T.av[:], PL[:, P1], A.mult, ["av", "psL:a"], ["psL:a"])
-        tt(PW[:, P2], T.bi[:], PL[:, P1], A.min, ["bi", "psL:a"], ["psW:2"])
-        tt(PW[:, P1], T.bk[:], PW[:, P0], A.is_le, ["bk", "psW:0"], ["psW:1"])
-        tt(PW[:, P3], T.bk[:], PW[:, P0], A.is_equal, ["bk", "psW:0"], ["psW:3"])
-        lane, site, wake = "ap", "bg", (PL[:, P2], "psL:b")
-        if last:
-            lane, site, wake = "na", "nc", (PV[:, P3], "psV:3")
-            act(T.ly[:], T.di[:], F.Identity, ["di"], ["ly"], scale=0.5)
-            tt(T.na[:], T.ap[:], T.ly[:], A.add, ["ap", "ly"], ["na"], 256)
-            tt(PV[:, P3], T.ly[:], PL[:, P2], A.add, ["ly", "psL:b"], ["psV:3"])
             act(T.ac[:], T.bg[:], F.Identity, ["bg"], ["ac"], bias=MB, scale=0.5)
-            act(PA[:, P1], T.ac[:], F.Identity, ["ac"], ["psA:1"], bias=-MB)
-            tt(T.nc[:], T.bg[:], PA[:, P1], A.subtract, ["bg", "psA:1"], ["nc"])
-        tt(T.y4[:], T.y3[:], wake[0], A.add, ["y3", wake[1]], ["y4"])
-        tt(PW[:, P2], T[lane][:], PW[:, P2], A.add, [lane, "psW:2"], ["psW:2"])
-        tt(T.t2[:], T.y4[:], PW[:, P3], A.mult, ["y4", "psW:3"], ["t2"])
-        tt(T.bp[:], T[site][:], PW[:, P1], A.mult, [site, "psW:1"], ["bp"])
-        tt(T.smv[:], T.sg[:], PW[:, P1], A.mult, ["sg", "psW:1"], ["smv"])
-        tt(PW[:, P3], T.t2[:], PW[:, P2], A.max, ["t2", "psW:2"], ["psW:3"])
-        if last:
-            ts(PL[:, P3], T.al[:], 8.0 + t, None, A.is_ge, None, ["al"], ["psL:c"])
-            tt(PV[:, P1], T.bp[:], PL[:, P3], A.is_lt, ["bp", "psL:c"], ["psV:1"])
+            act(PL[:, P2], T.ac[:], F.Identity, ["ac"], ["psL:b"] + ["psL:b%d" % b for b in range(4)], bias=-MB - OFF / 2)
+            act(PK[:, P2], T.az[:], F.Copy, ["az", "ks", "kh"], ["psK:2"])
         else:
-            tt(PV[:, P1], T.bp[:], PV[:, P0], A.is_lt, ["bp", "psV:0"], ["psV:1"])
-        tt(T.m2[:], T.smv[:], PV[:, P1], A.max, ["smv", "psV:1"], ["m2"])
-        tt(PV[:, P1], T.m2[:], PW[:, P3], A.mult, ["m2", "psW:3"], ["psV:1"])
-        tt(T.nb[:, o:o + 128], T.bp[:], PV[:, P1], A.max, ["bp", "psV:1"], ["nb%d" % t])
-        if not last:
-            scatter("tab", T.l2[:, 8 * t:8 * t + 8], T.nb[:, o:o + 128], ["l2%d" % t, "nb%d" % t], -OFF)
-        tt(PV[:, P2], T.ap[:], PW[:, P0], A.is_lt, ["ap", "psW:0"], ["psV:2"])
-        tt(PV[:, P3], T.bp[:], PW[:, P3], A.max, ["bp", "psW:3"], ["psV:3"])
-        tt(T.m3[:], T.smv[:], PV[:, P2], A.max, ["smv", "psV:2"], ["m3"])
-        tt(PV[:, P2], T.m3[:], PV[:, P3], A.mult, ["m3", "psV:3"], ["psV:2"])
-        tt(T.sn[:, o:o + 128], T[lane][:], PV[:, P2], A.max, [lane, "psV:2"], ["sn%d" % t])
-        send(dst, T.ln[:, o:o + 128], T.sn[:, o:o + 128], ["sn%d" % t], "rn%d" % t, "ln%d" % t)
+            mm(PK[:, P1], T.idn[:], T.az[:], True, False, ["idn", "az", "ks", "kh"], ["psK:1"], 512)
+            mm(PK[:, P1], T.idf[:], T.bg[:], False, True, ["idf", "bg", "~psA:1"], ["psK:1"], 512)
+        place = {"psA:1": PA[:, P1], "psK:1": PK[:, P1], "psK:2": PK[:, P2], "psL:a": PL[:, P1], "psL:b": PL[:, P2], "psL:c": PL[:, P3],
+                 "sn%d" % t: T.sn[:, o:o + 128]}
+        for i, s in enumerate((P0, P1, P2, P3)):
+            place["psV:%d" % i], place["psW:%d" % i] = PV[:, s], PW[:, s]
+        prev = ["~bh"]
+
+        def at(k):
+            return place[k] if k in place else T[k][:]
+
+        def one(w, r, s1, s2, o0, o1=None):
+            ts(at(w), at(r), s1, s2, o0, o1, [r] + prev, [w])
+            prev[0] = "~" + w
+
+        def two(w, r0, r1, o):
+            tt(at(w), at(r0), at(r1), o, [r0, r1] + prev, [w])
+            prev[0] = "~" + w
+
+        def site():
+            if last:
+                two("nr", "r0", "psV:1", A.mult)
+                two("dz", "bz", "psK:1", A.mult)
+                two("psV:0", "dz", "psW:1", A.mult)
+                two("nb", "az", "psV:0", A.add)
+            else:
+                two("nr", "r0", "psV:1", A.mult)
+                two("nb", "az", "psV:0", A.add)
+
+        one("bl", "bh", 31, None, A.bitwise_and)
+        one("bi", "bh", 16, None, A.bitwise_and)
+        tt(T.bj[:], TAB.indirect(T.l1[:]), T.bs[:], A.add, ["tab", "l1", "bs"] + prev, ["bj"], gc(128))
+        prev[0] = "~bj"
+        one("psW:0", "bl", 8.0 + t, 64.0, A.is_ge, A.mult)
+        two("f2", "bl", "psV:3", A.is_lt)
+        one("bk", "bj", 15, 7, A.arith_shift_right, A.bitwise_and)
+        one("psW:3", "bl", -1.0, 12.0 + t, A.mult, A.add)
+        two("wq", "bi", "psV:2", A.mult)
+        two("psW:1", "bk", "psW:0", A.is_le)
+        if last:
+            two("bn", "bg", "psL:b", A.subtract)
+            two("psL:c", "ap", "psW:0", A.is_lt)
+        two("t2", "f2", "psW:3", A.mult)
+        if last:
+            two("psL:a", "bn", "psL:c", A.mult)
+            two("psW:2", "t2", "psA:1", A.add)
+            two("psV:1", "dq", "psW:1", A.is_lt)
+            two("sx", "na", "psL:a", A.add)
+            two("m3", "wq", "psW:2", A.max)
+            two("psK:1", "bn", "psK:2", A.subtract)
+            two("psW:3", "m3", "psV:1", A.mult)
+            two("r0", "m3", "psA:1", A.subtract)
+            two("sn%d" % t, "sx", "psW:3", A.add)
+            site()
+        else:
+            two("psW:2", "wq", "psA:1", A.subtract)
+            two("dz", "bz", "psK:1", A.mult)
+            two("psV:1", "dq", "psW:1", A.is_lt)
+            two("r0", "t2", "psW:2", A.max)
+            two("psV:0", "dz", "psW:1", A.mult)
+            site()
+            two("sx", "ap", "psW:0", A.is_lt)
+            scatter("tab", t)
+            two("psW:3", "r0", "psA:1", A.add)
+            two("m3", "sx", "psV:1", A.max)
+            two("psW:2", "m3", "psW:3", A.mult)
+            two("sn%d" % t, "ay", "psW:2", A.add)
+        send(dst, T.lw[:, 2 * o + 128:2 * o + 256], T.sn[:, o:o + 128], ["sn%d" % t], "rn%d" % t, "ln%d" % t)
 
     def back(t):
-        o = 128 * t
-        tab, off = ("tab", -OFF) if t < RO - 1 else ("fin", 0.0)
-        vc(T.lr[:], T.la[:, 12 * t:12 * t + 8], ["la%d" % t], ["lr"], S)
-        scatter(tab, T.lr[:], T.ln[:, o:o + 128], ["lr", "ln%d" % t, "~se%d" % (t + 1), tab], off)
-        scatter(tab, T.l2[:, 8 * t:8 * t + 8], T.nb[:, o:o + 128], ["l2%d" % t, "nb%d" % t, tab], off)
+        o = 256 * t
+        tab, old = "tab", "so%d" % t
+        if t == RO - 1:
+            tab, old = "fin", "sf"
+            so = T.lw[:, 1024:1152]
+            act(T.c1[:], so, F.Identity, ["so%d" % t, "~ma1"], ["c1"], bias=MB, scale=0.5)
+            act(PA[:, P3], T.c1[:], F.Identity, ["c1"], ["psA:3"], bias=-MB - OFF / 2)
+            tt(T.lw[:, o:o + 128], so, PA[:, P3], A.subtract, ["so%d" % t, "psA:3"], [old])
+        ts(T.lr[:], T.la[:, 12 * t:12 * t + 8], -0.5, None, A.add, None, ["la%d" % t], ["lr"], S)
+        act(T[tab][:, SP + t:W:16], T.lw[:, o:o + 256].indirect(T.lr[:]), F.Copy,
+            ["lr", "ln%d" % t, old, "~se%d" % (t + 1), tab], [tab], c=gc(128) - 64)
+        scatter(tab, t)
 
     def last_table():
         for i in range(8):
@@ -644,7 +714,9 @@ def rank_program(g, core, T, topo):
         own_side(t)
         if t:
             back(t - 1)
+        cand_list(t)
         score(t)
+        own_rest(t)
         merged(t, caller, partner(t))
         meet(t, caller)
     last_table()

from concourse.mybir import AluOpType, ActivationFunctionType, AxisListType

N = 8
RO = 4
M0 = 1.5 * 2.0 ** 23
M16, M32, MB, MN = M0 * 16, M0 * 32, M0 * 2048, M0 * 4096
OFF = 2.0 ** 23
SP = 256
W = SP + 2048
F2 = 4112
NE = 8
CUTS = (0, 56, 96, 128)
GA = (2, 3)
TA = (0,)
AM = 6
SCALAR = ("bz", "xa2", "dq", "xb6", "xb7")
EARLY = 2
STEPS = ("dd0", "eh0", "dd1", "dd2", "mt1", "db1", "mt2", "db2", "in3")
LAST = (0, 1, 2, 4, 3, 5, 6, 7)
SEG = [8 * c * (c + 1) + c for c in range(9)]
SPLIT = (0, 4, 6, 8)
HOP, SLACK, ROOM = 260, 40, 100
MORE = {"lo0": 2000, "la3": 800}
FLIGHT = {"lu": 2100, "lo": 3300, "la": 3600, "ln": 4000}
GATHER, SCATTER = 1.5, 3.8
LOADED = {"wti": 4200, "kpi": 4200, "ents": 4000, "fw": 7000}

_F, _B, _I, _H, _U = "float32", "bfloat16", "int32", "float16", "uint16"
SCRATCH = {}
for _n, _w, _d in [
        ("ents", 2048, _I), ("tab", W, _F), ("fin", W, _F), ("st", 2048, _F), ("fw", F2 + 8192, _B), ("cf", 2048, _F),
        ("wti", 4, _I), ("kpi", 4, _I), ("pj", 8, _I), ("zl", 8, _F), ("pcol", 20, _F), ("sti", 64, _I), ("stj", 64, _I),
        ("ones", 128, _B), ("half", 128, _F), ("idf", 128, _F), ("bd0", 128, _B), ("bd", 128, _B), ("w4", 512, _B),
        ("ramp", 240, _B), ("r16", 128, _B), ("r4", 128, _B), ("cm", 128, _B), ("idb", 128, _B), ("ka", 128, _B),
        ("kr", 4, _B), ("k8", 4, _F), ("uc", 32, _B), ("c2k", 128, _B),
        ("mx", 4, _B), ("zg", 8, _F), ("zz", 24, _B), ("cb", 8, _H), ("sel", 32, _H), ("cl", 32, _U),
        ("c8", 8, _U), ("pmk", 128, _F), ("ri", 128, _H), ("rn", 584, _H), ("mk", 584, _B), ("spc", 8, _F), ("ls", 8, _F),
        ("rx", 136, _B), ("ramp2", 128, _B), ("fm", 2048, _B),
        ("i1", 128, _I), ("i3", 128, _I), ("ly", 128, _F), ("lst", 128, _U), ("fg", 2048, _B), ("fs", 2048, _B),
        ("ur", 32, _F), ("vq", 32, _F), ("u5", 128, _I), ("u6", 128, _I),
        ("su", 160, _F), ("lu", 160, _F), ("le", 128, _U), ("lw", 1152, _F), ("lo", 512, _F), ("sa", 48, _F), ("la", 48, _F),
        ("sn", 512, _F), ("nb", 128, _F), ("nr", 128, _F), ("sg", 128, _F), ("lr", 8, _U), ("c1", 128, _F), ("c2", 128, _F), ("c3", 128, _F),
        ("ox", 512, _F), ("dd", 2048, _B), ("da", 2048, _B), ("db", 2048, _B), ("mt", 2048, _B), ("eh", 512, _H),
        ("ks", 128, _F), ("kh", 128, _H), ("p8", 8, _F), ("pe", 128, _H), ("pm", 128, _H), ("l1", 8, _U), ("l2", 32, _U),
        ("mn", 8, _F), ("xa", 584, _F), ("xb", 584, _F), ("xc", 16, _F), ("bj", 128, _I), ("wj", 8, _F), ("aa", 8, _F),
        ("ah", 128, _I), ("al", 128, _I), ("ak", 128, _I), ("av", 128, _F), ("ap", 128, _F), ("as2", 128, _F), ("ac", 128, _F),
        ("ao", 128, _F), ("bg", 128, _F), ("bs", 128, _F), ("bh", 128, _I), ("bl", 128, _I), ("bk", 128, _I), ("bi", 128, _I),
        ("idn", 128, _F), ("ay", 128, _F), ("az", 128, _F), ("bz", 128, _F), ("bn", 128, _F), ("wq", 128, _F), ("dq", 128, _F),
        ("dz", 128, _F), ("f2", 128, _F), ("t2", 128, _F), ("m3", 128, _F), ("na", 128, _F), ("r0", 128, _F), ("sx", 128, _F)]:
    SCRATCH[_n] = ("sbuf", [128, _w], _d)
for _n in ("psU", "psK", "psD0", "psD1", "psL", "psA", "psV", "psW"):
    SCRATCH[_n] = ("psum", [128, 512], _F)
SEMAPHORES = (["sV", "sA", "sP", "sG", "dent", "dsm", "dfe", "dy", "loc"]
              + ["%s%d" % (k, t) for k in ("ro", "re", "rn", "ra") for t in range(RO)])


def plan(calls):
    n = len(calls)
    pre = [dict() for _ in calls]
    wr, rd = {}, {}
    for i, (q, c, r, w) in enumerate(calls):
        for k in r:
            if k in wr:
                pre[i][wr[k]] = HOP
            elif k[1:] in wr and k[0] == "~":
                pre[i].setdefault(wr[k[1:]], 0)
        for k in w:
            for j in rd.get(k, []) + ([wr[k]] if k in wr else []):
                if j != i:
                    pre[i][j] = max(pre[i].get(j, 0), 0 if calls[j][0] == q == "P" else HOP)
        for k in w:
            wr[k], rd[k] = i, []
        for k in r:
            rd.setdefault(k, []).append(i)
    post = [[] for _ in calls]
    way = [0] * n
    for i in range(n - 1, -1, -1):
        way[i] += calls[i][1]
        for j, h in pre[i].items():
            post[j].append(i)
            way[j] = max(way[j], way[i] + h)
    banks = [set(k.split(":")[0] for k in r + w if k[:2] == "ps") for q, c, r, w in calls]
    left = [len(p) for p in pre]
    ready = [i for i in range(n) if not left[i]]
    end, free, used, order = [0] * n, {}, {}, []

    def earliest(i):
        q = calls[i][0]
        t = max([free.get(q, 0) if q != "R" else 0] + [end[j] + h for j, h in pre[i].items()])
        return max([t] + [e + HOP for b in banks[i] for o, e in used.get(b, {}).items() if o != q])

    while ready:
        at = {i: earliest(i) for i in ready}
        i = min(ready, key=lambda j: (at[j], -way[j]))
        q = calls[i][0]
        mine = [j for j in ready if calls[j][0] == q]
        if q != "R":
            last = max(at[o] + way[o] for o in ready) + SLACK
            due = {o: max([0] + [end[j] + h for j, h in pre[o].items()]) for o in mine}
            fits = [j for j in mine
                    if all(way[o] <= way[j] or at[j] + calls[j][1] <= max(at[o], min(due[o] + ROOM, last - way[o])) for o in mine)]
            i = min(fits, key=lambda j: (at[j], -way[j]))
        ready.remove(i)
        end[i] = at[i] + calls[i][1]
        free[q] = end[i]
        for b in banks[i]:
            used.setdefault(b, {})[q] = end[i]
        order.append((at[i], len(order), i))
        for j in post[i]:
            left[j] -= 1
            if not left[j]:
                ready.append(j)
    return [i for t, k, i in sorted(order)]


def rank_program(g, core, T, topo):
    rank = T.rank_of(core)
    if rank is None:
        return
    A = AluOpType
    F = ActivationFunctionType
    Q = {"V": g.vector, "A": g.scalar, "P": g.tensor, "G": g, "S": g.sync}
    tot = {}
    seen = {"V": {}, "A": {}, "P": {}, "G": {}, "S": {}}
    wr, rd, bank = {}, {}, {}
    v, a, pe = g.vector, g.scalar, g.tensor
    calls, acts = [], []

    def wait(q, evs):
        evs = [e for e in evs if seen[q].get(e[0], 0) < e[1]]
        for e in evs:
            if seen[q].get(e[0], 0) >= e[1]:
                continue
            if any(o is not e and o[2].get(e[0], 0) >= e[1] and (o[0] != e[0] or o[1] > e[1]) for o in evs):
                continue
            Q[q].wait_ge(T.sem[e[0]], e[1])
            seen[q][e[0]] = e[1]
        for e in evs:
            for s, n in e[2].items():
                if seen[q].get(s, 0) < n:
                    seen[q][s] = n

    def deps(q, r, w):
        evs = []
        for k in r:
            evs += [e for o, e in wr.get(k, [])]
        for k in w:
            evs += [e for o, e in wr.get(k, []) + rd.get(k, []) if o != q or q != "P"]
        for k in list(r) + list(w):
            if k[:2] == "ps":
                evs += [e for o, e in bank.get(k.split(":")[0], {}).items() if o != q]
        return evs

    def note(q, r, w, ev):
        for k in w:
            wr[k] = [(q, ev)]
            rd[k] = []
        for k in r:
            rd[k] = [x for x in rd.get(k, []) if x[0] != q or q == "D"] + [(q, ev)]
        for k in list(r) + list(w):
            if k[:2] == "ps":
                bank.setdefault(k.split(":")[0], {})[q] = ev

    def parts(keys):
        return [p for k in keys for p in (["%s:%d" % (k, i) for i in range(4)] if k[:2] == "ps" and ":" not in k else [k])]

    def op(q, fn, r, w, c):
        r, w = parts(r), parts(w)

        def issue():
            wait(q, deps(q, r, w))
            s = "s" + q
            tot[s] = tot.get(s, 0) + 1
            fn().then_inc(T.sem[s], 1)
            clk = dict(seen[q])
            clk[s] = tot[s]
            note(q, r, w, (s, tot[s], clk))
        calls.append((q, c, r, w))
        acts.append(issue)

    def dma(q, out, in_, r, w, s):
        wait(q, deps("D" + q, r, w))
        Q[q].dma_start(out, in_).then_inc(T.sem[s], 16)
        tot[s] = tot.get(s, 0) + 16
        clk = dict(seen[q])
        clk[s] = tot[s]
        note("D", r, w, (s, tot[s], clk))

    def arrives(k, s, n, c, r):
        def issue():
            tot[s] = n
            wr[k] = [("R", (s, n, {s: n}))]
        calls.append(("R", c, r, [k]))
        acts.append(issue)

    def send(dst, out, in_, r, s, k):
        def issue():
            wait("G", deps("G", r, []))
            rid, pid = topo.addr(dst)[:2]
            m = 0
            for e in topo.engines(core, dst)[:NE]:
                m |= 1 << e
            g.remote_dma(out, in_, T.sem[s], T.sem["loc"], pid, rid, m)
            tot["loc"] = tot.get("loc", 0) + NE
        calls.append(("G", 300, r, ["sent" + s]))
        acts.append(issue)
        arrives(k, s, NE, FLIGHT[k[:2]] - 2 * HOP + MORE.get(k, 0), ["sent" + s])

    def ts(out, in0, s1, s2, o0, o1, r, w, c=128):
        if o1 is None:
            op("V", lambda: v.tensor_scalar(out, in0, s1, None, o0), r, w, c)
        else:
            op("V", lambda: v.tensor_scalar(out, in0, s1, s2, o0, o1), r, w, c)

    def tt(out, i0, i1, o, r, w, c=128):
        op("V", lambda: v.tensor_tensor(out, i0, i1, o), r, w, c)

    def vc(out, in_, r, w, c=128):
        op("V", lambda: v.tensor_copy(out, in_), r, w, c)

    def act(out, in_, f, r, w, bias=0.0, scale=1.0, c=128, acc=None):
        op("A", lambda: a.activation(out, in_, f, bias=bias, scale=scale, accum_out=acc), r, w, c + 64)

    def mm(out, l, rh, st, sp, r, w, c=64):
        op("P", lambda: pe.matmul(out, l, rh, st, sp), r, w, c)

    def ms(ap, x, w, r=(), c=64):
        op("V", lambda: v.memset(ap, x), list(r), w, c)

    def iota(out, pattern, base, cm, w, n, whole=False, r=()):
        if whole:
            op("G", lambda: g.iota(out, pattern, base, cm), r, w, 160 + 2 * n)
        else:
            op("G", lambda: g.iota(out, pattern, base, cm, allow_small_or_imprecise_dtypes=True), r, w, 160 + 2 * n)

    def pick(out, in_, pattern, o, base, cm, r, w):
        op("G", lambda: g.affine_select(out, in_, pattern, o, 0.0, base, cm), r, w, 460)

    def scan(out, mask, in_, r, w, c):
        op("V", lambda: v.tensor_tensor_scan(out, mask, in_, 0.0, A.mult, A.max), r, w, c)

    def least(out, in_, r, w, c):
        op("V", lambda: v.tensor_reduce(out, in_, AxisListType.X, A.min, apply_absolute_value=True), r, w, c)

    def col(i):
        return T.pcol[:, i:i + 1]

    def gc(n):
        return int(60 + GATHER * n)

    dma("S", T.ents[:, 0:1024], T.ent[:, 0:1024], [], [], "dent")
    dma("A", T.ents[:, 1024:2048], T.ent[:, 1024:2048], [], [], "dent")
    dma("S", T.wti[:, 0:1], T.wt[:, 0:1], [], [], "dsm")
    dma("A", T.kpi[:, 0:1], T.kap[:, 0:1], [], [], "dsm")
    dma("S", T.fw[:, 0:2048], T.feat[:, 0:2048], [], [], "dfe")
    dma("A", T.fw[:, 2048:4096], T.feat[:, 2048:4096], [], [], "dfe")
    for k, s in (("wti", "dsm"), ("kpi", "dsm"), ("ents", "dent"), ("fw", "dfe")):
        arrives(k, s, 32, LOADED[k], [])

    S = 64
    ms(T.ones[:], 1.0, ["ones"])
    PI = T.pj[:, 7:8]
    iota(PI, [[1, 1]], 0, 1, ["pi"], 1, True)
    iota(T.sti[:], [[37, 64]], 0, 0, ["sti"], 64, True, ["~pi"])
    iota(T.ramp[:], [[1, 240]], -112, 0, ["ramp"], 240, False, ["~pi"])
    pick(T.bd0[:], T.ones[:], [[-16, 8], [0, 16]], A.is_ge, 0, 1, ["ones", "~ramp", "~sti"], ["bd0"])
    pick(T.bd[:], T.bd0[:], [[16, 8], [0, 16]], A.is_ge, 15, -1, ["bd0"], ["bd"])
    iota(T.r4[:], [[0, 32], [1, 4]], 0, 0, ["r4"], 128)
    iota(T.r16[:], [[0, 8], [1, 16]], 0, 0, ["r16"], 128)
    R = T.ramp[:, 112:240]
    ms(T.fm[:, 1:256], 1.0, ["fm0"], c=128)
    ms(T.fm[:, 0:256:16], 0.0, ["fm"], ["fm0"])
    vc(T.fm[:, 256:512], T.fm[:, 0:256], ["fm"], ["fm"])
    for n in (512, 1024, 1536):
        act(T.fm[:, n:n + 512], T.fm[:, 0:512], F.Copy, ["fm"], ["fm%d" % n], c=512)
    ms(T.fw[:, 4096:4112], 0.0, ["fwz"])
    ms(T.uc[0:64, :], -32.0, ["uc0"])
    ms(T.uc[64:128, :], 1.0 / 128, ["uc"])
    for b in range(4):
        ms(T.c2k[:, b:128:4], 256.0 + 32.0 * (b in TA), ["c2k"], ["c2k"])
    ms(T.half[:], 1.0, ["half"], c=128)
    ms(T.sa[:], 0.0, ["sa"])
    for i, (sh, m) in enumerate(((0, 15), (2, 3), (0, 3), (4, 7), (2, 31), (2, 15), (6, 1))):
        ts(T.pj[:, i:i + 1], PI, sh, m, A.arith_shift_right, A.bitwise_and, ["pi"], ["pj%d" % i], S)
    ts(T.stj[:], T.sti[:], 63, None, A.bitwise_and, None, ["sti"], ["stj"], S)
    vc(T.pcol[:, 0:8], T.pj[:], ["pi"] + ["pj%d" % i for i in range(7)], ["pc"], S)
    ts(col(11), col(2), 32.0, col(4), A.mult, A.add, ["pc"], ["pc11"], S)
    ts(col(12), col(2), 2.0, col(6), A.mult, A.add, ["pc"], ["pc12"], S)
    ts(T.st[:, 0:64], T.stj[:], 4096.0, -2065.0, A.mult, A.add, ["stj"], ["st"], S)
    for n in (64, 128, 256):
        act(T.st[:, n:2 * n], T.st[:, 0:n], F.Copy, ["st"], ["st"], c=n)
    for n in (512, 1024, 1536):
        act(T.st[:, n:n + 512], T.st[:, 0:512], F.Copy, ["st"], ["st%d" % n], c=512)
    ST = ["st", "st512", "st1024", "st1536"]
    ts(col(13), col(3), 4.0, col(2), A.mult, A.add, ["pc"], ["pc13"], S)
    ts(col(14), col(1), 32.0, None, A.mult, None, ["pc"], ["pc14"], S)
    ts(T.zl[:], T.ramp[:, 112:120], col(12), None, A.is_equal, None, ["ramp", "pc12"], ["zl"], S)
    ts(col(8), col(0), 0.5, None, A.add, None, ["pc"], ["pc8"], S)
    ts(col(10), col(0), -8192.0, 4096.0, A.mult, A.add, ["pc"], ["pc10"], S)
    ts(T.zg[:], T.ramp[:, 112:120], col(3), None, A.is_equal, None, ["ramp", "pc"], ["zg"], S)
    ts(T.mx[:], T.ramp[:, 112:116], col(1), None, A.is_equal, None, ["ramp", "pc"], ["mx"], S)
    ts(T.cl[:], T.ramp[:, 112:144], col(14), None, A.add, None, ["ramp", "pc14"], ["cl"], S)
    vc(T.c8[:], T.ramp[:, 112:120], ["ramp"], ["c8"], S)
    ts(T.sel[:], T.ramp[:, 112:144], col(13), 1.0 / 64, A.is_equal, A.mult, ["ramp", "pc13"], ["sel"], S)
    ts(T.idb[:], R, col(7), None, A.is_equal, None, ["ramp", "pc"], ["idb"], S)
    ts(T.spc[:], T.ramp[:, 112:120], 16.0, col(8), A.mult, A.add, ["ramp", "pc8"], ["spc"], S)
    ts(T.ls[:], T.spc[:], 128.0, None, A.add, None, ["spc"], ["ls"], S)
    Z = {}
    for i, (k, x) in enumerate((("zp", 512.0), ("zn", -512.0), ("zh", 256.0))):
        Z[k] = T.zz[:, 8 * i:8 * i + 8]
        ts(Z[k], T.zg[:], x, None, A.mult, None, ["zg"], [k], S)
    vc(T.cb[:], T.zl[:], ["zl"], ["cb"], S)
    vc(col(16), T.wti[:, 0:1], ["wti"], ["wcol"], S)
    vc(col(17), T.kpi[:, 0:1], ["kpi"], ["kcol"], S)
    ts(T.bd0[:], T.r4[:], col(1), None, A.is_equal, None, ["r4", "pc"], ["bd0"], S)
    for x in range(4):
        w4 = T.w4[:, 128 * x:128 * x + 128]
        pick(w4, T.bd[:], [[0, 8], [1, 4], [0, 4]], A.is_equal, -x, 0, ["bd", "~r4", "~r16"], ["w4%d" % x])
        ts(w4, w4, col(16), None, A.mult, None, ["w4%d" % x, "wcol"], ["w4%d" % x], S)
    ts(T.kr[:], T.ramp[:, 112:116], col(2), col(17), A.is_equal, A.mult, ["ramp", "pc", "kcol"], ["kr"], S)
    tt(T.ka[:], T.bd0[:], T.bd[:], A.mult, ["bd0", "bd"], ["ka"], 256)
    mm(T.psL[:, 16:20], T.ka[:], T.kr[:], True, True, ["ka", "kr"], ["psL:1"])
    ts(T.pmk[:], T.r16[:], col(5), 64.0, A.is_equal, A.mult, ["r16", "pc"], ["pmk"])
    ts(T.cm[:], T.r16[:], -0.25, 3.75, A.mult, A.add, ["r16"], ["cm"], S)
    for t in range(RO):
        ts(T.su[:, 40 * t + 32:40 * t + 36], T.psL[:, 16:20], 2.0, None, A.mult, None, ["psL:1"], ["k16%d" % t], S)
    ts(T.k8[:], T.psL[:, 16:20], 4095.0, -0.25, A.mult, A.add, ["psL:1"], ["k8"], S)
    ts(T.su[:, 36:40], T.psL[:, 16:20], 4095.0, -0.25, A.mult, A.add, ["psL:1"], ["kc0"], S)
    ts(T.ri[:], R, col(11), 8192.0, A.is_equal, A.mult, ["ramp", "pc11"], ["ri"], S)
    ms(T.mk[:], 1024.0 + SP, ["mk0"], c=292)
    ms(T.rx[:, 0:128], -8192.0, ["rx0"])
    ms(T.rx[:, 128:136], 1.0, ["rx"])
    ts(T.ramp2[:], T.ramp[:, 0:128], 8192.0, None, A.mult, None, ["ramp"], ["ramp2"], S)
    for c in range(8):
        s, w = SEG[c], 16 * c + 16
        ts(T.rn[:, s:s + w + 1], T.rx[:, 128 - w:129], T.zl[:, c:c + 1], None, A.mult, None, ["rx0", "rx", "zl"], ["rn%d" % c], S)
        ts(T.mk[:, s:s + w], T.ramp2[:, 128 - w:128], col(10), T.spc[:, c:c + 1], A.add, A.max,
           ["ramp2", "pc10", "spc", "mk0"], ["mk%d" % c], S)

    ts(T.idf[:], R, col(7), None, A.is_equal, None, ["ramp", "pc"], ["idf"])
    act(T.idn[:], T.idf[:], F.Identity, ["idf"], ["idn"], scale=-1.0)
    PA, PV, PW, PL = T.psA, T.psV, T.psW, T.psL
    P0, P1, P2, P3 = [slice(128 * i, 128 * i + 128) for i in range(4)]
    TAB = T.tab[:, SP:W]
    CZ = -(MB + OFF - 2048.0)

    def first_lanes():
        e = T.ents[:, 0:2048:16]
        ts(T.c1[:], e, -1024.5, MB, A.add, A.add, ["ents"], ["c1"])
        ts(PV[:, P0], T.c1[:], CZ, None, A.add, None, ["c1"], ["psV:0"])
        tt(T.lw[:, 0:128], e, PV[:, P0], A.add, ["ents", "psV:0"], ["so0"])

    def first_table():
        for i in range(8):
            s, k = slice(256 * i, 256 * i + 256), ("psK", "psD0", "psD1", "psW")[i // 2]
            p, pk = T[k][:, 256 * (i % 2):256 * (i % 2) + 256], ["%s:%d" % (k, 2 * (i % 2) + j) for j in range(2)]
            ts(T.cf[:, s], T.ents[:, s], -1024.5, MB, A.add, A.add, ["ents"], ["cf%d" % i], 256)
            act(p, T.cf[:, s], F.Identity, ["cf%d" % i], pk, bias=CZ, c=256)
            tt(T.tab[:, SP + 256 * i:SP + 256 * i + 256], T.ents[:, s], p, A.add, pk + ["ents"], ["tab%d" % i], 256)
        ms(T.tab[:, 0:16], 0.0, ["tab"], ["tab%d" % i for i in range(8)])

    def lane_list(t, dst):
        o = 128 * t
        so = T.lw[:, 2 * o:2 * o + 128] if t < RO - 1 else T.lw[:, 1024:1152]
        src, sk = (so, "so0") if t == 0 else (T.tab[:, SP + t:W:16], "tab")
        if t:
            act(so, src, F.Copy, [sk], ["so%d" % t])
        send(dst, T.lo[:, o:o + 128], so, ["so%d" % t], "ro%d" % t, "lo%d" % t)
        if t:
            ts(T.i1[:], src, -2033.0, None, A.add, None, [sk], ["i1"])
            ts(T.i3[:], T.i1[:], 16 - 4096, None, A.bitwise_and, None, ["i1"], ["i3"])
            ts(T.lst[:], T.i3[:], 2.0 ** -11, 4096.496, A.mult, A.add, ["i3"], ["lst"])
            return
        e = T.ents[:, 0:2048:16]
        ts(T.i1[:], e, 15.0, None, A.add, None, ["ents"], ["i1"])
        ts(PA[:, P0], e, 2.0 ** -15, -4096.5 / 16, A.mult, A.add, ["ents"], ["psA:0"])
        ts(T.i3[:], T.i1[:], 16, None, A.bitwise_and, None, ["i1"], ["i3"])
        tt(T.ly[:], T.i3[:], PA[:, P0], A.mult, ["i3", "psA:0"], ["ly"])
        ts(T.lst[:], T.ly[:], M0 + 4096.0, -M0, A.add, A.add, ["ly"], ["lst"])

    def spread_features():
        for i in range(16):
            s = F2 + 512 * i
            iota(T.fw[:, s:s + 512:2], [[0, 256]], 0, 0, ["f2z%d" % i], 256)
            act(T.fw[:, s + 1:s + 512:2], T.fw[:, 256 * i:256 * i + 256], F.Copy, ["fw", "~sentre0"], ["f2%d" % i], c=256)

    def features(t, cuts):
        win, wk = T.fw[:, 0:F2], ["fw", "fwz"]
        if t:
            win, wk = T.fw[:, F2:F2 + 8192], ["f2%s%d" % (k, i) for k in ("", "z") for i in range(16)]
        for i in range(len(cuts) - 1):
            n0, n1 = cuts[i:i + 2]
            c = slice(16 * n0, 16 * n1)
            r = ["lst"] + wk + ["~fg%d" % (i - 1)] * (i > 1)
            if i:
                act(T.fg[:, c], win.indirect(T.lst[:, n0:n1]), F.Copy, r, ["fg%d" % i], c=gc(16 * (n1 - n0)) - 64)
            else:
                vc(T.fg[:, c], win.indirect(T.lst[:, n0:n1]), r, ["fg%d" % i], gc(16 * (n1 - n0)))
        prev = "~fg0"
        for i in [1, 0] + list(range(2, len(cuts) - 1)):
            c = slice(16 * cuts[i], 16 * cuts[i + 1])
            scan(T.fs[:, c], T.fm[:, c], T.fg[:, c], ["fm", "fm512", "fm1024", "fm1536", "fg%d" % i, prev], ["fs%d" % i], (c.stop - c.start) // 2)
            prev = "~fs%d" % i
        return ["fs%d" % i for i in range(len(cuts) - 1)]

    def cand(t, dst, fs):
        U = T.psU[:, 0:32]
        mm(U, T.ones[:], T.uc[:], True, False, ["ones", "uc0", "uc"], ["psU"])
        for x in range(4):
            mm(U, T.w4[:, 128 * x:128 * x + 128], T.fs[:, 512 * x + 15:512 * x + 512:16], False, x == 3,
               ["w4%d" % x] + [k for i, k in enumerate(fs) if CUTS[i] < 32 * x + 32 and CUTS[i + 1] > 32 * x], ["psU"])
        o = 40 * t
        if t:
            n, nk = T.la[:, 12 * t - 4:12 * t - 3], "la%d" % (t - 1)
            ts(T.aa[:, 1:2], n, -31.0, M32 * 2, A.add, A.add, [nk], ["aa1"], S)
            ts(T.aa[:, 2:3], T.aa[:, 1:2], -M32 * 2, -1.0, A.add, A.mult, ["aa1"], ["aa2"], S)
            ts(T.su[:, o + 36:o + 40], T.k8[:], n, T.aa[:, 2:3], A.add, A.add, ["k8", nk, "aa2"], ["kc%d" % t], S)
        ts(T.ur[:], U, MN, -MN, A.add, A.add, ["psU"], ["ur"], S)
        tt(T.su[:, o:o + 32], U, T.ur[:], A.subtract, ["psU", "ur"], ["se%d" % t], S)
        send(dst, T.lu[:, o:o + 40], T.su[:, o:o + 40], ["se%d" % t, "k16%d" % t, "kc%d" % t], "re%d" % t, "lu%d" % t)

    def cand_list(t):
        o, lk = 40 * t, "lu%d" % t
        u = T.lu[:, o:o + 32]
        act(T.vq[:], u, F.Square, [lk, "~ox"], ["vq"], bias=2047.5 / 4, scale=0.25, c=S)
        act(PW[:], T.ox[:], F.Copy, ["ox", "~vq"], ["psW"], c=512)
        for b in range(4):
            ts(PL[:, 256 + 32 * b:288 + 32 * b], u, T.lu[:, o + 32 + b:o + 33 + b], T.lu[:, o + 36 + b:o + 37 + b], A.mult, A.add,
               [lk], ["psL:b%d" % b], S)
        for b in range(4):
            tt(T.u5[:, 32 * b:32 * b + 32], T.vq[:], PL[:, 256 + 32 * b:288 + 32 * b], A.add, ["vq", "psL:b%d" % b, "~psL:b3"], ["u5%d" % b], S)
        ts(T.u6[:], T.u5[:], 1, 2047, A.arith_shift_right, A.bitwise_and, ["u5%d" % b for b in range(4)], ["u6"])
        vc(T.le[:], T.u6[:], ["u6"], ["le"])
        for x in range(EARLY):
            ts(T.eh[:, x:512:4], T.u6[:], -1023.5, T.mx[:, x:x + 1], A.add, A.mult, ["u6", "mx", "~le"], ["eh%d" % x])

    def scatter(tab, t):
        tt(T[tab][:].indirect(T.l2[:, 8 * t:8 * t + 8]), T.nb[:], T.nr[:], A.add, ["l2%d" % t, "nb", "nr", tab], [tab],
           int(60 + SCATTER * 128))

    def expand(t):
        av, lk = T.lo[:, 128 * t:128 * t + 128], "lo%d" % t
        act(T.c1[:], av, F.Identity, [lk], ["c1"], bias=-8.5)
        act(PA[:, P0], av, F.Identity, [lk], ["psA:0"], bias=OFF)
        act(PL[:, P1], T.st[:, t:2048:16], F.Copy, ST, ["psL:a"])
        act(T.c2[:], T.c1[:], F.Identity, ["c1"], ["c2"], bias=M16 + 16.0)
        act(T.c3[:], T.c2[:], F.Identity, ["c2"], ["c3"], bias=-M16 - 16.0)
        act(T.ox[:], T.c3[:].indirect(T.cl[:]), F.Identity, ["c3", "cl"], ["ox"], bias=8.5, c=gc(512) - 64)

    def own_side(t):
        tt(T.ah[:], T.lo[:, 128 * t:128 * t + 128], PL[:, P1], A.add, ["lo%d" % t, "psL:a"], ["ah"])
        ts(T.al[:], T.ah[:], 31, None, A.bitwise_and, None, ["ah"], ["al"])
        ts(T.ak[:], T.ah[:], 15, 7, A.arith_shift_right, A.bitwise_and, ["ah"], ["ak"])
        ts(PV[:, P0], T.al[:], 8.0 + t, 64.0, A.is_ge, A.mult, ["al"], ["psV:0"])
        tt(T.av[:], T.ak[:], PV[:, P0], A.is_le, ["ak", "psV:0"], ["av"])
        tt(T.as2[:], T.al[:], PV[:, P0], A.add, ["al", "psV:0"], ["as2"])
        tt(T.ap[:], T.av[:], PA[:, P0], A.mult, ["av", "psA:0"], ["ap"])

    def own_rest(t):
        act(T.ay[:], T.ap[:], F.Identity, ["ap"] + ["~ma1"] * (t < RO - 1), ["ay"], bias=-OFF)
        mm(PA[:, P1], T.idn[:], T.ay[:], True, False, ["idn", "ay"] + ["~" + k for k in KEYS], ["psA:1"], 512)
        act(PV[:, P2], T.as2[:], F.Relu, ["as2", "~ay"], ["psV:2"], bias=(12.0 + t) / 16, scale=-1.0 / 16)
        act(T.sg[:], T.as2[:], F.Sign, ["as2", "~ay"], ["sg"], bias=-79.5)
        act(PV[:, P3], T.sg[:], F.Identity, ["sg"], ["psV:3"], scale=8.0 + t)
        lane, lk, off = T.ap, "ap", -OFF
        if t == RO - 1:
            lane, lk, off = T.na, "na", 0.0
            act(T.ac[:], T.ap[:], F.Identity, ["ap", "~ay"], ["ac"], bias=MN)
            act(PA[:, P2], T.ac[:], F.Identity, ["ac"], ["psA:2"], bias=MN / 2, scale=-0.5)
            tt(T.na[:], T.ap[:], PA[:, P2], A.add, ["ap", "psA:2"], ["na"])
        tt(T.ao[:], lane[:], PV[:, P0], A.mult, [lk, "psV:0"], ["ao"])
        act(T.az[:], T.ao[:], F.Identity, ["ao", "~ay"], ["az"], bias=off, scale=1.0 / 64)

    KEYS = (["psK:%s%d%d" % (k, i, x) for i in range(4) for k in ("mt", "db")[:1 if i in TA else 2] for x in range(4)]
            + ["psK:e%d" % i for i in range(4)])

    def score(t):
        K = T.psK
        lk = "le"
        left = [len(KEYS)]
        EH = ["eh%d" % x for x in range(4)]

        def add(out, l, rh, r, k):
            def fn():
                left[0] -= 1
                return pe.matmul(out, l, rh, False, left[0] == 0)
            op("P", fn, r, [k], 64)

        mm(K[:, P0], T.ones[:], T.cm[:], True, False, ["ones", "cm"], ["psK"], 128)
        mm(K[:, P0], T.ones[:], T.c2k[:], False, False, ["ones", "c2k"], ["psK"] + KEYS, 128)

        def sums(i, tile, k, z, r=None):
            for x in range(4):
                add(K[:, 4 * x + i:128:16], tile[:, 512 * i + x:512 * i + 512:4], Z[z], (r or [k]) + [z], "psK:%s%d" % (k, x))

        for i in GA:
            act(T.cf[:, 512 * i:512 * i + 512], TAB.indirect(T.le[:, 32 * i:32 * i + 32]), F.Copy,
                ["tab", lk, "~cf%d" % (2 * i - 2)], ["cf%d" % (2 * i), "cf%d" % (2 * i + 1)], c=gc(512) - 64)
        tests = {"mt": (MN + 4096.0, "zp"), "db": (M16, "zn")}
        prev = "~eh%d" % (EARLY - 1)
        for step in STEPS:
            k, i = step[:2], int(step[2])
            c = slice(512 * i, 512 * i + 512)
            if k == "dd" and i in GA:
                tt(T.dd[:, c], T.cf[:, c], PW[:], A.subtract, ["cf%d" % (2 * i), "cf%d" % (2 * i + 1), "psW", prev], [step], 512)
            elif k == "dd":
                tt(T.dd[:, c], TAB.indirect(T.le[:, 32 * i:32 * i + 32]), T.ox[:], A.subtract, ["tab", lk, "ox", prev], [step], gc(512))
            elif k in tests:
                ts(T[k][:, c], T.dd[:, c], tests[k][0], tests[k][0], A.add, A.is_equal, ["dd%d" % i, prev], [step], 256)
                sums(i, T[k], step, tests[k][1])
            elif k == "eh":
                for x in range(EARLY, 4):
                    ts(T.eh[:, x:512:4], T.le[:], -1023.5, T.mx[:, x:x + 1], A.add, A.mult, [lk, "mx", prev], [EH[x]], S)
                    prev = "~" + EH[x]
                for b in range(4):
                    add(K[:, b:128:4], T.eh[:, 128 * b:128 * b + 128], T.sel[:], ["sel"] + EH, "psK:e%d" % b)
                step = EH[3]
            else:
                for j in LAST:
                    x = j % 4
                    c4 = slice(c.start + x, c.stop, 4)
                    if j < 4:
                        tt(T.dd[:, c4], T.cf[:, c4], PW[:, x:512:4], A.subtract, ["cf%d" % (2 * i), "cf%d" % (2 * i + 1), "psW", prev],
                           ["dd%d%d" % (i, x)])
                        prev = "~dd%d%d" % (i, x)
                        continue
                    for k, (m, z) in tests.items():
                        ts(T[k][:, c4], T.dd[:, c4], m, m, A.add, A.is_equal, ["dd%d%d" % (i, x), prev], ["%s%d%d" % (k, i, x)], S)
                        add(K[:, 4 * x + i:128:16], T[k][:, c4], Z[z], ["%s%d%d" % (k, i, x), z], "psK:%s%d%d" % (k, i, x))
                        prev = "~%s%d%d" % (k, i, x)
            prev = "~" + step
            if k == "dd" and i in TA:
                for h in (2 * i, 2 * i + 1):
                    c2 = slice(256 * h, 256 * h + 256)
                    act(T.da[:, c2], T.dd[:, c2], F.Abs, [step] + ["~cf%d" % (2 * j) for j in GA], ["da%d" % h], c=256)
                    act(T.cf[:, c2], T.da[:, c2], F.Abs, ["da%d" % h], ["cf%d" % h], bias=-1026.25, c=256)
                    act(T.mt[:, c2], T.cf[:, c2], F.Sign, ["cf%d" % h], ["ma%d" % h], bias=1018.0, scale=-1.0, c=256)
                sums(i, T.mt, "mt%d" % i, "zh", ["ma%d" % h for h in (2 * i, 2 * i + 1)])

    DB = [(k, SPLIT[i], SPLIT[i + 1]) for i, k in enumerate(("psD0", "psD1", "psU")[:len(SPLIT) - 1])]

    def partner(t):
        def pairs(i, l, lk, name, st, sp, after=()):
            k, c0, c1 = DB[i]
            mm(T[k][:, 0:SEG[c1] - SEG[c0]], l, T[name][:, SEG[c0]:SEG[c1]], st, sp,
               [lk] + ["%s%d" % (name, c) for c in range(c0, c1)] + list(after), [k], SEG[c1] - SEG[c0])

        for i in range(len(DB)):
            pairs(i, T.idb[:], "idb", "mk", True, False)
        scan(T.ks[:], T.fm[:, 0:128], T.psK[:, P0], ["fm", "psK"] + KEYS, ["ks"], 128)
        scan(T.kh[:], T.fm[:, 0:128], T.psK[:, P0], ["fm", "psK"] + KEYS, ["kh"], 128)
        tt(T.p8[:], T.ks[:, 15:128:16], T.kh[:, 15:128:16], A.subtract, ["ks", "kh"], ["p8"], S)
        tt(T.pm[:], T.p8[:].indirect(T.c8[:]), T.pmk[:], A.mult, ["p8", "c8", "pmk"], ["pm"], gc(128))
        mm(T.psL[:, 0:8], T.pm[:], T.cb[:], True, True, ["pm", "cb"], ["psL:0"])
        ts(T.pe[:], T.p8[:].indirect(T.c8[:]), 64.0, None, A.mult, None, ["p8", "c8"], ["pe"], gc(128))
        after = "~psL:0"
        for i in range(len(DB)):
            pairs(i, T.pm[:], "pm", "rn", False, False, [after])
            k, c0, c1 = DB[i]
            for c in range(c0, c1):
                s, w = SEG[c] - SEG[c0], 16 * c + 16
                mm(T[k][:, s:s + w], T.pe[:], T.ri[:, 0:w], False, c == c1 - 1, ["pe", "ri"], [k], max(S, w))
            after = "~%s:0" % DB[i][0]
        ts(T.l1[:], T.psL[:, 0:8], 1023.5, None, A.add, None, ["psL:0"], ["l1"], S)
        act(T.bs[:], T.st[:].indirect(T.l1[:]), F.Copy, ST + ["l1"], ["bs"], c=gc(128) - 64)
        act(T.bg[:], TAB.indirect(T.l1[:]), F.Copy, ["tab", "l1", "~bs"], ["bg"], c=gc(128) - 64)
        ts(T.bh[:], TAB.indirect(T.l1[:]), -2065.0, None, A.add, None, ["tab", "l1"], ["bh"], gc(128))
        mm(PA[:, P1], T.idf[:], T.bg[:], False, True, ["idf", "bg", "~psU:0"], ["psA:1"], 512)
        prev = "~bg"
        for step in SCALAR:
            if step == "dq":
                act(T.dq[:], PA[:, P1], F.Square, ["psA:1", prev], [step], scale=1.0 / 2048)
            elif step == "bz":
                act(T.bz[:], T.bg[:], F.Sign, ["bg", prev], [step], bias=OFF)
            elif step[1] == "a":
                k, c0, c1 = DB[int(step[2])]
                act(T.xa[:, SEG[c0]:SEG[c1]], T[k][:, 0:SEG[c1] - SEG[c0]], F.Abs, [k, prev], [step], c=SEG[c1] - SEG[c0])
            else:
                c = int(step[2])
                s = slice(SEG[c], SEG[c + 1])
                act(T.xb[:, s], T.xa[:, s], F.Relu, ["xa%d" % i for i in range(3) if SPLIT[i] <= c < SPLIT[i + 1]] + [prev], [step],
                    bias=4096.0, scale=-1.0, c=SEG[c + 1] - SEG[c] + 24, acc=T.xc[:, c:c + 1])
            prev = "~" + step
        for k, c0, c1 in DB:
            for c in range(c0, min(c1, AM)):
                least(T.mn[:, c:c + 1], T[k][:, SEG[c] - SEG[c0]:SEG[c + 1] - SEG[c0]], [k, "~bh"], ["mn%d" % c], max(S, SEG[c + 1] - SEG[c]))
        act(T.xc[:, 8 + AM:16], T.xc[:, AM:8], F.Identity, ["xb%d" % c for c in range(AM, 8)], ["xc"], bias=4096.0, scale=-1.0, c=S)
        tt(T.mn[:, AM:8], T.xc[:, 8 + AM:16], T.spc[:, AM:8], A.max, ["xc", "spc"], ["mn%d" % c for c in range(AM, 8)], S)
        mk = ["mn%d" % c for c in range(8)]
        ts(T.l2[:, 8 * t:8 * t + 8], T.mn[:], -0.5, None, A.add, None, mk, ["l2%d" % t], S)
        return mk

    def merged(t, dst, mk):
        o = 12 * t
        if t < RO - 1:
            act(T.wj[:], T.mn[:], F.Sign, mk, ["wj", "aa0"], bias=-SP + 0.75, c=S, acc=T.aa[:, 0:1])
            mm(T.psL[:, 32:33], T.half[:], T.aa[:, 0:1], True, True, ["half", "aa0"], ["psL:2"], 256)
            act(T.sa[:, o + 8:o + 9], T.psL[:, 32:33], F.Copy, ["psL:2", "sa"], ["sb%d" % t], c=S)
        tt(T.sa[:, o:o + 8], T.mn[:], T.ls[:], A.min, mk + ["ls", "sa"], ["sa%d" % t], S)
        send(dst, T.la[:, o:o + 12], T.sa[:, o:o + 12], ["sa", "sa%d" % t, "sb%d" % t], "ra%d" % t, "la%d" % t)

    def meet(t, dst):
        o = 128 * t
        last = t == RO - 1
        PK = T.psK
        if last:
            act(T.ac[:], T.bg[:], F.Identity, ["bg"], ["ac"], bias=MB, scale=0.5)
            act(PL[:, P2], T.ac[:], F.Identity, ["ac"], ["psL:b"] + ["psL:b%d" % b for b in range(4)], bias=-MB - OFF / 2)
            act(PK[:, P2], T.az[:], F.Copy, ["az", "ks", "kh"], ["psK:2"])
        else:
            mm(PK[:, P1], T.idn[:], T.az[:], True, False, ["idn", "az", "ks", "kh"], ["psK:1"], 512)
            mm(PK[:, P1], T.idf[:], T.bg[:], False, True, ["idf", "bg", "~psA:1"], ["psK:1"], 512)
        place = {"psA:1": PA[:, P1], "psK:1": PK[:, P1], "psK:2": PK[:, P2], "psL:a": PL[:, P1], "psL:b": PL[:, P2], "psL:c": PL[:, P3],
                 "sn%d" % t: T.sn[:, o:o + 128]}
        for i, s in enumerate((P0, P1, P2, P3)):
            place["psV:%d" % i], place["psW:%d" % i] = PV[:, s], PW[:, s]
        prev = ["~bh"]

        def at(k):
            return place[k] if k in place else T[k][:]

        def one(w, r, s1, s2, o0, o1=None):
            ts(at(w), at(r), s1, s2, o0, o1, [r] + prev, [w])
            prev[0] = "~" + w

        def two(w, r0, r1, o):
            tt(at(w), at(r0), at(r1), o, [r0, r1] + prev, [w])
            prev[0] = "~" + w

        def site():
            if last:
                two("nr", "r0", "psV:1", A.mult)
                two("dz", "bz", "psK:1", A.mult)
                two("psV:0", "dz", "psW:1", A.mult)
                two("nb", "az", "psV:0", A.add)
            else:
                two("nr", "r0", "psV:1", A.mult)
                two("nb", "az", "psV:0", A.add)

        one("bl", "bh", 31, None, A.bitwise_and)
        one("bi", "bh", 16, None, A.bitwise_and)
        tt(T.bj[:], TAB.indirect(T.l1[:]), T.bs[:], A.add, ["tab", "l1", "bs"] + prev, ["bj"], gc(128))
        prev[0] = "~bj"
        one("psW:0", "bl", 8.0 + t, 64.0, A.is_ge, A.mult)
        two("f2", "bl", "psV:3", A.is_lt)
        one("bk", "bj", 15, 7, A.arith_shift_right, A.bitwise_and)
        one("psW:3", "bl", -1.0, 12.0 + t, A.mult, A.add)
        two("wq", "bi", "psV:2", A.mult)
        two("psW:1", "bk", "psW:0", A.is_le)
        if last:
            two("bn", "bg", "psL:b", A.subtract)
            two("psL:c", "ap", "psW:0", A.is_lt)
        two("t2", "f2", "psW:3", A.mult)
        if last:
            two("psL:a", "bn", "psL:c", A.mult)
            two("psW:2", "t2", "psA:1", A.add)
            two("psV:1", "dq", "psW:1", A.is_lt)
            two("sx", "na", "psL:a", A.add)
            two("m3", "wq", "psW:2", A.max)
            two("psK:1", "bn", "psK:2", A.subtract)
            two("psW:3", "m3", "psV:1", A.mult)
            two("r0", "m3", "psA:1", A.subtract)
            two("sn%d" % t, "sx", "psW:3", A.add)
            site()
        else:
            two("psW:2", "wq", "psA:1", A.subtract)
            two("dz", "bz", "psK:1", A.mult)
            two("psV:1", "dq", "psW:1", A.is_lt)
            two("r0", "t2", "psW:2", A.max)
            two("psV:0", "dz", "psW:1", A.mult)
            site()
            two("sx", "ap", "psW:0", A.is_lt)
            scatter("tab", t)
            two("psW:3", "r0", "psA:1", A.add)
            two("m3", "sx", "psV:1", A.max)
            two("psW:2", "m3", "psW:3", A.mult)
            two("sn%d" % t, "ay", "psW:2", A.add)
        send(dst, T.lw[:, 2 * o + 128:2 * o + 256], T.sn[:, o:o + 128], ["sn%d" % t], "rn%d" % t, "ln%d" % t)

    def back(t):
        o = 256 * t
        tab, old = "tab", "so%d" % t
        if t == RO - 1:
            tab, old = "fin", "sf"
            so = T.lw[:, 1024:1152]
            act(T.c1[:], so, F.Identity, ["so%d" % t, "~ma1"], ["c1"], bias=MB, scale=0.5)
            act(PA[:, P3], T.c1[:], F.Identity, ["c1"], ["psA:3"], bias=-MB - OFF / 2)
            tt(T.lw[:, o:o + 128], so, PA[:, P3], A.subtract, ["so%d" % t, "psA:3"], [old])
        ts(T.lr[:], T.la[:, 12 * t:12 * t + 8], -0.5, None, A.add, None, ["la%d" % t], ["lr"], S)
        act(T[tab][:, SP + t:W:16], T.lw[:, o:o + 256].indirect(T.lr[:]), F.Copy,
            ["lr", "ln%d" % t, old, "~se%d" % (t + 1), tab], [tab], c=gc(128) - 64)
        scatter(tab, t)

    def last_table():
        for i in range(8):
            s, k = slice(SP + 256 * i, SP + 256 * i + 256), ("psK", "psU", "psD0", "psD1")[i // 2]
            p, pk = T[k][:, 256 * (i % 2):256 * (i % 2) + 256], ["%s:%d" % (k, 2 * (i % 2) + j) for j in range(2)]
            cf = T.cf[:, 256 * i:256 * i + 256]
            act(cf, T.tab[:, s], F.Identity, ["tab"], ["cf%d" % i], bias=MB, scale=0.5, c=256)
            act(p, cf, F.Identity, ["cf%d" % i], pk, bias=-MB - OFF / 2, c=256)
            tt(T.fin[:, s], T.tab[:, s], p, A.subtract, ["tab"] + pk, ["fin%d" % i], 256)
        ms(T.fin[:, 0:16], 0.0, ["fin"], ["fin%d" % i for i in range(8)])

    first_lanes()
    first_table()
    for t in range(RO):
        callee = T.cores[(rank + 1 + t % 7) % N]
        caller = T.cores[(rank - 1 - t % 7) % N]
        lane_list(t, callee)
        cand(t, callee, features(t, CUTS))
        if t == 0:
            spread_features()
        expand(t)
        own_side(t)
        if t:
            back(t - 1)
        cand_list(t)
        score(t)
        own_rest(t)
        merged(t, caller, partner(t))
        meet(t, caller)
    last_table()
    back(RO - 1)
    for i in plan(calls):
        acts[i]()
    dma("S", T.yent[:, 0:1024], T.fin[:, SP:SP + 1024], ["fin"], [], "dy")
    dma("A", T.yent[:, 1024:2048], T.fin[:, SP + 1024:W], ["fin"], [], "dy")
    for s in tot:
        wait("G", [(s, tot[s], {})])
